import numpy as np, ml_dtypes
CORES = [6,15,38,47]
N = 4
BF = ml_dtypes.bfloat16
def gentries(a):
    return np.ascontiguousarray(a.reshape(8, 16, -1).transpose(0, 2, 1)).reshape(8, -1)
def gtable(e):
    e = np.asarray(e); return np.ascontiguousarray(e.reshape(8, -1, 16).transpose(0, 2, 1)).reshape(128, -1).astype(np.int32)
W, L, U, T, A, K, Q = 4096, 192, 64, 7, 3, 1344, 1344
def pack(x, b, o, w, t):
    return {"xs": np.ascontiguousarray(x.reshape(N, 128, W)).astype(np.float32).astype(BF), "nb": np.ascontiguousarray(b.reshape(N, 128, W)).astype(np.int32),
            "od": np.stack([gtable(a) for a in o]), "wt": np.ascontiguousarray(w.reshape(N, 128, 1)).astype(np.int32), "th": np.ascontiguousarray(t.reshape(N, 8, 1)).astype(np.int32)}
def parts(rng):
    amp = 4 + 86 * rng.random((N, 8, 1, W)); mid = rng.integers(96, 160, (1, 8, 16, 1))
    x = np.clip(np.rint(mid + amp * rng.standard_normal((N, 8, 16, W), dtype=np.float32)), 0, 255).astype(np.int64)
    b = rng.integers(0, W, (N, 8, 16, W)); o = np.argsort(rng.random((N, 8, W)), axis=-1)[..., :Q]
    return x, b, o, rng.integers(0, 256, (N, 8, 16)), rng.integers(300, 1000, (N, 8))
def setup_inputs(rng):
    return pack(*parts(rng))
def setup_inputs_spread(rng):
    x, b, o, w, t = parts(rng)
    x = np.floor(np.exp2(8 * rng.random((N, 8, 1, W))) * rng.random((N, 8, 16, W))).astype(np.int64)
    b = np.floor(W * rng.random((N, 8, 16, W)) ** 3).astype(np.int64)
    w = np.floor(np.exp2(8 * rng.random((N, 8, 16))) - 1).astype(np.int64); t = np.floor(np.exp2(12 * rng.random((N, 8))) - 1).astype(np.int64)
    x[:, 6] = rng.integers(192, 256, (N, 16, W)); w[:, 6] = rng.integers(240, 256, (N, 16)); t[:, 6] = 0
    return pack(x, b, o, w, t)
def setup_inputs_ends(rng):
    lo = rng.integers(0, 2, 8) * 255; lo[7] = 0; base = lo.reshape(1, 8, 1, 1)
    u = rng.random((N, 8, 1, W)); e = 255 * rng.integers(0, 2, (N, 8, 16, W))
    x = np.where(u < 0.5, 255 - base, np.where(u < 0.7, base, e))
    x[..., [0, W - 1]] = base; x[:, ::2, :, 1] = lo[::2].reshape(1, 4, 1); x[:, 7, :, 1:8] = 0; x[:, 7, 15, W - 1] = 255
    b = (W - 1) * rng.integers(0, 2, (N, 8, 16, W))
    b = np.where(rng.random((N, 8, 1, W)) < 0.2, (W - 1) * rng.integers(0, 2, (N, 8, 1, W)), b)
    for step in range(A, T):
        place = (16 * 255 * 255 + 77 * step) & (W - 1)
        b[:, 7, :, place] = 0; b[1::2, 7, 15, place] = W - 1; b[:, 7, 5, (77 * step) & (W - 1)] = W - 1
    s = np.zeros(Q, np.int64); h = Q // 2; s[0::2] = np.arange(Q - h); s[1::2] = W - 1 - np.arange(h)
    key = rng.random((N, 8, T, L)); key[:, :, 0, 0] = -3; key[:, :, 0, 1] = -2; key[:, :, 0, 2] = -1
    o = s.reshape(T, L)[np.arange(T)[:, None], np.argsort(key, axis=-1)].reshape(N, 8, Q)
    for q in range(N):
        x[q, 7][:, o[q, 7][np.array([3, 4, U - 2, U - 1, L - 2, L - 1])]] = 255
    kd = rng.integers(0, 3, (N, 8, 1)); w = np.where(kd == 0, 255, np.where(kd == 1, 0, 255 * rng.integers(0, 2, (N, 8, 16))))
    w[:, 7] = 255; w[:, 0, ::2] = 0; w[:, 0, 1::2] = 255
    t = 4095 * (rng.random((N, 8)) < 0.3).astype(np.int64)
    for q in range(N): t[q, q % 7] = 4095
    t[:, 7] = 0
    return pack(x, b, o, w, t)
def setup_inputs_corners(rng):
    a = (np.arange(65536)[:, None] >> np.arange(16)) & 1
    par = np.stack([(np.arange(16) >> i) & 1 for i in range(4)] + [np.ones(16, np.int64)], axis=1)
    words = a[~np.any(((a @ par) & 1) == 1, axis=1)]
    few = words[np.sum(words, axis=1) <= 10]
    src = (N - 2 - (A - 1) % (N - 1)) % N
    late = (5 - A) * L
    x = rng.integers(100, 132, (N, 8, 16, W)); b = rng.integers(0, W, (N, 8, 16, W)); o = np.zeros((N, 8, Q), np.int64)
    far = np.arange(W) + 1 + rng.integers(W // 4, 3 * W // 4, (N, 8, W)); far = far & (W - 1); far = far - (far & 1); b[:, :, 0] = (far - 1) & (W - 1)
    for q in range(N):
        for g in range(8):
            n = int(rng.choice(np.array([0, 1, U - 1, U, U + 1, L])))
            if q == 0: n = (U, U + 1, L, U - 1, 1, 0, U, L)[g]
            if g == 4: n = U if q == src else 1 if q == (src + 1) % N else int(rng.choice(np.array([0, 1, U - 1, U])))
            if g == 5: n = 0
            odd = rng.permutation(W // 2) * 2 + 1; even = np.arange(W // 2) * 2
            rest = rng.permutation(np.concatenate([odd[n:], even]))
            first = rng.permutation(np.concatenate([odd[:n], rest[:L - n]])); more = rest[L - n:]
            o[q, g] = (np.concatenate([more[:late], first, more[late:]]) if g == 7 else np.concatenate([first, more]))[:Q]
            lone = np.zeros(W, bool)
            if g != 4 and g != 7: lone[odd[n:][rng.random(W // 2 - n) < 0.1]] = True
            lone[rest[:L - n]] = False; lone[odd[:n]] = True
            k = int(np.count_nonzero(lone))
            if g == 4: x[q, g][:, lone] = 30 + 160 * few[rng.permutation(few.shape[0])[:k]].T
            else: x[q, g][:, lone] = 255 * words[rng.permutation(2048)[:k]].T
            if g == 4 and q == src: x[q, g][:, first[np.flatnonzero(lone[first])[-1]]] = 255
    w = np.zeros((N, 8, 16), np.int64) + rng.choice(np.array([0, 1, 255]), (N, 8, 1)); w[:, 3] = 255; w[:, 2] = 0
    t = rng.choice(np.array([600, 600, 600, 0]), (N, 8)); t[0] = 600; t[1, 6] = 0; t[:, 4] = 600; t[:, 5] = 4095; t[:, 7] = 600
    return pack(x, b, o, w, t)
def setup_inputs_ties(rng):
    _, b, o, w, t = parts(rng)
    kd = np.repeat(rng.random((N, 8, W // 2)), 2, axis=-1); half = np.argsort(rng.random((N, 8, 16, W)), axis=2) < 8; kx = kd[:, :, None, :]
    x = np.where(kx < 0.35, 100, np.where(kx < 0.7, 140, np.where(half, 100, 140)))
    for q in range(N):
        for g in range(8):
            com = np.flatnonzero(kd[q, g, ::2] < 0.7) * 2
            b[q, g] = np.where(rng.random((16, W)) < 0.05, b[q, g], com[rng.integers(0, com.shape[0], (16, W))])
    t = rng.choice(np.array([0, 319, 320, 321]), (N, 8)); t[0, :4] = np.array([0, 319, 320, 321]); t[1, 4:] = np.array([320, 321, 0, 320])
    return pack(x, b, o, w, t)
def setup_inputs_near(rng):
    _, b, o, w, t = parts(rng)
    y = (np.add.accumulate(rng.integers(-3, 4, (N, 8, 16, W)), axis=3) + rng.integers(0, 512, (N, 8, 16, 1))) & 511
    x = np.where(y > 255, 511 - y, y); u = np.arange(W)
    b = np.where(rng.random((N, 8, 16, W)) < 0.7, (u + rng.choice(np.array([-17, -16, -15, -1, 0, 1, 15, 16, 17]), (N, 8, 16, W))) & (W - 1), b)
    b = np.where(rng.random((N, 8, 1, W)) < 0.25, (u + rng.integers(-15, 16, (N, 8, 16, W))) & (W - 1), b)
    key = rng.random((N, 8, W)); key[..., :16] -= 1; key[..., W - 16:] -= 1; o = np.argsort(key, axis=-1)[..., :Q]
    t = rng.choice(np.array([40, 100, 400, 900, 4095]), (N, 8)); t[0, 0] = 4095; t[0, 1] = 40; t[1, 2] = 100
    return pack(x, b, o, w, t)
def check_inputs(d):
    bad = []
    for k, lo, hi in (("xs", 0, 255), ("nb", 0, W - 1), ("od", 0, W - 1), ("wt", 0, 255), ("th", 0, 4095)):
        a = np.asarray(d[k]).astype(np.float32)
        if not (np.min(a) >= lo and np.max(a) <= hi): bad.append("range of " + k)
    a = np.asarray(d["xs"]).astype(np.float32)
    if np.any(a != np.floor(a)): bad.append("whole numbers in xs")
    o = np.sort(np.stack([gentries(a) for a in d["od"]]), axis=-1)
    if np.any(o[..., 1:] == o[..., :-1]): bad.append("different numbers in a group's od")
    return bad
def dist(X, c, x):
    n = c.shape[3]
    e = np.take_along_axis(X, c.reshape(N, 8, 1, 16 * n), 3).reshape(N, 8, 16, 16, n)
    return np.add.reduce(np.abs(e - x[:, :, :, None, :]), axis=2)
def reference(xs, nb, od, wt, th):
    X = xs.astype(np.float32).astype(np.int64).reshape(N, 8, 16, W); col = nb.astype(np.int64).reshape(N, 8, 16, W)
    order = np.stack([gentries(a) for a in od]).astype(np.int64); w = wt.astype(np.int64).reshape(N, 8, 16, 1); lim = th.astype(np.int64).reshape(N, 8)
    v = np.zeros((N, 8, L), np.int64); m = np.zeros((N, 8, L), np.int64); age = np.zeros((N, 8, L), np.int64); c = np.zeros((N, 8, 16, L), np.int64)
    free = np.ones((N, 8, L), bool); cur = np.zeros((N, 8, 1), np.int64); gx = np.zeros((N, 8, 16, U), np.int64); gm = np.zeros((N, 8, U), np.int64)
    seen = []; judged = gm
    for t in range(T):
        f = free.astype(np.int64); run = np.add.accumulate(f, axis=2)
        v = np.where(free, np.take_along_axis(order, np.minimum(cur + run - f, Q - 1), 2), v); cur = cur + run[:, :, L - 1:]
        m = np.where(free, 4095, m); age = np.where(free, 0, age)
        seed = (np.take_along_axis(col, ((v - 1) & (W - 1))[:, :, None, :], 3) + 1) & (W - 1)
        c = np.where(free[:, :, None, :], seed, c)
        h = (np.add.reduce(w * gx, axis=2) + 77 * t) & (W - 1)
        gc = np.take_along_axis(col, h[:, :, None, :], 3)
        own = np.take_along_axis(X, v[:, :, None, :], 3)
        D = np.where(np.abs(c - v[:, :, None, :]) < 16, 4095, dist(X, c, own))
        m = np.minimum(m, np.min(D, axis=2)); near = np.take_along_axis(c, np.argmin(D, axis=2)[:, :, None, :], 2)
        judged = np.minimum(gm, np.min(dist(X, gc, gx), axis=2))
        np.put_along_axis(col, v[:, :, None, :], c, 3)
        alive = m >= lim[:, :, None]; age = np.where(alive, age + 1, age)
        go = (alive & (age >= A)).astype(np.int64); before = np.add.accumulate(go, axis=2) - go
        leave = (go == 1) & (before < U) & (t < T - 1)
        c = np.take_along_axis(col, near, 3)
        free = ~alive | leave
        slot = np.where(leave, before, U); nx = np.zeros((N, 8, 16, U + 1), np.int64); nm = np.zeros((N, 8, U + 1), np.int64)
        np.put_along_axis(nx, slot[:, :, None, :], own, 3); np.put_along_axis(nm, slot, m, 2)
        gx = np.roll(nx[..., :U], 1 + t % (N - 1), axis=0); gm = np.roll(nm[..., :U], 1 + t % (N - 1), axis=0)
        best = np.max(judged, axis=(0, 2)); lim = lim + (np.maximum(best[None, :] - lim, 0) >> 2)
        seen.append(lim)
    yn = np.take_along_axis(col, order[:, :, None, :K], 3).reshape(N, 128, K)
    return {"yn": yn.astype(np.float32), "yv": v.astype(np.float32), "ym": m.astype(np.float32), "yg": judged.astype(np.float32), "yt": np.stack(seen, axis=2).astype(np.float32)}

@@ -1,0 +1,661 @@
+from concourse.bass import DstId, RemoteDMATransfer
+from concourse.mybir import AluOpType as OP, AxisListType, ActivationFunctionType as AF
+
+W, L, U, NT, Q = 4096, 192, 64, 7, 1344
+F32, BF, I32, U16 = "float32", "bfloat16", "int32", "uint16"
+MAGIC = 12582912.0
+MAGIC64 = 64 * MAGIC
+CUT = 512
+LATE = []
+NVB = [0, 1, 2]
+YCUT = [0, 448, 1024, 1344]
+SHARE = [6, 6, 6, 4, 4, 4, 8]
+
+
+def _sb(n, dt):
+    return ("sbuf", [128, n], dt)
+
+
+SCRATCH = {
+    "X": _sb(4112, BF), "col": _sb(W, I32), "odi": _sb(84, I32), "odf": _sb(88, F32), "odu": _sb(84, U16),
+    "odE": _sb(Q, F32), "odM": _sb(Q, F32), "odH": _sb(Q, BF), "odB": _sb(Q + 16, BF),
+    "wti": _sb(4, I32), "wtf": _sb(4, F32), "thi": _sb(4, I32), "thf": _sb(4, F32),
+    "pi": _sb(8, I32), "pf": _sb(24, F32), "j16": _sb(192, F32), "ia": _sb(128, F32), "ib": _sb(128, F32), "ic": _sb(128, F32),
+    "li": _sb(96, I32), "lf": _sb(96, F32),
+    "diag": _sb(192, F32), "diagS": _sb(192, F32), "diag4": _sb(64, F32), "clamp": _sb(192, F32),
+    "patg": _sb(64, F32), "pat24": _sb(24, F32), "offc": _sb(192, BF), "kcon": _sb(192, BF), "off12": _sb(12, F32), "qc": _sb(12, F32),
+    "blkf": _sb(128, F32), "blk1": _sb(128, F32), "nblkf": _sb(128, F32), "nblkb": _sb(128, BF), "tri": _sb(128, BF), "sel15": _sb(128, F32),
+    "idf": _sb(128, F32), "idb": _sb(128, BF), "nid": _sb(128, BF), "n2k": _sb(128, BF), "dbeta": _sb(128, BF),
+    "selA": _sb(2048, BF), "selW": _sb(2048, BF), "negE": _sb(1024, BF),
+    "bc84": _sb(84, U16), "bc4": _sb(4, U16), "bcp": _sb(4, U16), "bcg": _sb(4, U16), "perm1": _sb(12, U16), "perm2": _sb(12, U16),
+    "St": _sb(48, F32), "S2": _sb(48, F32), "nf3": _sb(48, F32), "free": _sb(16, F32), "kcnf": _sb(12, F32), "cur0": _sb(4, F32),
+    "idxu": _sb(12, U16), "GB": _sb(192, BF), "oi": _sb(12, I32), "oi2": _sb(12, I32), "ou": _sb(12, U16),
+    "v4u": _sb(48, U16), "vu": _sb(12, U16), "freeR": _sb(192, F32), "cbuf": _sb(224, F32), "trb": _sb(416, F32), "xo": _sb(192, U16),
+    "own4": _sb(768, BF), "dif": _sb(3072, BF), "A": _sb(3072, BF), "Gs": _sb(768, BF), "nvb": _sb(192, F32), "cO": _sb(192, F32), "sg": _sb(192, BF),
+    "ed": _sb(192, F32), "pen": _sb(192, BF), "Rb": _sb(200, F32), "keep": _sb(192, F32), "Kb": _sb(192, F32),
+    "Fl": _sb(24, F32), "In": _sb(24, BF), "Cl": _sb(12, F32), "lv": _sb(12, F32), "t1": _sb(12, F32), "t2": _sb(12, F32),
+    "leave": _sb(12, F32), "idxf": _sb(12, F32), "limoff": _sb(12, F32), "limh": _sb(8, F32), "tiny": _sb(8, F32),
+    "u1": _sb(12, F32), "u2": _sb(12, F32), "u3": _sb(12, F32), "slu": _sb(12, U16), "mt": _sb(16, F32), "mE": _sb(192, F32), "ownc": _sb(192, F32),
+    "snd": _sb(4 * 256, F32), "lnd": _sb(4 * 64, F32), "gy": _sb(64, F32), "gxc": _sb(64, BF), "gx": _sb(64, BF), "gxT": _sb(128, BF),
+    "mR": _sb(64, F32), "hi": _sb(4, I32), "hi2": _sb(4, I32), "hu": _sb(4, U16), "gcu": _sb(64, U16), "G": _sb(1024, BF), "Ag": _sb(1024, BF),
+    "Rg": _sb(64, F32), "Eg": _sb(64, F32), "jud": _sb(64, F32), "bl": _sb(32, F32),
+    "yni": _sb(Q, I32), "ynf": _sb(Q, F32), "yvf": _sb(12, F32), "ymf": _sb(12, F32),
+}
+for _b in range(8):
+    SCRATCH["ps%d" % _b] = ("psum", [128, 512], F32)
+
+NDMA = 13
+SEMAPHORES = ["cV", "cS", "cP", "cG", "sent"] + ["d%d" % i for i in range(NDMA)] + ["ga%d" % i for i in range(4)] + ["gb%d" % i for i in range(4)]
+
+
+def _emit(g, T, ops):
+    queue = {"V": g.vector, "S": g.scalar, "P": g.tensor, "G": g, "Y": g.sync}
+    writer, readers, banks = {}, {}, {}
+    known = {e: {} for e in queue}
+    for n, o in enumerate(ops):
+        e = o["e"]
+        deps = set(writer[k] for k in o["r"] + o["w"] if k in writer)
+        for k in o["w"]:
+            deps.update(readers.get(k, []))
+        for b in o["b"]:
+            deps.update(m for f, m in banks.setdefault(b, {}).items() if f != e)
+            banks[b][e] = n
+        o["need"] = []
+        for m in sorted(deps, reverse=True):
+            key = ("dma", m) if ops[m]["dma"] is not None else ops[m]["e"]
+            if known[e].get(key, -1) >= m:
+                continue
+            o["need"].append(m)
+            ops[m]["inc"] = True
+            for kk, vv in ops[m]["clock"].items():
+                known[e][kk] = max(known[e].get(kk, -1), vv)
+            known[e][key] = m
+        o["clock"] = dict(known[e])
+        for k in o["r"]:
+            readers.setdefault(k, []).append(n)
+        for k in o["w"]:
+            writer[k] = n
+            readers[k] = []
+    count = {e: 0 for e in queue}
+    for o in ops:
+        q = queue[o["e"]]
+        for m in o["need"]:
+            q.wait_ge(*ops[m]["done"])
+        for s, v in o["wait"]:
+            q.wait_ge(s, v)
+        if o["f"] is None:
+            continue
+        ins = o["f"]()
+        if o["dma"] is not None:
+            o["done"] = (T.sem["d%d" % o["dma"]], 16)
+            ins.then_inc(*o["done"])
+        elif o["inc"]:
+            count[o["e"]] += 1
+            o["done"] = (T.sem["c" + o["e"]], count[o["e"]])
+            ins.then_inc(o["done"][0], 1)
+
+
+def rank_program(g, core, T, topo):
+    rank = T.rank_of(core)
+    if rank is None:
+        return
+    N = len(T.cores)
+    ops = []
+    ndma = [0]
+    V, S, PE = g.vector, g.scalar, g.tensor
+
+    def op(e, f, r=(), w=(), b=(), wait=(), dma=None):
+        ops.append({"e": e, "f": f, "r": list(r), "w": list(w), "b": list(b), "wait": list(wait), "dma": dma, "inc": False})
+
+    def dma(e, out, in_, r, w):
+        q = g.sync if e == "Y" else g.scalar
+        op(e, lambda: q.dma_start(out, in_), r, w, dma=ndma[0])
+        ndma[0] += 1
+
+    def tt(out, a, b_, o, r, w, b=()):
+        op("V", lambda: V.tensor_tensor(out, a, b_, o), r, w, b)
+
+    def ts(out, a, s1, s2, o0, o1, r, w, b=()):
+        if o1 is None:
+            op("V", lambda: V.tensor_scalar(out, a, s1, None, o0), r, w, b)
+        else:
+            op("V", lambda: V.tensor_scalar(out, a, s1, s2, o0, o1), r, w, b)
+
+    def cp(out, a, r, w, b=()):
+        op("V", lambda: V.tensor_copy(out, a), r, w, b)
+
+    def ms(out, c, w):
+        op("V", lambda: V.memset(out, c), (), w)
+
+    def scan(out, d0, d1, o0, o1, r, w, b=()):
+        op("V", lambda: V.tensor_tensor_scan(out, d0, d1, 0.0, o0, o1), r, w, b)
+
+    def red(out, a, r, w, wait=()):
+        op("V", lambda: V.tensor_reduce(out, a, AxisListType.X, OP.max), r, w, wait=wait)
+
+    def act(out, a, fn, r, w, bias=0.0, scale=1.0, b=(), wait=()):
+        op("S", lambda: S.activation(out, a, fn, bias=bias, scale=scale), r, w, b, wait)
+
+    def mm(out, lhsT, rhs, st, sp, r, b):
+        op("P", lambda: PE.matmul(out, lhsT, rhs, st, sp), r, (), [b])
+
+    def iota(out, pat, base, cm, w, small=True):
+        if small:
+            op("G", lambda: g.iota(out, pat, base, cm, allow_small_or_imprecise_dtypes=True), (), w)
+        else:
+            op("G", lambda: g.iota(out, pat, base, cm), (), w)
+
+    def pick(out, a, pat, o, base, cm, r, w):
+        op("G", lambda: g.affine_select(out, a, pat, o, 0.0, base, cm), r, w)
+
+    PK, PC, PD, PP, PG0, PG1, PQ, PH = [T["ps%d" % i] for i in range(8)]
+    PG = ((PG0, 4), (PG1, 5))
+    Xw = T.X[:, 0:4112]
+    colw = T.col[:, 0:W]
+
+    dma("Y", T.odi[:], T.od[:], [], ["odi"])
+    dma("Y", T.col[:], T.nb[:], [], ["col"])
+    dma("Y", T.X[:, 0:W], T.xs[:], [], ["Xa"])
+    ms(T.thi[:], 0, ["thi"])
+    ms(T.selA[:], 0.0, ["selA0"])
+    dma("S", T.X[:, W:W + 16], T.xs[:, 0:16], [], ["Xb"])
+    dma("S", T.wti[:, 0:1], T.wt[:], [], ["wti"])
+    dma("S", T.thi[0:128:16, 0:1], T.th[:], [], ["thi"])
+    XK = ["Xa", "Xb"]
+
+    pm, pp, gam, pc15, pper = (T.pf[:, i:i + 1] for i in range(5))
+    iota(T.pi[:, 0:1], [[0, 1]], 0, 1, ["pi0"], False)
+    iota(T.j16[:], [[0, 12], [1, 16]], 0, 0, ["j16"])
+    iota(T.li[:, 0:84], [[1, 84]], 0, 0, ["li"], False)
+    iota(T.ia[:], [[-16, 8], [0, 16]], 0, 1, ["ia"])
+    iota(T.idf[:], [[1, 128]], 0, -1, ["idf0"])
+    ts(T.pi[:, 1:2], T.pi[:, 0:1], 15, None, OP.bitwise_and, None, ["pi0"], ["pi1"])
+    ms(T.odB[:, 0:1], 0.0, ["odB0"])
+    cp(pm, T.pi[:, 1:2], ["pi1"], ["pm"])
+    ts(T.diag[:], T.j16[:], pm, None, OP.is_equal, None, ["j16", "pm"], ["diag"])
+    cp(T.bc84[:], T.li[:, 0:84], ["li"], ["bc84"])
+    ts(T.pf[:, 16:17], pm, 1.0, None, OP.is_equal, None, ["pm"], ["p16"])
+    ts(T.pf[:, 17:18], pm, 0.0, None, OP.not_equal, None, ["pm"], ["p17"])
+    ts(T.ib[:], T.ia[:], 0.0, None, OP.is_ge, None, ["ia"], ["ib"])
+    ts(T.ic[:], T.ia[:], 15.0, None, OP.is_le, None, ["ia"], ["ic"])
+    ts(gam, T.pf[:, 16:17], 32.0, T.pf[:, 17:18], OP.mult, OP.add, ["p16", "p17"], ["gam"])
+    ts(T.pf[:, 18:19], T.pf[:, 16:17], T.pf[:, 17:18], -1.0, OP.add, OP.add, ["p16", "p17"], ["p18"])
+    tt(T.blkf[:], T.ib[:], T.ic[:], OP.mult, ["ib", "ic"], ["blkf"])
+    ts(T.ib[:], T.j16[:, 0:128], 1.0, None, OP.is_equal, None, ["j16"], ["ib"])
+    ts(T.idf[:], T.idf[:], 0.0, None, OP.is_equal, None, ["idf0"], ["idf"])
+    ts(T.odf[:, 0:84], T.odi[:], 4048.0, None, OP.add, None, ["odi"], ["odf"])
+    tt(T.blk1[:], T.ib[:], T.blkf[:], OP.mult, ["ib", "blkf"], ["blk1"])
+    act(T.dbeta[:], T.idf[:], AF.Copy, ["idf", "p18"], ["dbeta"], scale=T.pf[:, 18:19])
+    def od_spread(c):
+        tt(T.odE[:, 192 * c:192 * c + 192], T.odf[:, 0:84].indirect(T.bc84[:, 12 * c:12 * c + 12]), T.diag[:], OP.mult,
+           ["odf", "bc84", "diag"], ["odE%d" % c])
+
+    PIECES = [(0, 192, 7, 6), (192, 576, 7, 6), (576, 960, 7, 6), (960, 1344, 7, 6)]
+
+    def od_a(c):
+        lo, hi, b1, b2 = PIECES[c]
+        need = ["odE%d" % i for i in range(lo // 192, hi // 192)]
+        mm(T["ps%d" % b1][:, 0:hi - lo], T.blkf[:], T.odE[:, lo:hi], True, True, ["blkf"] + need, b1)
+        mm(T["ps%d" % b2][:, 0:hi - lo], T.blk1[:], T.odE[:, lo:hi], True, False, ["blk1"] + need, b2)
+
+    def od_b(c):
+        lo, hi, b1, b2 = PIECES[c]
+        act(T.odM[:, lo:hi], T["ps%d" % b1][:, 0:hi - lo], AF.Identity, [], ["odM%d" % c], bias=MAGIC64, b=[b1])
+        act(T.odH[:, lo:hi], T.odM[:, lo:hi], AF.Identity, ["odM%d" % c], ["odH%d" % c], bias=MAGIC64, scale=-1.0)
+        mm(T["ps%d" % b2][:, 0:hi - lo], T.dbeta[:], T.odH[:, lo:hi], False, True, ["dbeta", "odH%d" % c], b2)
+
+    def od_c(c):
+        lo, hi, b1, b2 = PIECES[c]
+        act(T.odB[:, 1 + lo:1 + hi], T["ps%d" % b2][:, 0:hi - lo], AF.Identity, ["gam"], ["odB%d" % (c + 1)], bias=gam, b=[b2])
+
+    od_spread(0)
+    od_a(0)
+    od_b(0)
+    od_c(0)
+    ODB = ["odB%d" % i for i in range(5)]
+    iota(T.lf[:, 0:12], [[1, 12]], 1, 0, ["lf0"])
+    iota(T.lf[:, 12:24], [[1, 4], [64, 3]], 0, 0, ["lf1"])
+    iota(T.lf[:, 24:36], [[16, 12]], 0, 0, ["lf2"])
+    iota(T.lf[:, 36:48], [[0, 6], [1, 2]], 0, 0, ["lf3"])
+    iota(T.lf[:, 48:51], [[4, 3]], 0, 0, ["lf4"])
+    iota(T.off12[:], [[4096, 12]], 5 * 4096, 0, ["off12"])
+    iota(T.clamp[:], [[4096, 12], [0, 16]], 4 * 4096 + 1, 0, ["clamp0"])
+    iota(T.ed[:], [[16, 12], [-1, 16]], 15, 0, ["ed"])
+    iota(T.diag4[:], [[1, 16], [0, 4]], 0, 0, ["diag4a"])
+    act(T.offc[:], T.clamp[:], AF.Identity, ["clamp0"], ["offc"], bias=4095.0)
+    act(T.tri[:], T.blkf[:], AF.Copy, ["blkf"], ["tri"])
+    pick(T.clamp[:], T.clamp[:], [[0, 12], [1, 16]], OP.is_equal, 0, 0, ["clamp0"], ["clamp0", "clamp"])
+    pick(T.tri[:], T.tri[:], [[1, 128]], OP.is_gt, 0, -1, ["tri"], ["tri"])
+    pick(T.sel15[:], T.blkf[:], [[-16, 8], [0, 16]], OP.is_equal, -15, 1, ["blkf"], ["sel15"])
+    iota(T.Rb[:, 0:1], [[0, 1]], 0, 0, ["Rb0"])
+    iota(T.free[:], [[0, 16]], 0, 0, ["free"])
+    iota(T.cur0[:], [[0, 4]], L, 0, ["cur0"])
+    iota(T.pat24[:], [[0, 24]], 1, 0, ["pat24"])
+    iota(T.Fl[:], [[0, 24]], 0, 0, ["dead", "go"])
+    iota(T.pat24[:, 12:13], [[0, 1]], 0, 0, ["pat24"])
+    iota(T.mt[:], [[0, 16]], 0, 0, ["mt"])
+    iota(T.patg[:], [[0, 64]], -65536, 0, ["patg"])
+    iota(T.negE[:], [[0, 1024]], -1, 0, ["negE"])
+    pick(T.patg[:], T.patg[:], [[0, 4], [1, 16]], OP.is_equal, 0, 0, ["patg"], ["patg"])
+    pick(T.negE[:], T.negE[:], [[1, 64], [0, 16]], OP.is_equal, 0, -1, ["negE"], ["negE"])
+    iota(T.snd[:], [[0, 1024]], 0, 0, ["snd0", "snd1", "snd2", "snd3"])
+    for a in range(16):
+        ts(T.selA[:, 129 * a:128 * a + 128:16], T.blkf[:, 0:128:16], -1.0, None, OP.mult, None, ["blkf", "selA0"], ["selA%d" % (a + 1)])
+    SELA = ["selA%d" % i for i in range(17)]
+    ts(T.pi[:, 2:3], T.pi[:, 1:2], 2, None, OP.arith_shift_right, None, ["pi1"], ["pi2"])
+    ts(T.pi[:, 3:4], T.pi[:, 1:2], 3, None, OP.bitwise_and, None, ["pi1"], ["pi3"])
+    ts(T.pi[:, 4:5], T.pi[:, 0:1], 4, 1, OP.arith_shift_right, OP.bitwise_and, ["pi0"], ["pi4"])
+    ts(T.pi[:, 5:6], T.pi[:, 0:1], 2, 1, OP.arith_shift_right, OP.bitwise_and, ["pi0"], ["pi5"])
+    ts(T.pf[:, 5:6], pm, 12.0, None, OP.mult, None, ["pm"], ["p12"])
+    cp(T.pf[:, 8:12], T.pi[:, 2:6], ["pi2", "pi3", "pi4", "pi5"], ["p8"])
+    ts(T.idxu[:], T.lf[:, 0:12], T.pf[:, 5:6], None, OP.add, None, ["lf0", "p12"], ["idxu"])
+    ms(T.S2[:], 0.0, ["S2"])
+    ms(T.St[:], 0.0, ["vp", "M", "nfp"])
+    ms(T.kcnf[:], 0.0, ["kcnf"])
+    ms(T.cbuf[:, 0:16], 0.0, ["c0"])
+    ms(T.cbuf[:, 208:224], 0.0, ["c1"])
+    ts(T.bc4[:, 0:3], T.lf[:, 48:51], T.pf[:, 8:9], None, OP.add, None, ["lf4", "p8"], ["bc4"])
+    tt(T.pf[:, 6:7], T.pf[:, 10:11], T.pf[:, 11:12], OP.not_equal, ["p8"], ["p6"])
+    ts(T.pf[:, 7:8], T.pf[:, 8:9], 16.0, None, OP.mult, None, ["p8"], ["p7"])
+    ts(T.lf[:, 52:64], T.lf[:, 36:48], T.pf[:, 10:11], 208.0, OP.not_equal, OP.mult, ["lf3", "p8"], ["lf5"])
+    ts(T.pf[:, 12:13], T.pf[:, 9:10], 4.0, T.pf[:, 7:8], OP.mult, OP.add, ["p8", "p7"], ["p12b"])
+    tt(T.lf[:, 64:76], T.lf[:, 52:64], T.lf[:, 24:36], OP.add, ["lf5", "lf2"], ["lf6"])
+    ts(pper, T.pf[:, 6:7], 208.0, T.pf[:, 12:13], OP.mult, OP.add, ["p6", "p12b"], ["pper"])
+    ts(T.perm2[:], T.lf[:, 64:76], pm, None, OP.add, None, ["lf6", "pm"], ["perm2"])
+    ts(T.perm1[:], T.lf[:, 12:24], pper, None, OP.add, None, ["lf1", "pper"], ["perm"])
+    act(T.idb[:], T.idf[:], AF.Copy, ["idf"], ["idb"])
+    act(T.n2k[:], T.idf[:], AF.Copy, ["idf"], ["n2k"], scale=-2048.0)
+    act(T.nid[:], T.idf[:], AF.Copy, ["idf"], ["nid"], scale=-1.0)
+    for c in range(1, 4):
+        od_spread(c)
+    act(T.kcon[:], T.ed[:], AF.Copy, ["ed"], ["kcon"], scale=8192.0)
+
+    def late_constants():
+        ts(T.qc[:], T.lf[:, 24:36], pm, 65.0, OP.add, OP.add, ["lf2", "pm"], ["qc"])
+        ts(T.bcp[:], T.lf[:, 0:4], 0.0, pm, OP.mult, OP.add, ["lf0", "pm"], ["bcp"])
+        ts(T.pf[:, 13:14], T.pf[:, 9:10], 16.0, 15.0, OP.mult, OP.add, ["p8"], ["p13"])
+        ts(T.bcg[:], T.lf[:, 0:4], 0.0, T.pf[:, 13:14], OP.mult, OP.add, ["lf0", "p13"], ["bcg"])
+
+    def input_constants():
+        cp(T.thf[:, 0:1], T.thi[:, 0:1], ["thi"], ["thf"])
+        ts(T.wtf[:, 0:1], T.wti[:, 0:1], -1.0, None, OP.mult, None, ["wti"], ["wtf"])
+        mm(PH[:, 8:9], T.blkf[:], T.thf[:, 0:1], True, True, ["blkf", "thf"], 7)
+        ts(T.diag4[:], T.diag4[:], pm, None, OP.is_equal, None, ["diag4a", "pm"], ["diag4"])
+        cp(T.odu[:], T.odi[:], ["odi"], ["odu"])
+        ts(T.limh[:, 0:3], T.lf[:, 0:3], 0.0, PH[:, 8:9], OP.mult, OP.add, ["lf0"], ["lim2"], [7])
+        ts(T.limoff[:], T.off12[:], T.limh[:, 2:3], None, OP.subtract, None, ["off12", "lim2"], ["limoff"])
+
+    def guest_constants(t):
+        if t == 0:
+            act(T.nblkb[:], T.blkf[:], AF.Copy, ["blkf"], ["nblkb"], scale=-1.0)
+            act(T.nblkf[:], T.blkf[:], AF.Copy, ["blkf"], ["nblkf"], scale=-1.0)
+            act(T.diagS[:], T.diag[:], AF.Copy, ["diag"], ["diagS"], scale=1.0 / 8192)
+            limits(2)
+        lo, hi = (0, 384, 1152, 2048)[t:t + 2]
+        act(T.selW[:, lo:hi], T.selA[:, lo:hi], AF.Copy, SELA + ["wtf"], ["selW"], scale=T.wtf[:, 0:1])
+
+    vp, M = T.St[:, 0:12], T.St[:, 16:28]
+    dead, go = T.Fl[:, 0:12], T.Fl[:, 12:24]
+    Id, Ig = T.In[:, 0:12], T.In[:, 12:24]
+    cnat = T.cbuf[:, 16:208]
+    nsent = [0]
+
+    def state():
+        ts(T.nf3[:], T.free[:, 0:16].indirect(T.bcp[:, 0:3]), -1.0, 1.0, OP.mult, OP.add, ["free", "bcp"], ["nf3"])
+
+    def state2():
+        tt(T.S2[:], T.St[:], T.nf3[:], OP.mult, ["vp", "M", "nfp", "nf3"], ["S2"])
+
+    def state3():
+        tt(T.kcnf[:], T.Kb[:, 15:192:16], T.nf3[:, 0:12], OP.mult, ["Kb", "nf3"], ["kcnf"])
+
+    def leavers(t):
+        i = t - 2
+        tt(T.u1[:], T.Cl[:], T.qc[:], OP.subtract, ["Cl", "qc"], ["u1"])
+        tt(T.mt[:, 0:12], T.off12[:], M, OP.subtract, ["off12", "M"], ["mt"])
+        tt(T.u2[:], T.u1[:], T.leave[:], OP.mult, ["u1", "leave"], ["u2"])
+        tt(T.mE[:], T.mt[:, 0:16].indirect(T.bc84[:, 0:12]), T.diagS[:], OP.mult, ["mt", "bc84", "diagS"], ["mE"])
+        tt(T.u3[:], T.u2[:], T.qc[:], OP.add, ["u2", "qc"], ["u3"])
+        state()
+        ts(T.slu[:], T.u3[:], -1.0, None, OP.add, None, ["u3"], ["slu"])
+        state2()
+        tt(T.snd[:, 256 * i:256 * i + 256].indirect(T.slu[:]), T.ownc[:], T.mE[:], OP.add, ["slu", "ownc", "mE"], ["snd%d" % i])
+        dst = T.cores[(rank + 1 + t % (N - 1)) % N]
+        rid, pid, _ = topo.addr(dst)
+        mask = topo.mask(core, dst)
+        op("G", lambda: g.remote_dma(T.lnd[:, 64 * i:64 * i + 64], T.snd[:, 256 * i:256 * i + 64], T.sem["ga%d" % i], T.sem.sent, pid, rid, mask),
+           ["snd%d" % i])
+        nsent[0] += len(topo.engines(core, dst))
+
+    def unpack(t):
+        i = t - 3
+        src = T.cores[(rank - 1 - (t - 1) % (N - 1)) % N]
+        p = T.lnd[:, 64 * i:64 * i + 64]
+        act(T.gy[:], p, AF.Identity, [], ["gy"], bias=MAGIC, wait=[(T.sem["ga%d" % i], len(topo.engines(src, core)))])
+        act(T.gx[:], T.gy[:], AF.Identity, ["gy"], ["gx"], bias=128.0 - MAGIC)
+        act(T.gxc[:], T.gy[:], AF.Identity, ["gy"], ["gxc"], bias=-MAGIC)
+
+    def unpack_p(t):
+        p = T.lnd[:, 64 * (t - 3):64 * (t - 3) + 64]
+        for a in range(16):
+            mm(PH[:, 0:4], T.selW[:, 128 * a:128 * a + 128], T.gx[:, a:64:16], a == 0, a == 15, ["selW", "gx"], 7)
+        mm(PD[0:64, 256:384], T.gx[:], T.idb[:], True, True, ["gx", "idb"], 2)
+        mm(PD[:, 384:448], T.blkf[:], p, True, False, ["blkf", "gxc"], 2)
+        mm(PD[:, 384:448], T.nblkb[:], T.gxc[:], False, True, ["nblkb", "gxc"], 2)
+
+    def unpack2():
+        act(T.gxT[0:64, :], PD[0:64, 256:384], AF.Copy, [], ["gxT"], b=[2])
+        act(T.mR[:], PD[:, 384:448], AF.Copy, [], ["mR"], scale=8192.0, b=[2])
+
+    def hchain(t, best=False):
+        ts(T.hi[:], PH[:, 0:4], 77.0 * t, None, OP.add, None, [], ["hi"], [7])
+        ts(T.hi2[:], T.hi[:], W - 1, None, OP.bitwise_and, None, ["hi"], ["hi2"])
+        cp(T.hu[:], T.hi2[:], ["hi2"], ["hu"])
+        if best:
+            thresholds(t - 1)
+        cp(T.gcu[:], colw.indirect(T.hu[:]), ["col", "hu"], ["gcu"])
+
+    def gdist_a(halves=False):
+        if halves:
+            for h in range(2):
+                act(T.G[:, 512 * h:512 * h + 512], Xw.indirect(T.gcu[:, 32 * h:32 * h + 32]), AF.Copy, XK + ["gcu"], ["G%d" % h])
+        else:
+            act(T.G[:], Xw.indirect(T.gcu[:]), AF.Copy, XK + ["gcu"], ["G0", "G1"])
+
+    def gdist_p():
+        for h, (bank, nm) in enumerate(PG):
+            mm(bank[:], T.gxT[0:64, :], T.negE[0:64, 512 * h:512 * h + 512], True, False, ["gxT", "negE"], nm)
+            mm(bank[:], T.idb[:], T.G[:, 512 * h:512 * h + 512], False, True, ["idb", "G%d" % h], nm)
+
+    def gdist_s(h):
+        act(T.Ag[:, 512 * h:512 * h + 512], PG[h][0][:], AF.Abs, [], ["Ag%d" % h], b=[PG[h][1]])
+
+    def gdist_r():
+        for a in range(16):
+            mm(PQ[:, 0:64], T.selA[:, 128 * a:128 * a + 128], T.Ag[:, 64 * a:64 * a + 64], a == 0, a == 15, SELA + ["Ag%d" % (a // 8)], 6)
+
+    def judge_a():
+        scan(T.Rg[:], T.patg[:], PQ[:, 0:64], OP.add, OP.max, ["patg"], ["Rg"], [6])
+        tt(T.Eg[:], T.Rg[:, 0:64].indirect(T.bcg[:]), T.diag4[:], OP.mult, ["Rg", "bcg", "diag4"], ["Eg"])
+        mm(PQ[:, 64:128], T.nblkf[:], T.Eg[:], True, True, ["nblkf", "Eg"], 6)
+
+    def to_all(s):
+        mask = -1
+        for d in T.cores:
+            if d != s:
+                mask &= topo.mask(s, d)
+        return mask
+
+    def judge_b(t):
+        i = t - 3
+        tt(T.jud[:], PQ[:, 64:128], T.mR[:], OP.min, ["mR"], ["jud"], [6])
+        red(T.bl[:, 8 * i + 4:8 * i + 5], T.jud[:], ["jud"], ["bl%d" % i])
+        ids, dsts = [], []
+        for d in range(1, N):
+            rid, pid, _ = topo.addr(T.cores[(rank + d) % N])
+            ids.append(DstId(rid=rid, pnc=pid))
+            dsts.append(T.bl[:, 8 * i + d:8 * i + d + 1])
+        tr = RemoteDMATransfer(dst_ids=ids, dma_engine_mask=to_all(core), remote_sem=T.sem["gb%d" % i], srcs=[T.bl[:, 8 * i + 4:8 * i + 5]], dsts=dsts)
+        op("G", lambda: g.remote_dma_fused([tr], local_sem=T.sem.sent), ["bl%d" % i])
+        nsent[0] += bin(to_all(core)).count("1")
+
+    def thresholds(t):
+        i = t - 3
+        n = sum(bin(to_all(s)).count("1") for s in T.cores if s != core)
+        red(T.tiny[:, 0:1], T.bl[:, 8 * i + 1:8 * i + 5], ["bl%d" % i], ["bq"], wait=[(T.sem["gb%d" % i], n)])
+
+    def thresholds_s(t):
+        bq, y, z, nlim, nl4, limM, nlimM = (T.tiny[:, j:j + 1] for j in range(7))
+        act(y, bq, AF.Relu, ["bq", "nl4"], ["y"], bias=nl4, scale=0.25)
+        act(z, y, AF.Identity, ["y"], ["z"], bias=MAGIC)
+        if t < NT - 2:
+            act(nlim, z, AF.Identity, ["z", "nlimM"], ["nlim"], bias=nlimM, scale=-1.0)
+        act(T.limh[:, t:t + 1], z, AF.Identity, ["z", "limM"], ["lim%d" % t], bias=limM)
+        if t < NT - 2:
+            act(T.limoff[:], T.off12[:], AF.Identity, ["off12", "nlim"], ["limoff"], bias=nlim)
+        if t < NT - 1:
+            limits(t)
+
+    def limits(t):
+        lim = T.limh[:, t:t + 1]
+        act(T.tiny[:, 4:5], lim, AF.Identity, ["lim%d" % t], ["nl4"], bias=-0.375, scale=-0.25)
+        act(T.tiny[:, 5:6], lim, AF.Identity, ["lim%d" % t], ["limM"], bias=-MAGIC)
+        if t < NT - 3:
+            act(T.tiny[:, 6:7], lim, AF.Identity, ["lim%d" % t], ["nlimM"], bias=MAGIC, scale=-1.0)
+
+    def gath(c, lo=0, hi=768):
+        tt(T.dif[:, 768 * c + lo:768 * c + hi], Xw.indirect(T.xo[:, 48 * c + lo // 16:48 * c + hi // 16]), T.own4[:, lo:hi], OP.subtract,
+           XK + ["xo", "own4", "own4b"], ["dif%d_%d" % (c, lo > 0)])
+
+    def absol(c, lo=0, hi=768):
+        act(T.A[:, 768 * c + lo:768 * c + hi], T.dif[:, 768 * c + lo:768 * c + hi], AF.Abs, ["dif%d_%d" % (c, lo > 0)], ["A%d_%d" % (c, lo > 0)])
+
+    def ksum(c, stop, more=()):
+        for a in range(16):
+            mm(PK[:, c:192:4], T.selA[:, 128 * a:128 * a + 128], T.A[:, 768 * c + a:768 * c + 768:16], False, stop and a == 15,
+               SELA + ["A%d_0" % c, "A%d_1" % c] + list(more), 0)
+
+    def share_a(n):
+        act(T.Gs[:, 0:n], Xw.indirect(T.xo[:, 192 - n // 16:192]), AF.Copy, XK + ["xo"], ["Gs"])
+        for h, (bank, nm) in enumerate(PG):
+            lo, hi = 512 * h, min(n, 512 * h + 512)
+            if lo < hi:
+                mm(bank[:, 0:hi - lo], T.nid[:], T.own4[:, 768 - n + lo:768 - n + hi], True, False, ["nid", "own4", "own4b"], nm)
+                mm(bank[:, 0:hi - lo], T.idb[:], T.Gs[:, lo:hi], False, True, ["idb", "Gs"], nm)
+
+    def share_b(n):
+        for h, (bank, nm) in enumerate(PG):
+            lo, hi = 512 * h, min(n, 512 * h + 512)
+            if lo < hi:
+                act(T.A[:, 3072 - n + lo:3072 - n + hi], bank[:, 0:hi - lo], AF.Abs, [], ["As%d" % h, "A3_1"], b=[nm])
+
+    def ynpart(c, second):
+        lo, hi = YCUT[c:c + 2]
+        if not second:
+            ts(T.yni[:, lo:hi], colw.indirect(T.odu[:, lo // 16:hi // 16]), W - 1, None, OP.bitwise_and, None, ["col", "odu"], ["yni%d" % c])
+            return
+        cp(T.ynf[:, lo:hi], T.yni[:, lo:hi], ["yni%d" % c], ["ynf%d" % c])
+        dma("Y", T.yn[:, lo:hi], T.ynf[:, lo:hi], ["ynf%d" % c], ["out%d" % c])
+
+    for t in range(NT):
+        last = t == NT - 1
+        ns = 64 * SHARE[t]
+        pc = min(t, 3)
+        act(T.GB[:], T.odB[:, 0:PIECES[pc][1] + 1].indirect(T.idxu[:]), AF.Copy, ODB[:pc + 2] + ["idxu"], ["GB"])
+        if t >= 4:
+            gdist_p()
+        for a in range(16):
+            mm(PH[:, 16:28], T.selA[:, 128 * a:128 * a + 128], T.GB[:, a:192:16], a == 0, a == 15, SELA + ["GB"], 7)
+        if t >= 4:
+            gdist_s(0)
+            gdist_s(1)
+            gdist_r()
+        act(T.freeR[:], T.GB[:], AF.Sign, ["GB"], ["freeR"])
+        if t >= 3:
+            leavers(t - 1)
+            state3()
+        elif t > 0:
+            state()
+            if t - 1 in LATE:
+                cp(colw.indirect(T.vu[:]), cnat, ["vu", "c"], ["col"])
+            state2()
+            state3()
+        tt(vp, T.S2[:, 0:12], PH[:, 16:28], OP.subtract, ["S2"], ["vp"], [7])
+        tt(T.oi[:], T.kcnf[:], PH[:, 16:28], OP.subtract, ["kcnf"], ["oi"], [7])
+        ts(T.v4u[:], T.St[:, 0:16].indirect(T.bc4[:, 0:3]), -4095.0, None, OP.add, None, ["vp", "bc4"], ["v4u"])
+        ts(T.oi2[:], T.oi[:], W - 1, None, OP.bitwise_and, None, ["oi"], ["oi2"])
+        ts(T.vu[:], vp, -4095.0, None, OP.add, None, ["vp"], ["vu"])
+        cp(T.ou[:], T.oi2[:], ["oi2"], ["ou"])
+        if t in NVB:
+            act(T.nvb[:], T.St[:, 0:16].indirect(T.bc84[:, 0:12]), AF.Identity, ["vp", "bc84"], ["nvb"], bias=2047.0, scale=-1.0)
+        if t > 0:
+            act(T.own4[:], Xw.indirect(T.v4u[:]), AF.Copy, XK + ["v4u"], ["own4", "own4b"])
+        if t == 0:
+            for c in range(4, 7):
+                od_spread(c)
+        tt(cnat, colw.indirect(T.ou[:]), T.freeR[:], OP.add, ["col", "ou", "freeR"], ["c"])
+        if t >= 4:
+            judge_a()
+        op("V", lambda: V.transpose(T.trb[:, 0:192], T.cbuf[:, 16:208]), ["c"], ["tr1"])
+        op("V", lambda: V.transpose(T.trb[:, 192:416], T.cbuf[:, 0:224]), ["c", "c0", "c1"], ["tr2"])
+        cp(T.xo[:], T.trb[:, 0:416].indirect(T.perm1[:]), ["tr1", "tr2", "perm"], ["xo"])
+        if t >= 4:
+            judge_b(t - 1)
+        if t not in NVB:
+            act(T.nvb[:], T.St[:, 0:16].indirect(T.bc84[:, 0:12]), AF.Identity, ["vp", "bc84"], ["nvb"], bias=2047.0, scale=-1.0)
+        act(T.cO[:], T.trb[:, 0:416].indirect(T.perm2[:]), AF.Copy, ["tr1", "tr2", "perm2"], ["cO"])
+        act(T.sg[:], T.cO[:], AF.Sign, ["cO"], ["sg"], bias=-4095.5)
+        mm(PK[:, 0:192], T.idb[:], T.offc[:], True, False, ["idb", "offc"], 0)
+        mm(PD[:, 0:192], T.idf[:], T.nvb[:], True, False, ["idf", "nvb"], 2)
+        mm(PD[:, 0:192], T.idf[:], T.cO[:], False, False, ["idf", "cO"], 2)
+        mm(PD[:, 0:192], T.n2k[:], T.sg[:], False, True, ["n2k", "sg"], 2)
+        if t == 0:
+            late_constants()
+            act(T.ed[:], PD[:, 0:192], AF.Abs, [], ["ed"], b=[2])
+            act(T.pen[:], T.ed[:], AF.Relu, ["ed"], ["pen"], bias=32.0, scale=-2.0)
+            act(T.own4[:, 384:768], Xw.indirect(T.v4u[:, 24:48]), AF.Copy, XK + ["v4u"], ["own4b"])
+            cp(T.own4[:, 0:384], Xw.indirect(T.v4u[:, 0:24]), XK + ["v4u"], ["own4"])
+        gath(0)
+        if ns and not last:
+            share_a(ns)
+        if t == 0:
+            input_constants()
+        if not last:
+            mm(PC[:, 0:192], T.idb[:], T.kcon[:], True, False, ["idb", "kcon"], 1)
+            mm(PC[:, 0:192], T.idf[:], T.cO[:], False, True, ["idf", "cO"], 1)
+        if t < 3:
+            od_a(t + 1)
+        if last:
+            act(T.ed[:], PD[:, 0:192], AF.Abs, [], ["ed"], b=[2])
+            act(T.pen[:], T.ed[:], AF.Relu, ["ed"], ["pen"], bias=32.0, scale=-2.0)
+            unpack(t)
+            unpack_p(t)
+        absol(0)
+        if 0 < t < NT - 1:
+            act(T.ed[:], PD[:, 0:192], AF.Abs, [], ["ed"], b=[2])
+            act(T.pen[:], T.ed[:], AF.Relu, ["ed"], ["pen"], bias=32.0, scale=-2.0)
+        if last:
+            unpack2()
+        ksum(0, False)
+        mm(PK[:, 0:192], T.n2k[:], T.pen[:], False, False, ["n2k", "pen"], 0)
+        gath(1)
+        if last:
+            hchain(t)
+            gdist_a(True)
+            gdist_p()
+        if ns and not last:
+            share_b(ns)
+        if 3 <= t < NT - 1:
+            unpack(t)
+            unpack_p(t)
+        if last:
+            gdist_s(0)
+            gdist_s(1)
+            gdist_r()
+        if not last:
+            absol(1)
+            ksum(1, False)
+        if 3 <= t < NT - 1:
+            unpack2()
+        if last:
+            gath(2)
+            if ns < 768:
+                gath(3, 0, 768 - ns)
+        elif ns == 768:
+            ksum(3, False, ["As0", "As1"])
+            gath(2, 0, CUT)
+            absol(2, 0, CUT)
+            gath(2, CUT, 768)
+            absol(2, CUT, 768)
+            ksum(2, True)
+        else:
+            gath(2)
+            absol(2)
+            ksum(2, False)
+            if ns == 0 and not last:
+                gath(3, 0, CUT)
+                absol(3, 0, CUT)
+                gath(3, CUT, 768)
+                absol(3, CUT, 768)
+            else:
+                gath(3, 0, 768 - ns)
+                absol(3, 0, 768 - ns)
+            ksum(3, True, ["As0", "As1"])
+        if 3 <= t < NT - 1:
+            hchain(t, t >= 4)
+        if 4 <= t < NT - 1:
+            thresholds_s(t - 1)
+        if 3 <= t < NT - 1:
+            gdist_a()
+        if 2 <= t < NT - 1:
+            act(T.ownc[:], Xw.indirect(T.vu[:]), AF.Identity, XK + ["vu"], ["ownc"], bias=-128.0)
+        if 1 <= t < NT - 2:
+            act(T.St[:, 32:48], T.nf3[:, 0:16], AF.Copy, ["nf3"], ["nfp"])
+        if t < 3:
+            od_b(t + 1)
+        if t < 3:
+            guest_constants(t)
+        if t not in LATE:
+            cp(colw.indirect(T.vu[:]), cnat, ["vu", "c"], ["col"])
+        if last:
+            thresholds(t - 1)
+            ts(T.yvf[:], vp, -4095.0, None, OP.add, None, ["vp"], ["yvf"])
+            dma("Y", T.yv[:], T.yvf[:], ["yvf"], ["outv"])
+            ynpart(0, 0)
+            judge_a()
+            if ns:
+                share_a(ns)
+            absol(1)
+            ksum(1, False)
+            absol(2)
+            ksum(2, False)
+            if ns:
+                share_b(ns)
+            if ns < 768:
+                absol(3, 0, 768 - ns)
+            ksum(3, True, ["As0", "As1"])
+            thresholds_s(t - 1)
+            ynpart(0, 1)
+            judge_b(t)
+            dma("Y", T.yg[:], T.jud[0:128:16, :], ["jud"], ["outg"])
+            for c in (1, 2):
+                ynpart(c, 0)
+                ynpart(c, 1)
+        scan(T.Rb[:, 1:193], T.clamp[:], PK[:, 0:192], OP.max, OP.max, ["clamp"], ["Rb"], [0])
+        tt(M, T.S2[:, 16:28], T.Rb[:, 16:193:16], OP.max, ["S2", "Rb"], ["M"])
+        if last:
+            tt(T.ymf[:], T.off12[:], M, OP.subtract, ["off12", "M"], ["ymf"])
+            dma("Y", T.ym[:], T.ymf[:], ["ymf"], ["outm"])
+            thresholds(t)
+            thresholds_s(t)
+            dma("S", T.yt[:], T.limh[0:128:16, 0:NT], ["lim2", "lim3", "lim4", "lim5", "lim6"], ["outt"])
+            break
+        tt(dead, M, T.limoff[:], OP.is_gt, ["M", "limoff"], ["dead"])
+        tt(T.keep[:], PK[:, 0:192], T.Rb[:, 0:192], OP.is_le, ["Rb", "Rb0"], ["keep"], [0])
+        if t >= 2:
+            tt(go, T.S2[:, 32:44], dead, OP.is_gt, ["S2", "dead"], ["go"])
+        scan(T.In[:], T.pat24[:], T.Fl[:], OP.mult, OP.add, ["pat24", "dead", "go"], ["In"])
+        mm(PP[:, 0:2], T.tri[:], T.In[:, 11:24:12], True, True, ["tri", "In"], 3)
+        scan(T.Kb[:], T.keep[:], PC[:, 0:192], OP.mult, OP.max, ["keep"], ["Kb"], [1])
+        bd, bg = PP[:, 0:1], PP[:, 1:2]
+        cur = T.cur0[:, 0:1] if t == 0 else PP[:, 8 + t:9 + t]
+        if t >= 2:
+            ts(T.Cl[:], Ig, bg, float(U), OP.add, OP.min, ["In"], ["Cl"], [3])
+            ts(T.lv[:], Ig, bg, float(U), OP.add, OP.is_le, ["In"], ["lv"], [3])
+            tt(T.t1[:], T.Cl[:], Id, OP.add, ["Cl", "In"], ["t1"])
+            tt(T.leave[:], T.lv[:], go, OP.mult, ["lv", "go"], ["leave"])
+            ts(T.t2[:], T.t1[:], bd, cur, OP.add, OP.add, ["t1", "cur0"], ["t2"], [3])
+            tt(T.free[:, 0:12], T.leave[:], dead, OP.add, ["leave", "dead"], ["free"])
+            tt(T.idxf[:], T.t2[:], T.free[:, 0:12], OP.mult, ["t2", "free"], ["idxf"])
+        else:
+            ts(T.t2[:], Id, bd, cur, OP.add, OP.add, ["In", "cur0"], ["t2"], [3])
+            cp(T.free[:, 0:12], dead, ["dead"], ["free"])
+            tt(T.idxf[:], T.t2[:], dead, OP.mult, ["t2", "dead"], ["idxf"])
+        cp(T.idxu[:], T.idxf[:], ["idxf"], ["idxu"])
+        if t < NT - 2:
+            mm(PP[:, 9 + t:10 + t], T.sel15[:], T.t2[:, 11:12], True, True, ["sel15", "t2"], 3)
+        if t < 3:
+            od_c(t + 1)
+
+    op("G", None, ["out0", "out1", "out2", "outv", "outg", "outm", "outt"], wait=[(T.sem.sent, nsent[0])])
+    _emit(g, T, ops)

@@ -6,7 +6,9 @@ F32, BF, I32, U16 = "float32", "bfloat16", "int32", "uint16"
 MAGIC = 12582912.0
 MAGIC64 = 64 * MAGIC
 CUT = 512
+OPT = {"hearly": 0, "red": 1, "pen": 1, "shb": 0, "ag": 1, "nfs": 0}
 LATE = []
+THV = [False]
 NVB = [0, 1, 2]
 YCUT = [0, 448, 1024, 1344]
 SHARE = [6, 6, 6, 4, 4, 4, 8]
@@ -34,7 +36,7 @@ SCRATCH = {
     "own4": _sb(768, BF), "dif": _sb(3072, BF), "A": _sb(3072, BF), "Gs": _sb(768, BF), "nvb": _sb(192, F32), "cO": _sb(192, F32), "sg": _sb(192, BF),
     "ed": _sb(192, F32), "pen": _sb(192, BF), "Rb": _sb(200, F32), "keep": _sb(192, F32), "Kb": _sb(192, F32),
     "Fl": _sb(24, F32), "In": _sb(24, BF), "Cl": _sb(12, F32), "lv": _sb(12, F32), "t1": _sb(12, F32), "t2": _sb(12, F32),
-    "leave": _sb(12, F32), "idxf": _sb(12, F32), "limoff": _sb(12, F32), "limh": _sb(8, F32), "tiny": _sb(8, F32),
+    "leave": _sb(12, F32), "idxf": _sb(12, F32), "limoff": _sb(12, F32), "limh": _sb(8, F32), "tiny": _sb(8, F32), "tinyi": _sb(4, I32),
     "u1": _sb(12, F32), "u2": _sb(12, F32), "u3": _sb(12, F32), "slu": _sb(12, U16), "mt": _sb(16, F32), "mE": _sb(192, F32), "ownc": _sb(192, F32),
     "snd": _sb(4 * 256, F32), "lnd": _sb(4 * 64, F32), "gy": _sb(64, F32), "gxc": _sb(64, BF), "gx": _sb(64, BF), "gxT": _sb(128, BF),
     "mR": _sb(64, F32), "hi": _sb(4, I32), "hi2": _sb(4, I32), "hu": _sb(4, U16), "gcu": _sb(64, U16), "G": _sb(1024, BF), "Ag": _sb(1024, BF),
@@ -123,6 +125,9 @@ def rank_program(g, core, T, topo):
 
     def cp(out, a, r, w, b=()):
         op("V", lambda: V.tensor_copy(out, a), r, w, b)
+
+    def turn(out, a, r, w):
+        op("V", lambda: V.transpose(out, a), r, w)
 
     def ms(out, c, w):
         op("V", lambda: V.memset(out, c), (), w)
@@ -222,10 +227,6 @@ def rank_program(g, core, T, topo):
     iota(T.clamp[:], [[4096, 12], [0, 16]], 4 * 4096 + 1, 0, ["clamp0"])
     iota(T.ed[:], [[16, 12], [-1, 16]], 15, 0, ["ed"])
     iota(T.diag4[:], [[1, 16], [0, 4]], 0, 0, ["diag4a"])
-    act(T.offc[:], T.clamp[:], AF.Identity, ["clamp0"], ["offc"], bias=4095.0)
-    act(T.tri[:], T.blkf[:], AF.Copy, ["blkf"], ["tri"])
-    pick(T.clamp[:], T.clamp[:], [[0, 12], [1, 16]], OP.is_equal, 0, 0, ["clamp0"], ["clamp0", "clamp"])
-    pick(T.tri[:], T.tri[:], [[1, 128]], OP.is_gt, 0, -1, ["tri"], ["tri"])
     pick(T.sel15[:], T.blkf[:], [[-16, 8], [0, 16]], OP.is_equal, -15, 1, ["blkf"], ["sel15"])
     iota(T.Rb[:, 0:1], [[0, 1]], 0, 0, ["Rb0"])
     iota(T.free[:], [[0, 16]], 0, 0, ["free"])
@@ -235,10 +236,10 @@ def rank_program(g, core, T, topo):
     iota(T.pat24[:, 12:13], [[0, 1]], 0, 0, ["pat24"])
     iota(T.mt[:], [[0, 16]], 0, 0, ["mt"])
     iota(T.patg[:], [[0, 64]], -65536, 0, ["patg"])
-    iota(T.negE[:], [[0, 1024]], -1, 0, ["negE"])
     pick(T.patg[:], T.patg[:], [[0, 4], [1, 16]], OP.is_equal, 0, 0, ["patg"], ["patg"])
-    pick(T.negE[:], T.negE[:], [[1, 64], [0, 16]], OP.is_equal, 0, -1, ["negE"], ["negE"])
-    iota(T.snd[:], [[0, 1024]], 0, 0, ["snd0", "snd1", "snd2", "snd3"])
+    ts(T.pf[:, 5:6], pm, 12.0, None, OP.mult, None, ["pm"], ["p12"])
+    ms(T.S2[:], 0.0, ["S2"])
+    ts(T.idxu[:], T.lf[:, 0:12], T.pf[:, 5:6], None, OP.add, None, ["lf0", "p12"], ["idxu"])
     for a in range(16):
         ts(T.selA[:, 129 * a:128 * a + 128:16], T.blkf[:, 0:128:16], -1.0, None, OP.mult, None, ["blkf", "selA0"], ["selA%d" % (a + 1)])
     SELA = ["selA%d" % i for i in range(17)]
@@ -246,11 +247,8 @@ def rank_program(g, core, T, topo):
     ts(T.pi[:, 3:4], T.pi[:, 1:2], 3, None, OP.bitwise_and, None, ["pi1"], ["pi3"])
     ts(T.pi[:, 4:5], T.pi[:, 0:1], 4, 1, OP.arith_shift_right, OP.bitwise_and, ["pi0"], ["pi4"])
     ts(T.pi[:, 5:6], T.pi[:, 0:1], 2, 1, OP.arith_shift_right, OP.bitwise_and, ["pi0"], ["pi5"])
-    ts(T.pf[:, 5:6], pm, 12.0, None, OP.mult, None, ["pm"], ["p12"])
-    cp(T.pf[:, 8:12], T.pi[:, 2:6], ["pi2", "pi3", "pi4", "pi5"], ["p8"])
-    ts(T.idxu[:], T.lf[:, 0:12], T.pf[:, 5:6], None, OP.add, None, ["lf0", "p12"], ["idxu"])
-    ms(T.S2[:], 0.0, ["S2"])
     ms(T.St[:], 0.0, ["vp", "M", "nfp"])
+    cp(T.pf[:, 8:12], T.pi[:, 2:6], ["pi2", "pi3", "pi4", "pi5"], ["p8"])
     ms(T.kcnf[:], 0.0, ["kcnf"])
     ms(T.cbuf[:, 0:16], 0.0, ["c0"])
     ms(T.cbuf[:, 208:224], 0.0, ["c1"])
@@ -263,12 +261,21 @@ def rank_program(g, core, T, topo):
     ts(pper, T.pf[:, 6:7], 208.0, T.pf[:, 12:13], OP.mult, OP.add, ["p6", "p12b"], ["pper"])
     ts(T.perm2[:], T.lf[:, 64:76], pm, None, OP.add, None, ["lf6", "pm"], ["perm2"])
     ts(T.perm1[:], T.lf[:, 12:24], pper, None, OP.add, None, ["lf1", "pper"], ["perm"])
-    act(T.idb[:], T.idf[:], AF.Copy, ["idf"], ["idb"])
-    act(T.n2k[:], T.idf[:], AF.Copy, ["idf"], ["n2k"], scale=-2048.0)
-    act(T.nid[:], T.idf[:], AF.Copy, ["idf"], ["nid"], scale=-1.0)
-    for c in range(1, 4):
-        od_spread(c)
-    act(T.kcon[:], T.ed[:], AF.Copy, ["ed"], ["kcon"], scale=8192.0)
+    od_spread(1)
+    od_spread(2)
+
+    def matrices():
+        act(T.offc[:], T.clamp[:], AF.Identity, ["clamp0"], ["offc"], bias=4095.0)
+        act(T.tri[:], T.blkf[:], AF.Copy, ["blkf"], ["tri"])
+        act(T.idb[:], T.idf[:], AF.Copy, ["idf"], ["idb"])
+        act(T.n2k[:], T.idf[:], AF.Copy, ["idf"], ["n2k"], scale=-2048.0)
+        act(T.nid[:], T.idf[:], AF.Copy, ["idf"], ["nid"], scale=-1.0)
+        act(T.kcon[:], T.ed[:], AF.Copy, ["ed"], ["kcon"], scale=8192.0)
+        pick(T.clamp[:], T.clamp[:], [[0, 12], [1, 16]], OP.is_equal, 0, 0, ["clamp0"], ["clamp0", "clamp"])
+        pick(T.tri[:], T.tri[:], [[1, 128]], OP.is_gt, 0, -1, ["tri"], ["tri"])
+        iota(T.negE[:], [[0, 1024]], -1, 0, ["negE"])
+        pick(T.negE[:], T.negE[:], [[1, 64], [0, 16]], OP.is_equal, 0, -1, ["negE"], ["negE"])
+        iota(T.snd[:], [[0, 1024]], 0, 0, ["snd0", "snd1", "snd2", "snd3"])
 
     def late_constants():
         ts(T.qc[:], T.lf[:, 24:36], pm, 65.0, OP.add, OP.add, ["lf2", "pm"], ["qc"])
@@ -279,10 +286,10 @@ def rank_program(g, core, T, topo):
     def input_constants():
         cp(T.thf[:, 0:1], T.thi[:, 0:1], ["thi"], ["thf"])
         ts(T.wtf[:, 0:1], T.wti[:, 0:1], -1.0, None, OP.mult, None, ["wti"], ["wtf"])
-        mm(PH[:, 8:9], T.blkf[:], T.thf[:, 0:1], True, True, ["blkf", "thf"], 7)
+        mm(PP[:, 20:21], T.blkf[:], T.thf[:, 0:1], True, True, ["blkf", "thf"], 3)
         ts(T.diag4[:], T.diag4[:], pm, None, OP.is_equal, None, ["diag4a", "pm"], ["diag4"])
         cp(T.odu[:], T.odi[:], ["odi"], ["odu"])
-        ts(T.limh[:, 0:3], T.lf[:, 0:3], 0.0, PH[:, 8:9], OP.mult, OP.add, ["lf0"], ["lim2"], [7])
+        ts(T.limh[:, 0:3], T.lf[:, 0:3], 0.0, PP[:, 20:21], OP.mult, OP.add, ["lf0"], ["lim2"], [3])
         ts(T.limoff[:], T.off12[:], T.limh[:, 2:3], None, OP.subtract, None, ["off12", "lim2"], ["limoff"])
 
     def guest_constants(t):
@@ -290,7 +297,8 @@ def rank_program(g, core, T, topo):
             act(T.nblkb[:], T.blkf[:], AF.Copy, ["blkf"], ["nblkb"], scale=-1.0)
             act(T.nblkf[:], T.blkf[:], AF.Copy, ["blkf"], ["nblkf"], scale=-1.0)
             act(T.diagS[:], T.diag[:], AF.Copy, ["diag"], ["diagS"], scale=1.0 / 8192)
-            limits(2)
+            if not THV[0]:
+                limits(2)
         lo, hi = (0, 384, 1152, 2048)[t:t + 2]
         act(T.selW[:, lo:hi], T.selA[:, lo:hi], AF.Copy, SELA + ["wtf"], ["selW"], scale=T.wtf[:, 0:1])
 
@@ -299,6 +307,7 @@ def rank_program(g, core, T, topo):
     Id, Ig = T.In[:, 0:12], T.In[:, 12:24]
     cnat = T.cbuf[:, 16:208]
     nsent = [0]
+    ODA = []
 
     def state():
         ts(T.nf3[:], T.free[:, 0:16].indirect(T.bcp[:, 0:3]), -1.0, 1.0, OP.mult, OP.add, ["free", "bcp"], ["nf3"])
@@ -311,14 +320,12 @@ def rank_program(g, core, T, topo):
 
     def leavers(t):
         i = t - 2
-        tt(T.u1[:], T.Cl[:], T.qc[:], OP.subtract, ["Cl", "qc"], ["u1"])
-        tt(T.mt[:, 0:12], T.off12[:], M, OP.subtract, ["off12", "M"], ["mt"])
-        tt(T.u2[:], T.u1[:], T.leave[:], OP.mult, ["u1", "leave"], ["u2"])
-        tt(T.mE[:], T.mt[:, 0:16].indirect(T.bc84[:, 0:12]), T.diagS[:], OP.mult, ["mt", "bc84", "diagS"], ["mE"])
         tt(T.u3[:], T.u2[:], T.qc[:], OP.add, ["u2", "qc"], ["u3"])
-        state()
+        if not OPT["nfs"]:
+            state()
         ts(T.slu[:], T.u3[:], -1.0, None, OP.add, None, ["u3"], ["slu"])
-        state2()
+        if not OPT["nfs"]:
+            state2()
         tt(T.snd[:, 256 * i:256 * i + 256].indirect(T.slu[:]), T.ownc[:], T.mE[:], OP.add, ["slu", "ownc", "mE"], ["snd%d" % i])
         dst = T.cores[(rank + 1 + t % (N - 1)) % N]
         rid, pid, _ = topo.addr(dst)
@@ -347,11 +354,17 @@ def rank_program(g, core, T, topo):
         act(T.gxT[0:64, :], PD[0:64, 256:384], AF.Copy, [], ["gxT"], b=[2])
         act(T.mR[:], PD[:, 384:448], AF.Copy, [], ["mR"], scale=8192.0, b=[2])
 
-    def hchain(t, best=False):
+    def hsum(t):
         ts(T.hi[:], PH[:, 0:4], 77.0 * t, None, OP.add, None, [], ["hi"], [7])
+
+    def hchain(t, best=False):
+        if t == NT - 1 or not OPT["hearly"]:
+            hsum(t)
         ts(T.hi2[:], T.hi[:], W - 1, None, OP.bitwise_and, None, ["hi"], ["hi2"])
+        if best and OPT["red"] == 0:
+            thresholds(t - 1)
         cp(T.hu[:], T.hi2[:], ["hi2"], ["hu"])
-        if best:
+        if best and OPT["red"] == 1:
             thresholds(t - 1)
         cp(T.gcu[:], colw.indirect(T.hu[:]), ["col", "hu"], ["gcu"])
 
@@ -374,8 +387,11 @@ def rank_program(g, core, T, topo):
         for a in range(16):
             mm(PQ[:, 0:64], T.selA[:, 128 * a:128 * a + 128], T.Ag[:, 64 * a:64 * a + 64], a == 0, a == 15, SELA + ["Ag%d" % (a // 8)], 6)
 
-    def judge_a():
-        scan(T.Rg[:], T.patg[:], PQ[:, 0:64], OP.add, OP.max, ["patg"], ["Rg"], [6])
+    def judge_a(part=None):
+        if part != 1:
+            scan(T.Rg[:], T.patg[:], PQ[:, 0:64], OP.add, OP.max, ["patg"], ["Rg"], [6])
+        if part == 0:
+            return
         tt(T.Eg[:], T.Rg[:, 0:64].indirect(T.bcg[:]), T.diag4[:], OP.mult, ["Rg", "bcg", "diag4"], ["Eg"])
         mm(PQ[:, 64:128], T.nblkf[:], T.Eg[:], True, True, ["nblkf", "Eg"], 6)
 
@@ -386,9 +402,12 @@ def rank_program(g, core, T, topo):
                 mask &= topo.mask(s, d)
         return mask
 
-    def judge_b(t):
+    def judge_b(t, part=None):
         i = t - 3
-        tt(T.jud[:], PQ[:, 64:128], T.mR[:], OP.min, ["mR"], ["jud"], [6])
+        if part != 1:
+            tt(T.jud[:], PQ[:, 64:128], T.mR[:], OP.min, ["mR"], ["jud"], [6])
+        if part == 0:
+            return
         red(T.bl[:, 8 * i + 4:8 * i + 5], T.jud[:], ["jud"], ["bl%d" % i])
         ids, dsts = [], []
         for d in range(1, N):
@@ -413,8 +432,17 @@ def rank_program(g, core, T, topo):
         act(T.limh[:, t:t + 1], z, AF.Identity, ["z", "limM"], ["lim%d" % t], bias=limM)
         if t < NT - 2:
             act(T.limoff[:], T.off12[:], AF.Identity, ["off12", "nlim"], ["limoff"], bias=nlim)
-        if t < NT - 1:
+        if t == NT - 2:
             limits(t)
+
+    def thresholds_v(t):
+        lim = T.limh[:, t - 1:t]
+        thresholds(t)
+        ts(T.tiny[:, 1:2], T.tiny[:, 0:1], lim, 0.0, OP.subtract, OP.max, ["bq", "lim%d" % (t - 1)], ["y"])
+        ts(T.tinyi[:, 0:1], T.tiny[:, 1:2], 0.25, -0.375, OP.mult, OP.add, ["y"], ["bi"])
+        tt(T.limh[:, t:t + 1], lim, T.tinyi[:, 0:1], OP.add, ["bi", "lim%d" % (t - 1)], ["lim%d" % t])
+        if t < NT - 2:
+            ts(T.limoff[:], T.off12[:], T.limh[:, t:t + 1], None, OP.subtract, None, ["off12", "lim%d" % t], ["limoff"])
 
     def limits(t):
         lim = T.limh[:, t:t + 1]
@@ -460,47 +488,66 @@ def rank_program(g, core, T, topo):
     for t in range(NT):
         last = t == NT - 1
         ns = 64 * SHARE[t]
-        pc = min(t, 3)
+        pc = (t + 1) // 2
+        if t >= 4 and OPT["ag"]:
+            gdist_s(0)
         act(T.GB[:], T.odB[:, 0:PIECES[pc][1] + 1].indirect(T.idxu[:]), AF.Copy, ODB[:pc + 2] + ["idxu"], ["GB"])
-        if t >= 4:
-            gdist_p()
+        if t >= 3 and OPT["nfs"]:
+            act(T.nf3[:], T.free[:, 0:16].indirect(T.bcp[:, 0:3]), AF.Identity, ["free", "bcp"], ["nf3"], bias=1.0, scale=-1.0)
         for a in range(16):
             mm(PH[:, 16:28], T.selA[:, 128 * a:128 * a + 128], T.GB[:, a:192:16], a == 0, a == 15, SELA + ["GB"], 7)
+        if t < 2:
+            ODA.append((1, 3)[t])
         if t >= 4:
-            gdist_s(0)
+            if not OPT["ag"]:
+                gdist_s(0)
             gdist_s(1)
             gdist_r()
         act(T.freeR[:], T.GB[:], AF.Sign, ["GB"], ["freeR"])
+        if t >= 5:
+            limits(t - 2)
+        if t in (1, 2):
+            od_c(t + 1)
         if t >= 3:
             leavers(t - 1)
+            if OPT["nfs"]:
+                state2()
             state3()
         elif t > 0:
-            state()
             if t - 1 in LATE:
                 cp(colw.indirect(T.vu[:]), cnat, ["vu", "c"], ["col"])
             state2()
-            state3()
         tt(vp, T.S2[:, 0:12], PH[:, 16:28], OP.subtract, ["S2"], ["vp"], [7])
         tt(T.oi[:], T.kcnf[:], PH[:, 16:28], OP.subtract, ["kcnf"], ["oi"], [7])
         ts(T.v4u[:], T.St[:, 0:16].indirect(T.bc4[:, 0:3]), -4095.0, None, OP.add, None, ["vp", "bc4"], ["v4u"])
         ts(T.oi2[:], T.oi[:], W - 1, None, OP.bitwise_and, None, ["oi"], ["oi2"])
-        ts(T.vu[:], vp, -4095.0, None, OP.add, None, ["vp"], ["vu"])
+        if t >= 4:
+            judge_a(0)
+        else:
+            ts(T.vu[:], vp, -4095.0, None, OP.add, None, ["vp"], ["vu"])
         cp(T.ou[:], T.oi2[:], ["oi2"], ["ou"])
+        if t >= 4:
+            judge_a(1)
         if t in NVB:
             act(T.nvb[:], T.St[:, 0:16].indirect(T.bc84[:, 0:12]), AF.Identity, ["vp", "bc84"], ["nvb"], bias=2047.0, scale=-1.0)
         if t > 0:
             act(T.own4[:], Xw.indirect(T.v4u[:]), AF.Copy, XK + ["v4u"], ["own4", "own4b"])
+        if ODA:
+            od_a(ODA.pop())
         if t == 0:
-            for c in range(4, 7):
-                od_spread(c)
+            matrices()
+            od_b(1)
+            od_c(1)
         tt(cnat, colw.indirect(T.ou[:]), T.freeR[:], OP.add, ["col", "ou", "freeR"], ["c"])
         if t >= 4:
-            judge_a()
-        op("V", lambda: V.transpose(T.trb[:, 0:192], T.cbuf[:, 16:208]), ["c"], ["tr1"])
-        op("V", lambda: V.transpose(T.trb[:, 192:416], T.cbuf[:, 0:224]), ["c", "c0", "c1"], ["tr2"])
+            ts(T.vu[:], vp, -4095.0, None, OP.add, None, ["vp"], ["vu"])
+        turn(T.trb[:, 0:192], T.cbuf[:, 16:208], ["c"], ["tr1"])
+        turn(T.trb[:, 192:416], T.cbuf[:, 0:224], ["c", "c0", "c1"], ["tr2"])
+        if t >= 4:
+            judge_b(t - 1, 0)
         cp(T.xo[:], T.trb[:, 0:416].indirect(T.perm1[:]), ["tr1", "tr2", "perm"], ["xo"])
         if t >= 4:
-            judge_b(t - 1)
+            judge_b(t - 1, 1)
         if t not in NVB:
             act(T.nvb[:], T.St[:, 0:16].indirect(T.bc84[:, 0:12]), AF.Identity, ["vp", "bc84"], ["nvb"], bias=2047.0, scale=-1.0)
         act(T.cO[:], T.trb[:, 0:416].indirect(T.perm2[:]), AF.Copy, ["tr1", "tr2", "perm2"], ["cO"])
@@ -511,8 +558,9 @@ def rank_program(g, core, T, topo):
         mm(PD[:, 0:192], T.n2k[:], T.sg[:], False, True, ["n2k", "sg"], 2)
         if t == 0:
             late_constants()
-            act(T.ed[:], PD[:, 0:192], AF.Abs, [], ["ed"], b=[2])
-            act(T.pen[:], T.ed[:], AF.Relu, ["ed"], ["pen"], bias=32.0, scale=-2.0)
+            for c in range(3, 7):
+                od_spread(c)
+            od_a(2)
             act(T.own4[:, 384:768], Xw.indirect(T.v4u[:, 24:48]), AF.Copy, XK + ["v4u"], ["own4b"])
             cp(T.own4[:, 0:384], Xw.indirect(T.v4u[:, 0:24]), XK + ["v4u"], ["own4"])
         gath(0)
@@ -520,18 +568,17 @@ def rank_program(g, core, T, topo):
             share_a(ns)
         if t == 0:
             input_constants()
-        if not last:
-            mm(PC[:, 0:192], T.idb[:], T.kcon[:], True, False, ["idb", "kcon"], 1)
-            mm(PC[:, 0:192], T.idf[:], T.cO[:], False, True, ["idf", "cO"], 1)
-        if t < 3:
-            od_a(t + 1)
-        if last:
+        early = last or OPT["pen"]
+        if early:
             act(T.ed[:], PD[:, 0:192], AF.Abs, [], ["ed"], b=[2])
             act(T.pen[:], T.ed[:], AF.Relu, ["ed"], ["pen"], bias=32.0, scale=-2.0)
+        if last:
             unpack(t)
             unpack_p(t)
+        if ns and not last and OPT["shb"]:
+            share_b(ns)
         absol(0)
-        if 0 < t < NT - 1:
+        if not early:
             act(T.ed[:], PD[:, 0:192], AF.Abs, [], ["ed"], b=[2])
             act(T.pen[:], T.ed[:], AF.Relu, ["ed"], ["pen"], bias=32.0, scale=-2.0)
         if last:
@@ -543,7 +590,7 @@ def rank_program(g, core, T, topo):
             hchain(t)
             gdist_a(True)
             gdist_p()
-        if ns and not last:
+        if ns and not last and not OPT["shb"]:
             share_b(ns)
         if 3 <= t < NT - 1:
             unpack(t)
@@ -554,6 +601,8 @@ def rank_program(g, core, T, topo):
             gdist_r()
         if not last:
             absol(1)
+            mm(PC[:, 0:192], T.idb[:], T.kcon[:], True, False, ["idb", "kcon"], 1)
+            mm(PC[:, 0:192], T.idf[:], T.cO[:], False, True, ["idf", "cO"], 1)
             ksum(1, False)
         if 3 <= t < NT - 1:
             unpack2()
@@ -572,6 +621,8 @@ def rank_program(g, core, T, topo):
             gath(2)
             absol(2)
             ksum(2, False)
+            if t >= 3 and OPT["hearly"]:
+                hsum(t)
             if ns == 0 and not last:
                 gath(3, 0, CUT)
                 absol(3, 0, CUT)
@@ -582,8 +633,8 @@ def rank_program(g, core, T, topo):
                 absol(3, 0, 768 - ns)
             ksum(3, True, ["As0", "As1"])
         if 3 <= t < NT - 1:
-            hchain(t, t >= 4)
-        if 4 <= t < NT - 1:
+            hchain(t, t >= 4 and not THV[0])
+        if 4 <= t < NT - 1 and not THV[0]:
             thresholds_s(t - 1)
         if 3 <= t < NT - 1:
             gdist_a()
@@ -591,14 +642,17 @@ def rank_program(g, core, T, topo):
             act(T.ownc[:], Xw.indirect(T.vu[:]), AF.Identity, XK + ["vu"], ["ownc"], bias=-128.0)
         if 1 <= t < NT - 2:
             act(T.St[:, 32:48], T.nf3[:, 0:16], AF.Copy, ["nf3"], ["nfp"])
-        if t < 3:
-            od_b(t + 1)
+        if t < 2:
+            od_b(t + 2)
         if t < 3:
             guest_constants(t)
         if t not in LATE:
             cp(colw.indirect(T.vu[:]), cnat, ["vu", "c"], ["col"])
+        if THV[0] and t >= 4:
+            thresholds_v(t - 1)
         if last:
-            thresholds(t - 1)
+            if not THV[0]:
+                thresholds(t - 1)
             ts(T.yvf[:], vp, -4095.0, None, OP.add, None, ["vp"], ["yvf"])
             dma("Y", T.yv[:], T.yvf[:], ["yvf"], ["outv"])
             ynpart(0, 0)
@@ -614,7 +668,8 @@ def rank_program(g, core, T, topo):
             if ns < 768:
                 absol(3, 0, 768 - ns)
             ksum(3, True, ["As0", "As1"])
-            thresholds_s(t - 1)
+            if not THV[0]:
+                thresholds_s(t - 1)
             ynpart(0, 1)
             judge_b(t)
             dma("Y", T.yg[:], T.jud[0:128:16, :], ["jud"], ["outg"])
@@ -626,17 +681,27 @@ def rank_program(g, core, T, topo):
         if last:
             tt(T.ymf[:], T.off12[:], M, OP.subtract, ["off12", "M"], ["ymf"])
             dma("Y", T.ym[:], T.ymf[:], ["ymf"], ["outm"])
-            thresholds(t)
-            thresholds_s(t)
+            if THV[0]:
+                thresholds_v(t)
+            else:
+                thresholds(t)
+                thresholds_s(t)
             dma("S", T.yt[:], T.limh[0:128:16, 0:NT], ["lim2", "lim3", "lim4", "lim5", "lim6"], ["outt"])
             break
-        tt(dead, M, T.limoff[:], OP.is_gt, ["M", "limoff"], ["dead"])
         tt(T.keep[:], PK[:, 0:192], T.Rb[:, 0:192], OP.is_le, ["Rb", "Rb0"], ["keep"], [0])
+        tt(dead, M, T.limoff[:], OP.is_gt, ["M", "limoff"], ["dead"])
         if t >= 2:
+            tt(T.mt[:, 0:12], T.off12[:], M, OP.subtract, ["off12", "M"], ["mt"])
             tt(go, T.S2[:, 32:44], dead, OP.is_gt, ["S2", "dead"], ["go"])
+            scan(T.Kb[:], T.keep[:], PC[:, 0:192], OP.mult, OP.max, ["keep"], ["Kb"], [1])
         scan(T.In[:], T.pat24[:], T.Fl[:], OP.mult, OP.add, ["pat24", "dead", "go"], ["In"])
         mm(PP[:, 0:2], T.tri[:], T.In[:, 11:24:12], True, True, ["tri", "In"], 3)
-        scan(T.Kb[:], T.keep[:], PC[:, 0:192], OP.mult, OP.max, ["keep"], ["Kb"], [1])
+        if t >= 3:
+            gdist_p()
+        if t >= 2:
+            tt(T.mE[:], T.mt[:, 0:16].indirect(T.bc84[:, 0:12]), T.diagS[:], OP.mult, ["mt", "bc84", "diagS"], ["mE"])
+        else:
+            scan(T.Kb[:], T.keep[:], PC[:, 0:192], OP.mult, OP.max, ["keep"], ["Kb"], [1])
         bd, bg = PP[:, 0:1], PP[:, 1:2]
         cur = T.cur0[:, 0:1] if t == 0 else PP[:, 8 + t:9 + t]
         if t >= 2:
@@ -646,16 +711,17 @@ def rank_program(g, core, T, topo):
             tt(T.leave[:], T.lv[:], go, OP.mult, ["lv", "go"], ["leave"])
             ts(T.t2[:], T.t1[:], bd, cur, OP.add, OP.add, ["t1", "cur0"], ["t2"], [3])
             tt(T.free[:, 0:12], T.leave[:], dead, OP.add, ["leave", "dead"], ["free"])
+            tt(T.u1[:], T.Cl[:], T.qc[:], OP.subtract, ["Cl", "qc"], ["u1"])
             tt(T.idxf[:], T.t2[:], T.free[:, 0:12], OP.mult, ["t2", "free"], ["idxf"])
+            tt(T.u2[:], T.u1[:], T.leave[:], OP.mult, ["u1", "leave"], ["u2"])
         else:
             ts(T.t2[:], Id, bd, cur, OP.add, OP.add, ["In", "cur0"], ["t2"], [3])
-            cp(T.free[:, 0:12], dead, ["dead"], ["free"])
+            ts(T.nf3[:], T.Fl[:, 0:16].indirect(T.bcp[:, 0:3]), -1.0, 1.0, OP.mult, OP.add, ["dead", "go", "bcp"], ["nf3"])
             tt(T.idxf[:], T.t2[:], dead, OP.mult, ["t2", "dead"], ["idxf"])
+            state3()
         cp(T.idxu[:], T.idxf[:], ["idxf"], ["idxu"])
         if t < NT - 2:
             mm(PP[:, 9 + t:10 + t], T.sel15[:], T.t2[:, 11:12], True, True, ["sel15", "t2"], 3)
-        if t < 3:
-            od_c(t + 1)
 
     op("G", None, ["out0", "out1", "out2", "outv", "outg", "outm", "outt"], wait=[(T.sem.sent, nsent[0])])
     _emit(g, T, ops)

@@ -6,12 +6,12 @@ F32, BF, I32, U16 = "float32", "bfloat16", "int32", "uint16"
 MAGIC = 12582912.0
 MAGIC64 = 64 * MAGIC
 CUT = 512
-OPT = {"hearly": 0, "red": 1, "pen": 1, "shb": 0, "ag": 1, "nfs": 0}
-LATE = []
+OPT = {"hearly": 2, "relu": [], "end": [128] * 3 + [0] * 4, "un": 1, "vr": [128] * 3 + [256] * 4, "xo": [1, 2, 3], "gv": 0, "yb": 0, "half": [0, 1, 2], "pen": 1, "shb": 0, "ag": 1, "nfs": 0}
+LATE = [0, 1]
 THV = [False]
 NVB = [0, 1, 2]
-YCUT = [0, 448, 1024, 1344]
-SHARE = [6, 6, 6, 4, 4, 4, 8]
+YCUT = [0, 512, 896, 1344]
+SHARE = [7, 7, 7, 7, 7, 7, 10]
 
 
 def _sb(n, dt):
@@ -283,14 +283,17 @@ def rank_program(g, core, T, topo):
         ts(T.pf[:, 13:14], T.pf[:, 9:10], 16.0, 15.0, OP.mult, OP.add, ["p8"], ["p13"])
         ts(T.bcg[:], T.lf[:, 0:4], 0.0, T.pf[:, 13:14], OP.mult, OP.add, ["lf0", "p13"], ["bcg"])
 
-    def input_constants():
-        cp(T.thf[:, 0:1], T.thi[:, 0:1], ["thi"], ["thf"])
+    def input_constants(part):
+        if part == 0:
+            cp(T.thf[:, 0:1], T.thi[:, 0:1], ["thi"], ["thf"])
+            mm(PP[:, 20:21], T.blkf[:], T.thf[:, 0:1], True, True, ["blkf", "thf"], 3)
+            return
         ts(T.wtf[:, 0:1], T.wti[:, 0:1], -1.0, None, OP.mult, None, ["wti"], ["wtf"])
-        mm(PP[:, 20:21], T.blkf[:], T.thf[:, 0:1], True, True, ["blkf", "thf"], 3)
         ts(T.diag4[:], T.diag4[:], pm, None, OP.is_equal, None, ["diag4a", "pm"], ["diag4"])
-        cp(T.odu[:], T.odi[:], ["odi"], ["odu"])
+        if 0 not in OPT["relu"]:
+            cp(T.odu[:], T.odi[:], ["odi"], ["odu"])
         ts(T.limh[:, 0:3], T.lf[:, 0:3], 0.0, PP[:, 20:21], OP.mult, OP.add, ["lf0"], ["lim2"], [3])
-        ts(T.limoff[:], T.off12[:], T.limh[:, 2:3], None, OP.subtract, None, ["off12", "lim2"], ["limoff"])
+        ts(T.limoff[:], T.off12[:], PP[:, 20:21], None, OP.subtract, None, ["off12"], ["limoff"], [3])
 
     def guest_constants(t):
         if t == 0:
@@ -299,7 +302,7 @@ def rank_program(g, core, T, topo):
             act(T.diagS[:], T.diag[:], AF.Copy, ["diag"], ["diagS"], scale=1.0 / 8192)
             if not THV[0]:
                 limits(2)
-        lo, hi = (0, 384, 1152, 2048)[t:t + 2]
+        lo, hi = (0, 1024, 1536, 2048)[t:t + 2]
         act(T.selW[:, lo:hi], T.selA[:, lo:hi], AF.Copy, SELA + ["wtf"], ["selW"], scale=T.wtf[:, 0:1])
 
     vp, M = T.St[:, 0:12], T.St[:, 16:28]
@@ -334,11 +337,13 @@ def rank_program(g, core, T, topo):
            ["snd%d" % i])
         nsent[0] += len(topo.engines(core, dst))
 
-    def unpack(t):
+    def unpack(t, part):
         i = t - 3
         src = T.cores[(rank - 1 - (t - 1) % (N - 1)) % N]
         p = T.lnd[:, 64 * i:64 * i + 64]
-        act(T.gy[:], p, AF.Identity, [], ["gy"], bias=MAGIC, wait=[(T.sem["ga%d" % i], len(topo.engines(src, core)))])
+        if part == 0:
+            act(T.gy[:], p, AF.Identity, [], ["gy"], bias=MAGIC, wait=[(T.sem["ga%d" % i], len(topo.engines(src, core)))])
+            return
         act(T.gx[:], T.gy[:], AF.Identity, ["gy"], ["gx"], bias=128.0 - MAGIC)
         act(T.gxc[:], T.gy[:], AF.Identity, ["gy"], ["gxc"], bias=-MAGIC)
 
@@ -357,21 +362,28 @@ def rank_program(g, core, T, topo):
     def hsum(t):
         ts(T.hi[:], PH[:, 0:4], 77.0 * t, None, OP.add, None, [], ["hi"], [7])
 
-    def hchain(t, best=False):
-        if t == NT - 1 or not OPT["hearly"]:
+    def hchain(t, best=False, part=None):
+        early = OPT["hearly"] and t < NT - 1
+        if part != 1 and not early:
             hsum(t)
-        ts(T.hi2[:], T.hi[:], W - 1, None, OP.bitwise_and, None, ["hi"], ["hi2"])
-        if best and OPT["red"] == 0:
+        if (part != 1) if early else (part != 0):
+            ts(T.hi2[:], T.hi[:], W - 1, None, OP.bitwise_and, None, ["hi"], ["hi2"])
+        if part == 0:
+            return
+        if best and not early:
             thresholds(t - 1)
         cp(T.hu[:], T.hi2[:], ["hi2"], ["hu"])
-        if best and OPT["red"] == 1:
+        if best and early:
             thresholds(t - 1)
         cp(T.gcu[:], colw.indirect(T.hu[:]), ["col", "hu"], ["gcu"])
 
     def gdist_a(halves=False):
         if halves:
-            for h in range(2):
-                act(T.G[:, 512 * h:512 * h + 512], Xw.indirect(T.gcu[:, 32 * h:32 * h + 32]), AF.Copy, XK + ["gcu"], ["G%d" % h])
+            act(T.G[:, 0:512], Xw.indirect(T.gcu[:, 0:32]), AF.Copy, XK + ["gcu"], ["G0"])
+            if OPT["gv"]:
+                cp(T.G[:, 512:1024], Xw.indirect(T.gcu[:, 32:64]), XK + ["gcu"], ["G1"])
+            else:
+                act(T.G[:, 512:1024], Xw.indirect(T.gcu[:, 32:64]), AF.Copy, XK + ["gcu"], ["G1"])
         else:
             act(T.G[:], Xw.indirect(T.gcu[:]), AF.Copy, XK + ["gcu"], ["G0", "G1"])
 
@@ -423,9 +435,11 @@ def rank_program(g, core, T, topo):
         n = sum(bin(to_all(s)).count("1") for s in T.cores if s != core)
         red(T.tiny[:, 0:1], T.bl[:, 8 * i + 1:8 * i + 5], ["bl%d" % i], ["bq"], wait=[(T.sem["gb%d" % i], n)])
 
-    def thresholds_s(t):
+    def thresholds_s(t, between=None):
         bq, y, z, nlim, nl4, limM, nlimM = (T.tiny[:, j:j + 1] for j in range(7))
         act(y, bq, AF.Relu, ["bq", "nl4"], ["y"], bias=nl4, scale=0.25)
+        if between:
+            between()
         act(z, y, AF.Identity, ["y"], ["z"], bias=MAGIC)
         if t < NT - 2:
             act(nlim, z, AF.Identity, ["z", "nlimM"], ["nlim"], bias=nlimM, scale=-1.0)
@@ -453,18 +467,26 @@ def rank_program(g, core, T, topo):
 
     def gath(c, lo=0, hi=768):
         tt(T.dif[:, 768 * c + lo:768 * c + hi], Xw.indirect(T.xo[:, 48 * c + lo // 16:48 * c + hi // 16]), T.own4[:, lo:hi], OP.subtract,
-           XK + ["xo", "own4", "own4b"], ["dif%d_%d" % (c, lo > 0)])
+           XK + (["xo0"], ["xo0", "xo"], ["xo"], ["xo"])[c] + ["own4", "own4b"], ["dif%d_%d" % (c, lo > 0)])
+
+    def record(t):
+        if 2 <= t:
+            act(T.ownc[:], Xw.indirect(T.vu[:]), AF.Identity, XK + ["vu"], ["ownc"], bias=-128.0)
+        if 1 <= t < NT - 2:
+            act(T.St[:, 32:48], T.nf3[:, 0:16], AF.Copy, ["nf3"], ["nfp"])
 
     def absol(c, lo=0, hi=768):
-        act(T.A[:, 768 * c + lo:768 * c + hi], T.dif[:, 768 * c + lo:768 * c + hi], AF.Abs, ["dif%d_%d" % (c, lo > 0)], ["A%d_%d" % (c, lo > 0)])
+        act(T.A[:, 768 * c + lo:768 * c + hi], T.dif[:, 768 * c + lo:768 * c + hi], AF.Abs, ["dif%d_0" % c], ["A%d_%d" % (c, lo > 0)])
 
     def ksum(c, stop, more=()):
         for a in range(16):
             mm(PK[:, c:192:4], T.selA[:, 128 * a:128 * a + 128], T.A[:, 768 * c + a:768 * c + 768:16], False, stop and a == 15,
                SELA + ["A%d_0" % c, "A%d_1" % c] + list(more), 0)
 
-    def share_a(n):
+    def share_g(n):
         act(T.Gs[:, 0:n], Xw.indirect(T.xo[:, 192 - n // 16:192]), AF.Copy, XK + ["xo"], ["Gs"])
+
+    def share_a(n):
         for h, (bank, nm) in enumerate(PG):
             lo, hi = 512 * h, min(n, 512 * h + 512)
             if lo < hi:
@@ -496,8 +518,8 @@ def rank_program(g, core, T, topo):
             act(T.nf3[:], T.free[:, 0:16].indirect(T.bcp[:, 0:3]), AF.Identity, ["free", "bcp"], ["nf3"], bias=1.0, scale=-1.0)
         for a in range(16):
             mm(PH[:, 16:28], T.selA[:, 128 * a:128 * a + 128], T.GB[:, a:192:16], a == 0, a == 15, SELA + ["GB"], 7)
-        if t < 2:
-            ODA.append((1, 3)[t])
+        if t < 3:
+            ODA.append(t + 1)
         if t >= 4:
             if not OPT["ag"]:
                 gdist_s(0)
@@ -506,8 +528,8 @@ def rank_program(g, core, T, topo):
         act(T.freeR[:], T.GB[:], AF.Sign, ["GB"], ["freeR"])
         if t >= 5:
             limits(t - 2)
-        if t in (1, 2):
-            od_c(t + 1)
+        if t in (2, 3):
+            od_c(t)
         if t >= 3:
             leavers(t - 1)
             if OPT["nfs"]:
@@ -537,7 +559,6 @@ def rank_program(g, core, T, topo):
         if t == 0:
             matrices()
             od_b(1)
-            od_c(1)
         tt(cnat, colw.indirect(T.ou[:]), T.freeR[:], OP.add, ["col", "ou", "freeR"], ["c"])
         if t >= 4:
             ts(T.vu[:], vp, -4095.0, None, OP.add, None, ["vp"], ["vu"])
@@ -545,105 +566,131 @@ def rank_program(g, core, T, topo):
         turn(T.trb[:, 192:416], T.cbuf[:, 0:224], ["c", "c0", "c1"], ["tr2"])
         if t >= 4:
             judge_b(t - 1, 0)
-        cp(T.xo[:], T.trb[:, 0:416].indirect(T.perm1[:]), ["tr1", "tr2", "perm"], ["xo"])
+        if t in OPT["xo"]:
+            cp(T.xo[:, 0:64], T.trb[:, 0:416].indirect(T.perm1[:, 0:4]), ["tr1", "tr2", "perm"], ["xo0"])
+            cp(T.xo[:, 64:192], T.trb[:, 0:416].indirect(T.perm1[:, 4:12]), ["tr1", "tr2", "perm"], ["xo"])
+        else:
+            cp(T.xo[:], T.trb[:, 0:416].indirect(T.perm1[:]), ["tr1", "tr2", "perm"], ["xo", "xo0"])
         if t >= 4:
             judge_b(t - 1, 1)
         if t not in NVB:
             act(T.nvb[:], T.St[:, 0:16].indirect(T.bc84[:, 0:12]), AF.Identity, ["vp", "bc84"], ["nvb"], bias=2047.0, scale=-1.0)
         act(T.cO[:], T.trb[:, 0:416].indirect(T.perm2[:]), AF.Copy, ["tr1", "tr2", "perm2"], ["cO"])
         act(T.sg[:], T.cO[:], AF.Sign, ["cO"], ["sg"], bias=-4095.5)
+        if 0 < t < NT - 1:
+            share_g(ns)
         mm(PK[:, 0:192], T.idb[:], T.offc[:], True, False, ["idb", "offc"], 0)
         mm(PD[:, 0:192], T.idf[:], T.nvb[:], True, False, ["idf", "nvb"], 2)
         mm(PD[:, 0:192], T.idf[:], T.cO[:], False, False, ["idf", "cO"], 2)
         mm(PD[:, 0:192], T.n2k[:], T.sg[:], False, True, ["n2k", "sg"], 2)
+        if 0 < t < NT - 1:
+            share_a(ns)
         if t == 0:
             late_constants()
-            for c in range(3, 7):
-                od_spread(c)
-            od_a(2)
             act(T.own4[:, 384:768], Xw.indirect(T.v4u[:, 24:48]), AF.Copy, XK + ["v4u"], ["own4b"])
             cp(T.own4[:, 0:384], Xw.indirect(T.v4u[:, 0:24]), XK + ["v4u"], ["own4"])
         gath(0)
-        if ns and not last:
-            share_a(ns)
-        if t == 0:
-            input_constants()
-        early = last or OPT["pen"]
-        if early:
+        if last:
             act(T.ed[:], PD[:, 0:192], AF.Abs, [], ["ed"], b=[2])
             act(T.pen[:], T.ed[:], AF.Relu, ["ed"], ["pen"], bias=32.0, scale=-2.0)
-        if last:
-            unpack(t)
+            unpack(t, 0)
+            unpack(t, 1)
             unpack_p(t)
-        if ns and not last and OPT["shb"]:
-            share_b(ns)
-        absol(0)
-        if not early:
-            act(T.ed[:], PD[:, 0:192], AF.Abs, [], ["ed"], b=[2])
-            act(T.pen[:], T.ed[:], AF.Relu, ["ed"], ["pen"], bias=32.0, scale=-2.0)
-        if last:
+            absol(0)
             unpack2()
-        ksum(0, False)
-        mm(PK[:, 0:192], T.n2k[:], T.pen[:], False, False, ["n2k", "pen"], 0)
-        gath(1)
-        if last:
+            ksum(0, False)
+            mm(PK[:, 0:192], T.n2k[:], T.pen[:], False, False, ["n2k", "pen"], 0)
+            gath(1)
+            gath(2, 0, 384)
+            absol(1)
+            ksum(1, False)
             hchain(t)
             gdist_a(True)
             gdist_p()
-        if ns and not last and not OPT["shb"]:
-            share_b(ns)
-        if 3 <= t < NT - 1:
-            unpack(t)
-            unpack_p(t)
-        if last:
             gdist_s(0)
             gdist_s(1)
             gdist_r()
-        if not last:
-            absol(1)
+            gath(2, 384, 768)
+            gath(3, 0, 768 - ns)
+        else:
+            if t == 0:
+                share_g(ns)
+                share_a(ns)
+            act(T.ed[:], PD[:, 0:192], AF.Abs, [], ["ed"], b=[2])
+            absol(0)
             mm(PC[:, 0:192], T.idb[:], T.kcon[:], True, False, ["idb", "kcon"], 1)
             mm(PC[:, 0:192], T.idf[:], T.cO[:], False, True, ["idf", "cO"], 1)
-            ksum(1, False)
-        if 3 <= t < NT - 1:
-            unpack2()
-        if last:
-            gath(2)
-            if ns < 768:
-                gath(3, 0, 768 - ns)
-        elif ns == 768:
-            ksum(3, False, ["As0", "As1"])
-            gath(2, 0, CUT)
-            absol(2, 0, CUT)
-            gath(2, CUT, 768)
-            absol(2, CUT, 768)
-            ksum(2, True)
-        else:
-            gath(2)
-            absol(2)
-            ksum(2, False)
-            if t >= 3 and OPT["hearly"]:
-                hsum(t)
-            if ns == 0 and not last:
-                gath(3, 0, CUT)
-                absol(3, 0, CUT)
-                gath(3, CUT, 768)
-                absol(3, CUT, 768)
+            ksum(0, False)
+            gath(1)
+            if t >= 3:
+                unpack(t, 0)
+            act(T.pen[:], T.ed[:], AF.Relu, ["ed"], ["pen"], bias=32.0, scale=-2.0)
+            if t < 3 or not OPT["un"]:
+                share_b(ns)
+            n = OPT["vr"][t]
+            if t >= 3 and OPT["un"]:
+                unpack(t, 1)
+                unpack_p(t)
+                share_b(ns)
+            if n < 768:
+                absol(1, n, 768)
+            if t >= 3 and not OPT["un"]:
+                unpack(t, 1)
+                unpack_p(t)
+            mm(PK[:, 0:192], T.n2k[:], T.pen[:], False, False, ["n2k", "pen"], 0)
+            if n:
+                for a in range(16):
+                    mm(PK[:, 1:1 + n // 4:4], T.selA[:, 128 * a:128 * a + 128], T.dif[:, 768 + a:768 + n:16], False, False, SELA + ["dif1_0"], 0)
             else:
-                gath(3, 0, 768 - ns)
-                absol(3, 0, 768 - ns)
-            ksum(3, True, ["As0", "As1"])
+                ksum(1, False)
+            if t == 0:
+                input_constants(0)
+            half = t in OPT["half"]
+            gath(2, 0, 384 if half else 768)
+            if t >= 3 and OPT["hearly"] == 2:
+                hsum(t)
+            if n:
+                ts(T.A[:, 768:768 + n], T.dif[:, 768:768 + n], -2.0, 0.0, OP.mult, OP.max, ["dif1_0"], ["A1_0"])
+                ksum(1, False)
+            absol(2, 0, 384 if half else 768)
+            if half:
+                gath(2, 384, 768)
+                act(T.A[:, 1920:2304], T.dif[:, 1920:2304], AF.Abs, ["dif2_1"], ["A2_1"])
+            if t >= 3:
+                unpack2()
+            ksum(2, False)
+            if t >= 3 and OPT["hearly"] == 1:
+                hsum(t)
+            if t >= 3 and OPT["hearly"] == 2:
+                hchain(t, t >= 4, 0)
+            m = 768 - ns - OPT["end"][t]
+            if OPT["end"][t]:
+                gath(3, 0, m)
+                absol(3, 0, m)
+                gath(3, m, 768 - ns)
+                act(T.A[:, 2304 + m:3072 - ns], T.dif[:, 2304 + m:3072 - ns], AF.Abs, ["dif3_1"], ["A3_2"])
+            else:
+                gath(3, 0, m)
+                absol(3, 0, m)
+            if t >= 3 and OPT["hearly"] != 2:
+                hchain(t, t >= 4, 0)
+            ksum(3, True, ["As0", "As1", "A3_2"])
+        if t == 0:
+            input_constants(1)
+            od_c(1)
+        if t < 2:
+            od_spread(3 + 2 * t)
+            od_spread(4 + 2 * t)
         if 3 <= t < NT - 1:
-            hchain(t, t >= 4 and not THV[0])
-        if 4 <= t < NT - 1 and not THV[0]:
-            thresholds_s(t - 1)
+            hchain(t, t >= 4, 1)
+        if 4 <= t < NT - 1:
+            thresholds_s(t - 1, lambda: record(t))
         if 3 <= t < NT - 1:
             gdist_a()
-        if 2 <= t < NT - 1:
-            act(T.ownc[:], Xw.indirect(T.vu[:]), AF.Identity, XK + ["vu"], ["ownc"], bias=-128.0)
-        if 1 <= t < NT - 2:
-            act(T.St[:, 32:48], T.nf3[:, 0:16], AF.Copy, ["nf3"], ["nfp"])
-        if t < 2:
-            od_b(t + 2)
+        if t < 4:
+            record(t)
+        if t in (1, 2):
+            od_b(t + 1)
         if t < 3:
             guest_constants(t)
         if t not in LATE:
@@ -653,15 +700,14 @@ def rank_program(g, core, T, topo):
         if last:
             if not THV[0]:
                 thresholds(t - 1)
+            ynpart(0, 0)
             ts(T.yvf[:], vp, -4095.0, None, OP.add, None, ["vp"], ["yvf"])
             dma("Y", T.yv[:], T.yvf[:], ["yvf"], ["outv"])
-            ynpart(0, 0)
+            ynpart(0, 1)
             judge_a()
-            if ns:
-                share_a(ns)
-            absol(1)
-            ksum(1, False)
-            absol(2)
+            share_g(ns)
+            share_a(ns)
+            act(T.A[:, 1536:2304], T.dif[:, 1536:2304], AF.Abs, ["dif2_0", "dif2_1"], ["A2_0", "A2_1"])
             ksum(2, False)
             if ns:
                 share_b(ns)
@@ -670,23 +716,27 @@ def rank_program(g, core, T, topo):
             ksum(3, True, ["As0", "As1"])
             if not THV[0]:
                 thresholds_s(t - 1)
-            ynpart(0, 1)
-            judge_b(t)
+            ynpart(1, 0)
+            judge_b(t, 0)
             dma("Y", T.yg[:], T.jud[0:128:16, :], ["jud"], ["outg"])
-            for c in (1, 2):
-                ynpart(c, 0)
-                ynpart(c, 1)
+            if OPT["yb"]:
+                ynpart(1, 1)
+            judge_b(t, 1)
+            if not OPT["yb"]:
+                ynpart(1, 1)
+            ynpart(2, 0)
         scan(T.Rb[:, 1:193], T.clamp[:], PK[:, 0:192], OP.max, OP.max, ["clamp"], ["Rb"], [0])
+        if last:
+            ynpart(2, 1)
         tt(M, T.S2[:, 16:28], T.Rb[:, 16:193:16], OP.max, ["S2", "Rb"], ["M"])
         if last:
             tt(T.ymf[:], T.off12[:], M, OP.subtract, ["off12", "M"], ["ymf"])
             dma("Y", T.ym[:], T.ymf[:], ["ymf"], ["outm"])
-            if THV[0]:
-                thresholds_v(t)
-            else:
-                thresholds(t)
-                thresholds_s(t)
-            dma("S", T.yt[:], T.limh[0:128:16, 0:NT], ["lim2", "lim3", "lim4", "lim5", "lim6"], ["outt"])
+            thresholds(t)
+            lim = T.limh[:, t - 1:t]
+            ts(T.tinyi[:, 0:1], T.tiny[:, 0:1], 0.25, T.tiny[:, 4:5], OP.mult, OP.add, ["bq", "nl4"], ["bi"])
+            ts(T.limh[:, t:t + 1], T.tinyi[:, 0:1], lim, lim, OP.add, OP.max, ["bi", "lim%d" % (t - 1)], ["lim%d" % t])
+            dma("Y", T.yt[:], T.limh[0:128:16, 0:NT], ["lim2", "lim3", "lim4", "lim5", "lim6"], ["outt"])
             break
         tt(T.keep[:], PK[:, 0:192], T.Rb[:, 0:192], OP.is_le, ["Rb", "Rb0"], ["keep"], [0])
         tt(dead, M, T.limoff[:], OP.is_gt, ["M", "limoff"], ["dead"])

@@ -4,14 +4,25 @@ from concourse.mybir import AluOpType as OP, AxisListType, ActivationFunctionTyp
 W, L, U, NT, Q = 4096, 192, 64, 7, 1344
 F32, BF, I32, U16 = "float32", "bfloat16", "int32", "uint16"
 MAGIC = 12582912.0
-MAGIC64 = 64 * MAGIC
-CUT = 512
-OPT = {"hearly": 2, "relu": [], "end": [128] * 3 + [0] * 4, "un": 1, "vr": [128] * 3 + [256] * 4, "xo": [1, 2, 3], "gv": 0, "yb": 0, "half": [0, 1, 2], "pen": 1, "shb": 0, "ag": 1, "nfs": 0}
-LATE = [0, 1]
-THV = [False]
-NVB = [0, 1, 2]
-YCUT = [0, 512, 896, 1344]
-SHARE = [7, 7, 7, 7, 7, 7, 10]
+SHARE = [7, 7, 7, 4, 4, 4, 8]
+RELU = [256, 256, 256, 256, 256, 256, 0]
+CUT = [(384, 640)] * 6 + [(768, 768)]
+YCUT = [0, 512, 960, 1344]
+
+R0 = '+odB2 +qc +odu GB V oi vp and ou c tr1 tr2 nvb vu Dv +wtf xo1 own0 own1 zero own2 cO sg +thf +th_ xo0 Dc Gown Gs ed +p3 tag +bcg pen g0 Gsub g1 Kp a0 r1 g2 relu a1 k0 As a2 g3 g4 k1 g5 a3 +lim0 a4 col k3 a5 +p8k k2'
+R1 = '+nhi -Rb -M +selW1 -dead -go -In -X -vm -B +nlo -idxu +nblkf -keep GB -I -Kb Vm V -kcnf +selW0 +diagS oi vu and own0 ou own1 c vp +diag4 tr2 own2 nvb tr1 -PM xo0 Gown Dv xo1 g0 cO -PA g1 sg g2 relu Gs Dc ed pen -cur zero a0 Gsub Kp a1 g3 r1 a2 As k0 g4 k1 g5 a3 k3 a4 a5 k2 col tag'
+R3 = '-Rb -M -sub1 -lim15 -dead -go -Ag0 -Xg -keep -In -mE -Xd -X -B -nf -q -Ag1 -T -vm -Kb -S -idxu -slf GB -kcnf -slu -gsum Vm V -snd -Rg -I oi vu and -Eg ou own0 -gspread -PM c -jud vp own1 tr1 tr2 -best -send xo0 -PA nvb Dv xo1 own2 cO sg g0 Gs Dc Gsub a0 zero -tell gy gx g2 Gown k0 hash -bq g1 gxT_ g3 ed hi r1 g4 hi2 As g5 a2 a1 pen -cur relu m_ hu a3 gcu a4 -bi k3 a5 k1 col Kp gxT G0 G1 k2 sub0 mR -lim tag'
+R6 = '-sub1 -Rb -M -dead -go -Xd -keep -In -mE -cur -Xg -X -B -q -nf -PA -T -Ag0 -Kb -vm -idxu -S -Ag1 -slf -slu -kcnf GB -gsum -snd Vm V -I -Rg -send oi vu own0 and -Eg ou zero -gspread c -jud vp own1 nvb tr1 tr2 -PM own2 xo0 yvf Dv gy gx cO g0 hash -lim15 hi xo1 sg a0 hi2 -best gxT_ Dc hu m_ gcu ed g1 G0 gxT col k0 sub0 G1 g2 sub1 mR yn0 g3 Ag0 outv pen Ag1 gsum Rg a1 Gs -tell a3 k1 -bq yf0 Eg gspread -bi jud best outg tell yn1 Gsub out0 a2 As -lim Kp yn2 k2 bq yf1 k3 out1 lim15 Rb bi M yf2 ymf out2 lim outt outm'
+SHARE, RELU = [8, 8, 8, 6, 6, 6, 8], [512] * 6 + [0]
+R0 = 'zero +odB2 ownc GB +qc V oi vu and ou vp c tr2 v4u +odu nvb tr1 +wtf Dv +p3 own cO Gown sg xo1 Dc xo0 Gs +thf ed pen Gsub g0 a0 tag g1 g2 a1 Kp As relu g3 a2 +th_ a3 r1 g4 a4 g5 +lim0 a5 k0 k1 k3 +bcg col +p8k k2'
+R1 = '-Rb +nblkf -M +nlo -dead -go -In -X -B -idxu -vm -keep +selW1 +nhi -Kb +diag4 -I Vm +diagS -kcnf GB +selW0 V oi vp -PM and -PA v4u nvb ou c own tr1 tr2 Dv Gown vu cO xo0 sg xo1 Gs Dc -cur ed pen g0 g1 zero g2 a0 relu g3 a1 Gsub tag a2 Kp r1 g4 k0 k1 As a3 g5 a4 k3 a5 col ownc k2'
+R3 = '-Rb -sub1 -M -dead -go -keep -Xd -In -mE -Ag0 -Xg -lim15 -Ag1 -X -B -nf -q -T -S -vm -Kb -idxu -slf -slu Vm GB -kcnf -gsum V -snd -Rg vp oi -I v4u and -Eg own -PM ou vu c -PA -gspread -jud tr2 Gown nvb tr1 -best cO Dv xo0 xo1 g0 -cur zero g2 Gs -send Gsub sg Dc a0 ed g1 gy gx -tell g3 k0 pen As gxT_ hash a2 hi m_ Kp r1 g5 g4 a1 hi2 relu hu a5 -bq k3 a3 gcu gxT k1 mR -bi a4 k2 tag -lim G0 col G1 ownc sub0'
+R6 = '-PA -Rb -Ag0 -M -sub1 -dead -Ag1 -go -Xg -keep -In -Xd -mE -X -B -cur -q -nf -Kb -T -S -vm -gsum -idxu -slf -slu GB -kcnf Vm -snd -Rg V vp oi v4u -send and zero yvf -Eg nvb ou c -gspread -PM -jud Dv tr2 tr1 own vu gy xo0 g0 gx hash cO hi xo1 sg gxT_ Dc hi2 -lim15 a0 m_ hu gcu ed G0 gxT k0 -best g1 sub0 G1 sub1 mR col pen g3 -tell outv -bq Ag0 Ag1 g2 a1 a2 gsum yn0 k1 Rg Gs Eg gspread Kp jud best yn1 a3 -I yf0 -bi out0 yn2 tell Gsub As yf1 outg -lim bq out1 k2 lim15 k3 Rb yf2 bi M ymf out2 lim outt ownc outm'
+R0 = 'GB zero V +odu vp oi +odB2 nvb v4u Cv and +qc ou Dv c tr2 tr1 +thf own Gown +th_ cO +wtf xo0 vu +p3 xo1 sg Gs g0 Dc g1 g2 Cc ed pen Gsub a0 a1 Kp relu g3 As a2 a3 r1 g4 g5 a4 +bcg k0 k1 k3 a5 +p8k col k2 +lim0'
+R1 = '-Rb -M -dead +selW1 -go -In +nblkf -X +nhi -B -vm -idxu GB -keep Vm V +diag4 -Kb -kcnf zero +diagS oi -I vp and +selW0 v4u ou +nlo c nvb Dv own -PM -PA tr2 tr1 Gown cO -cur Cc sg vu xo0 xo1 Dc Gs g0 Cv ed pen g1 g2 a0 a1 Gsub relu g3 a2 g4 As g5 Kp r1 a3 a4 a5 k0 k1 k3 k2 col ownc'
+R3 = '-sub1 -Rb -M -dead -go -In -Xg -Ag0 -Ag1 -Xd -X -B -mE -nf -q -vm -T -S -gsum -keep Vm -idxu -Kb GB V -slf -lim15 -kcnf -slu -I -Rg -snd vp oi v4u own and -Eg -gspread ou -PM nvb c -PA zero -jud tr1 -send -cur tr2 -best cO Gown Dv xo0 xo1 g0 vu Cc Cv g5 Gs sg a0 a5 Gsub g3 g2 gy g1 Dc -tell gx k0 ed hash gxT_ As hi m_ a2 g4 hi2 relu a3 k3 pen hu a1 a4 -bq gxT mR gcu r1 k1 col Kp -bi G0 -lim k2 G1 ownc sub0'
+R6 = '-sub1 -Ag0 -Rb -M -Ag1 -dead -Xd -go -In -X -keep -Xg -B -Kb -nf -q -vm -T -mE -S -idxu -gsum -slf -kcnf -slu Vm GB V -snd -Rg oi vp -send and v4u ou -Eg c nvb -gspread tr1 zero own tr2 -PM xo0 -jud gy vu Dv g0 -lim15 gx cO hash sg hi yvf Dc -best gxT_ a0 hi2 hu xo1 m_ ed gcu G0 g3 gxT outv G1 k0 pen mR col sub0 Ag0 sub1 g1 Ag1 gsum a1 g2 -tell k1 yn0 Rg Eg gspread Kp jud Gs a3 -bq best a2 -bi yn1 yf0 -lim out0 yn2 Gsub k2 As outg yf1 yf2 k3 lim15 out1 out2 tell bq Rb bi M lim outt ymf outm'
+ROUNDS = [R0, R1, R1, R3, R3, R3, R6]
 
 
 def _sb(n, dt):
@@ -19,26 +30,25 @@ def _sb(n, dt):
 
 
 SCRATCH = {
-    "X": _sb(4112, BF), "col": _sb(W, I32), "odi": _sb(84, I32), "odf": _sb(88, F32), "odu": _sb(84, U16),
-    "odE": _sb(Q, F32), "odM": _sb(Q, F32), "odH": _sb(Q, BF), "odB": _sb(Q + 16, BF),
-    "wti": _sb(4, I32), "wtf": _sb(4, F32), "thi": _sb(4, I32), "thf": _sb(4, F32),
-    "pi": _sb(8, I32), "pf": _sb(24, F32), "j16": _sb(192, F32), "ia": _sb(128, F32), "ib": _sb(128, F32), "ic": _sb(128, F32),
-    "li": _sb(96, I32), "lf": _sb(96, F32),
-    "diag": _sb(192, F32), "diagS": _sb(192, F32), "diag4": _sb(64, F32), "clamp": _sb(192, F32),
-    "patg": _sb(64, F32), "pat24": _sb(24, F32), "offc": _sb(192, BF), "kcon": _sb(192, BF), "off12": _sb(12, F32), "qc": _sb(12, F32),
-    "blkf": _sb(128, F32), "blk1": _sb(128, F32), "nblkf": _sb(128, F32), "nblkb": _sb(128, BF), "tri": _sb(128, BF), "sel15": _sb(128, F32),
-    "idf": _sb(128, F32), "idb": _sb(128, BF), "nid": _sb(128, BF), "n2k": _sb(128, BF), "dbeta": _sb(128, BF),
-    "selA": _sb(2048, BF), "selW": _sb(2048, BF), "negE": _sb(1024, BF),
-    "bc84": _sb(84, U16), "bc4": _sb(4, U16), "bcp": _sb(4, U16), "bcg": _sb(4, U16), "perm1": _sb(12, U16), "perm2": _sb(12, U16),
-    "St": _sb(48, F32), "S2": _sb(48, F32), "nf3": _sb(48, F32), "free": _sb(16, F32), "kcnf": _sb(12, F32), "cur0": _sb(4, F32),
-    "idxu": _sb(12, U16), "GB": _sb(192, BF), "oi": _sb(12, I32), "oi2": _sb(12, I32), "ou": _sb(12, U16),
-    "v4u": _sb(48, U16), "vu": _sb(12, U16), "freeR": _sb(192, F32), "cbuf": _sb(224, F32), "trb": _sb(416, F32), "xo": _sb(192, U16),
-    "own4": _sb(768, BF), "dif": _sb(3072, BF), "A": _sb(3072, BF), "Gs": _sb(768, BF), "nvb": _sb(192, F32), "cO": _sb(192, F32), "sg": _sb(192, BF),
-    "ed": _sb(192, F32), "pen": _sb(192, BF), "Rb": _sb(200, F32), "keep": _sb(192, F32), "Kb": _sb(192, F32),
-    "Fl": _sb(24, F32), "In": _sb(24, BF), "Cl": _sb(12, F32), "lv": _sb(12, F32), "t1": _sb(12, F32), "t2": _sb(12, F32),
-    "leave": _sb(12, F32), "idxf": _sb(12, F32), "limoff": _sb(12, F32), "limh": _sb(8, F32), "tiny": _sb(8, F32), "tinyi": _sb(4, I32),
-    "u1": _sb(12, F32), "u2": _sb(12, F32), "u3": _sb(12, F32), "slu": _sb(12, U16), "mt": _sb(16, F32), "mE": _sb(192, F32), "ownc": _sb(192, F32),
-    "snd": _sb(4 * 256, F32), "lnd": _sb(4 * 64, F32), "gy": _sb(64, F32), "gxc": _sb(64, BF), "gx": _sb(64, BF), "gxT": _sb(128, BF),
+    "X": _sb(4112, BF), "col": _sb(W, I32), "odi": _sb(272, I32), "odu": _sb(84, U16), "Zi": _sb(96, I32), "nib": _sb(252, I32),
+    "odT": _sb(Q, BF), "odB": _sb(Q + 16, BF), "wti": _sb(4, I32), "thi": _sb(4, I32),
+    "pi": _sb(8, I32), "pf": _sb(32, F32), "j16": _sb(192, F32), "ia": _sb(128, F32), "ib": _sb(128, F32), "ic": _sb(128, F32),
+    "lf": _sb(96, F32), "diagS": _sb(192, F32), "diag4": _sb(64, F32), "clamp": _sb(192, F32), "kf": _sb(192, F32),
+    "patg": _sb(64, F32), "pat24": _sb(24, F32), "zero": _sb(192, BF), "kcon": _sb(192, BF), "qc": _sb(12, F32), "cb": _sb(32, BF),
+    "blkf": _sb(128, F32), "nblkf": _sb(128, F32), "blkb": _sb(128, BF), "lof": _sb(128, F32), "hif": _sb(128, F32),
+    "nlo": _sb(128, BF), "nhi": _sb(128, BF), "tri": _sb(128, BF), "sel15": _sb(128, BF),
+    "idf": _sb(128, F32), "idb": _sb(128, BF), "nid": _sb(128, BF), "n2k": _sb(128, BF), "p8k": _sb(128, BF),
+    "selA": _sb(2048, BF), "selW": _sb(2048, BF), "selO": _sb(2048, BF), "negE": _sb(1024, BF),
+    "bc12": _sb(12, U16), "bcg": _sb(4, U16), "perm1": _sb(12, U16), "perm2": _sb(12, U16), "zl": _sb(8, U16),
+    "vp": _sb(12, F32), "vm": _sb(12, F32), "M": _sb(12, F32), "kcnf": _sb(12, F32), "nf": _sb(96, BF), "q": _sb(12, BF), "cur": _sb(8, F32),
+    "idxu": _sb(12, U16), "GBb": _sb(192, BF), "oi": _sb(12, I32), "oi2": _sb(12, I32), "ou": _sb(12, U16), "vu": _sb(12, U16),
+    "cbuf": _sb(224, F32), "trb": _sb(416, F32), "xo": _sb(192, U16),
+    "own4": _sb(768, BF), "v4u": _sb(48, U16), "bc4": _sb(4, U16), "dif": _sb(3072, BF), "A": _sb(3072, BF), "Gs": _sb(512, BF),
+    "nvb": _sb(192, F32), "cO": _sb(192, F32), "sg": _sb(192, BF), "ed": _sb(192, F32), "pen": _sb(192, BF),
+    "Rb": _sb(200, F32), "keep": _sb(192, F32), "Kb": _sb(192, F32), "Fl": _sb(24, BF), "In": _sb(24, BF),
+    "limh": _sb(8, F32), "tiny": _sb(8, F32), "tinyi": _sb(4, I32),
+    "slf": _sb(12, F32), "slu": _sb(12, U16), "mE": _sb(192, F32), "ownc": _sb(192, F32),
+    "snd": _sb(4 * 256, F32), "lnd": _sb(4 * 64, F32), "gy": _sb(64, F32), "gx": _sb(64, BF), "gxT": _sb(128, BF),
     "mR": _sb(64, F32), "hi": _sb(4, I32), "hi2": _sb(4, I32), "hu": _sb(4, U16), "gcu": _sb(64, U16), "G": _sb(1024, BF), "Ag": _sb(1024, BF),
     "Rg": _sb(64, F32), "Eg": _sb(64, F32), "jud": _sb(64, F32), "bl": _sb(32, F32),
     "yni": _sb(Q, I32), "ynf": _sb(Q, F32), "yvf": _sb(12, F32), "ymf": _sb(12, F32),
@@ -46,8 +56,18 @@ SCRATCH = {
 for _b in range(8):
     SCRATCH["ps%d" % _b] = ("psum", [128, 512], F32)
 
-NDMA = 13
+NDMA = 17
 SEMAPHORES = ["cV", "cS", "cP", "cG", "sent"] + ["d%d" % i for i in range(NDMA)] + ["ga%d" % i for i in range(4)] + ["gb%d" % i for i in range(4)]
+
+
+def _sequence(setup, calls):
+    ops, left = list(setup), dict(calls)
+    for t in range(NT):
+        for name in ROUNDS[t].split():
+            ops += left.pop({"-": (name[1:], t - 1), "+": (name[1:], "late")}.get(name[0], (name, t)), [])
+    ops += left.pop(("end", "end"))
+    assert not left, sorted(left, key=str)
+    return ops
 
 
 def _emit(g, T, ops):
@@ -79,7 +99,9 @@ def _emit(g, T, ops):
             writer[k] = n
             readers[k] = []
     count = {e: 0 for e in queue}
-    for o in ops:
+    first = {o["sum"]: n for n, o in reversed(list(enumerate(ops))) if o["e"] == "P"}
+    last = {o["sum"]: n for n, o in enumerate(ops) if o["e"] == "P"}
+    for n, o in enumerate(ops):
         q = queue[o["e"]]
         for m in o["need"]:
             q.wait_ge(*ops[m]["done"])
@@ -87,7 +109,7 @@ def _emit(g, T, ops):
             q.wait_ge(s, v)
         if o["f"] is None:
             continue
-        ins = o["f"]()
+        ins = o["f"](first[o["sum"]] == n, last[o["sum"]] == n) if o["e"] == "P" else o["f"]()
         if o["dma"] is not None:
             o["done"] = (T.sem["d%d" % o["dma"]], 16)
             ins.then_inc(*o["done"])
@@ -102,26 +124,30 @@ def rank_program(g, core, T, topo):
     if rank is None:
         return
     N = len(T.cores)
-    ops = []
+    setup, calls, step = [], {}, [None]
     ndma = [0]
     V, S, PE = g.vector, g.scalar, g.tensor
 
-    def op(e, f, r=(), w=(), b=(), wait=(), dma=None):
-        ops.append({"e": e, "f": f, "r": list(r), "w": list(w), "b": list(b), "wait": list(wait), "dma": dma, "inc": False})
+    def op(e, f, r=(), w=(), b=(), wait=(), dma=None, name=None, total=None):
+        o = {"e": e, "f": f, "r": list(r), "w": list(w), "b": list(b), "wait": list(wait), "dma": dma, "inc": False, "sum": total}
+        if step[0] is None:
+            setup.append(o)
+        else:
+            calls.setdefault((name or w[0], step[0]), []).append(o)
 
     def dma(e, out, in_, r, w):
         q = g.sync if e == "Y" else g.scalar
         op(e, lambda: q.dma_start(out, in_), r, w, dma=ndma[0])
         ndma[0] += 1
 
-    def tt(out, a, b_, o, r, w, b=()):
-        op("V", lambda: V.tensor_tensor(out, a, b_, o), r, w, b)
+    def tt(out, a, b_, o, r, w, b=(), name=None):
+        op("V", lambda: V.tensor_tensor(out, a, b_, o), r, w, b, name=name)
 
-    def ts(out, a, s1, s2, o0, o1, r, w, b=()):
+    def ts(out, a, s1, s2, o0, o1, r, w, b=(), name=None):
         if o1 is None:
-            op("V", lambda: V.tensor_scalar(out, a, s1, None, o0), r, w, b)
+            op("V", lambda: V.tensor_scalar(out, a, s1, None, o0), r, w, b, name=name)
         else:
-            op("V", lambda: V.tensor_scalar(out, a, s1, s2, o0, o1), r, w, b)
+            op("V", lambda: V.tensor_scalar(out, a, s1, s2, o0, o1), r, w, b, name=name)
 
     def cp(out, a, r, w, b=()):
         op("V", lambda: V.tensor_copy(out, a), r, w, b)
@@ -135,14 +161,18 @@ def rank_program(g, core, T, topo):
     def scan(out, d0, d1, o0, o1, r, w, b=()):
         op("V", lambda: V.tensor_tensor_scan(out, d0, d1, 0.0, o0, o1), r, w, b)
 
-    def red(out, a, r, w, wait=()):
-        op("V", lambda: V.tensor_reduce(out, a, AxisListType.X, OP.max), r, w, wait=wait)
+    def red(out, a, r, w, o=OP.max, wait=(), name=None):
+        op("V", lambda: V.tensor_reduce(out, a, AxisListType.X, o), r, w, wait=wait, name=name)
 
-    def act(out, a, fn, r, w, bias=0.0, scale=1.0, b=(), wait=()):
-        op("S", lambda: S.activation(out, a, fn, bias=bias, scale=scale), r, w, b, wait)
+    def act(out, a, fn, r, w, bias=0.0, scale=1.0, b=(), wait=(), name=None):
+        op("S", lambda: S.activation(out, a, fn, bias=bias, scale=scale), r, w, b, wait, name=name)
 
-    def mm(out, lhsT, rhs, st, sp, r, b):
-        op("P", lambda: PE.matmul(out, lhsT, rhs, st, sp), r, (), [b])
+    def mms(name, total, terms, r, b, go_on=False):
+        def f(first, last):
+            for i, (out, lhsT, rhs) in enumerate(terms):
+                ins = PE.matmul(out, lhsT, rhs, first and i == 0 and not go_on, last and i == len(terms) - 1)
+            return ins
+        op("P", f, r, (), [b], name=name, total=(total, step[0]))
 
     def iota(out, pat, base, cm, w, small=True):
         if small:
@@ -150,262 +180,142 @@ def rank_program(g, core, T, topo):
         else:
             op("G", lambda: g.iota(out, pat, base, cm), (), w)
 
-    def pick(out, a, pat, o, base, cm, r, w):
-        op("G", lambda: g.affine_select(out, a, pat, o, 0.0, base, cm), r, w)
+    def pick(out, a, pat, o, base, cm, r, w, fill=0.0, name=None):
+        op("G", lambda: g.affine_select(out, a, pat, o, fill, base, cm), r, w, name=name)
 
-    PK, PC, PD, PP, PG0, PG1, PQ, PH = [T["ps%d" % i] for i in range(8)]
+    PK, PD, PC, PP, PG0, PG1, PQ, PH = [T["ps%d" % i] for i in range(8)]
     PG = ((PG0, 4), (PG1, 5))
     Xw = T.X[:, 0:4112]
     colw = T.col[:, 0:W]
+    pf = lambda i: T.pf[:, i:i + 1]
 
-    dma("Y", T.odi[:], T.od[:], [], ["odi"])
+    def sel(m, lo=0, hi=16):
+        return [m[:, 128 * a:128 * a + 128] for a in range(lo, hi)]
+
+    dma("Y", T.odi[:, 0:84], T.od[:], [], ["odi"])
+    dma("Y", T.odi[0:112, 84:168], T.od[16:128, :], [], ["odU"])
+    dma("Y", T.odi[16:128, 168:252], T.od[0:112, :], [], ["odD"])
+    dma("S", T.odi[112:128, 84:168], T.od[0:16, :], [], ["odU2"])
+    dma("S", T.odi[0:16, 168:252], T.od[112:128, :], [], ["odD2"])
     dma("Y", T.col[:], T.nb[:], [], ["col"])
     dma("Y", T.X[:, 0:W], T.xs[:], [], ["Xa"])
     ms(T.thi[:], 0, ["thi"])
+    ms(T.odi[:, 252:272], 0, ["odP"])
     ms(T.selA[:], 0.0, ["selA0"])
     dma("S", T.X[:, W:W + 16], T.xs[:, 0:16], [], ["Xb"])
     dma("S", T.wti[:, 0:1], T.wt[:], [], ["wti"])
     dma("S", T.thi[0:128:16, 0:1], T.th[:], [], ["thi"])
     XK = ["Xa", "Xb"]
 
-    pm, pp, gam, pc15, pper = (T.pf[:, i:i + 1] for i in range(5))
+    pm = pf(0)
     iota(T.pi[:, 0:1], [[0, 1]], 0, 1, ["pi0"], False)
-    iota(T.j16[:], [[0, 12], [1, 16]], 0, 0, ["j16"])
-    iota(T.li[:, 0:84], [[1, 84]], 0, 0, ["li"], False)
     iota(T.ia[:], [[-16, 8], [0, 16]], 0, 1, ["ia"])
+    iota(T.lf[:, 24:36], [[16, 12]], 0, 0, ["lf2"])
+    iota(T.lf[:, 0:12], [[1, 12]], 0, 0, ["lf0"])
     iota(T.idf[:], [[1, 128]], 0, -1, ["idf0"])
-    ts(T.pi[:, 1:2], T.pi[:, 0:1], 15, None, OP.bitwise_and, None, ["pi0"], ["pi1"])
-    ms(T.odB[:, 0:1], 0.0, ["odB0"])
-    cp(pm, T.pi[:, 1:2], ["pi1"], ["pm"])
-    ts(T.diag[:], T.j16[:], pm, None, OP.is_equal, None, ["j16", "pm"], ["diag"])
-    cp(T.bc84[:], T.li[:, 0:84], ["li"], ["bc84"])
-    ts(T.pf[:, 16:17], pm, 1.0, None, OP.is_equal, None, ["pm"], ["p16"])
-    ts(T.pf[:, 17:18], pm, 0.0, None, OP.not_equal, None, ["pm"], ["p17"])
+    iota(T.lf[:, 12:24], [[1, 4], [64, 3]], 0, 0, ["lf1"])
+    iota(T.lf[:, 36:48], [[0, 6], [1, 2]], 0, 0, ["lf3"])
+    iota(T.cbuf[:, 0:16], [[0, 16]], 0, 0, ["c0"])
+    iota(T.cbuf[:, 208:224], [[0, 16]], 0, 0, ["c1"])
+    iota(T.zero[:], [[0, 192]], 0, 0, ["zero"])
+    iota(T.kf[:], [[16, 12], [-1, 16]], 16, 0, ["kf"])
+    iota(T.clamp[:], [[0, 192]], -4095, 0, ["clamp0"])
+    iota(T.Rb[:, 0:1], [[0, 1]], 0, 0, ["Rb0"])
+    pick(T.clamp[:], T.clamp[:], [[0, 12], [1, 16]], OP.is_equal, 0, 0, ["clamp0"], ["clamp0", "clamp"], 65536.0)
     ts(T.ib[:], T.ia[:], 0.0, None, OP.is_ge, None, ["ia"], ["ib"])
     ts(T.ic[:], T.ia[:], 15.0, None, OP.is_le, None, ["ia"], ["ic"])
-    ts(gam, T.pf[:, 16:17], 32.0, T.pf[:, 17:18], OP.mult, OP.add, ["p16", "p17"], ["gam"])
-    ts(T.pf[:, 18:19], T.pf[:, 16:17], T.pf[:, 17:18], -1.0, OP.add, OP.add, ["p16", "p17"], ["p18"])
+    ts(T.pi[:, 1:2], T.pi[:, 0:1], 15, None, OP.bitwise_and, None, ["pi0"], ["pi1"])
     tt(T.blkf[:], T.ib[:], T.ic[:], OP.mult, ["ib", "ic"], ["blkf"])
-    ts(T.ib[:], T.j16[:, 0:128], 1.0, None, OP.is_equal, None, ["j16"], ["ib"])
-    ts(T.idf[:], T.idf[:], 0.0, None, OP.is_equal, None, ["idf0"], ["idf"])
-    ts(T.odf[:, 0:84], T.odi[:], 4048.0, None, OP.add, None, ["odi"], ["odf"])
-    tt(T.blk1[:], T.ib[:], T.blkf[:], OP.mult, ["ib", "blkf"], ["blk1"])
-    act(T.dbeta[:], T.idf[:], AF.Copy, ["idf", "p18"], ["dbeta"], scale=T.pf[:, 18:19])
-    def od_spread(c):
-        tt(T.odE[:, 192 * c:192 * c + 192], T.odf[:, 0:84].indirect(T.bc84[:, 12 * c:12 * c + 12]), T.diag[:], OP.mult,
-           ["odf", "bc84", "diag"], ["odE%d" % c])
-
-    PIECES = [(0, 192, 7, 6), (192, 576, 7, 6), (576, 960, 7, 6), (960, 1344, 7, 6)]
-
-    def od_a(c):
-        lo, hi, b1, b2 = PIECES[c]
-        need = ["odE%d" % i for i in range(lo // 192, hi // 192)]
-        mm(T["ps%d" % b1][:, 0:hi - lo], T.blkf[:], T.odE[:, lo:hi], True, True, ["blkf"] + need, b1)
-        mm(T["ps%d" % b2][:, 0:hi - lo], T.blk1[:], T.odE[:, lo:hi], True, False, ["blk1"] + need, b2)
-
-    def od_b(c):
-        lo, hi, b1, b2 = PIECES[c]
-        act(T.odM[:, lo:hi], T["ps%d" % b1][:, 0:hi - lo], AF.Identity, [], ["odM%d" % c], bias=MAGIC64, b=[b1])
-        act(T.odH[:, lo:hi], T.odM[:, lo:hi], AF.Identity, ["odM%d" % c], ["odH%d" % c], bias=MAGIC64, scale=-1.0)
-        mm(T["ps%d" % b2][:, 0:hi - lo], T.dbeta[:], T.odH[:, lo:hi], False, True, ["dbeta", "odH%d" % c], b2)
-
-    def od_c(c):
-        lo, hi, b1, b2 = PIECES[c]
-        act(T.odB[:, 1 + lo:1 + hi], T["ps%d" % b2][:, 0:hi - lo], AF.Identity, ["gam"], ["odB%d" % (c + 1)], bias=gam, b=[b2])
-
-    od_spread(0)
-    od_a(0)
-    od_b(0)
-    od_c(0)
-    ODB = ["odB%d" % i for i in range(5)]
-    iota(T.lf[:, 0:12], [[1, 12]], 1, 0, ["lf0"])
-    iota(T.lf[:, 12:24], [[1, 4], [64, 3]], 0, 0, ["lf1"])
-    iota(T.lf[:, 24:36], [[16, 12]], 0, 0, ["lf2"])
-    iota(T.lf[:, 36:48], [[0, 6], [1, 2]], 0, 0, ["lf3"])
-    iota(T.lf[:, 48:51], [[4, 3]], 0, 0, ["lf4"])
-    iota(T.off12[:], [[4096, 12]], 5 * 4096, 0, ["off12"])
-    iota(T.clamp[:], [[4096, 12], [0, 16]], 4 * 4096 + 1, 0, ["clamp0"])
-    iota(T.ed[:], [[16, 12], [-1, 16]], 15, 0, ["ed"])
-    iota(T.diag4[:], [[1, 16], [0, 4]], 0, 0, ["diag4a"])
-    pick(T.sel15[:], T.blkf[:], [[-16, 8], [0, 16]], OP.is_equal, -15, 1, ["blkf"], ["sel15"])
-    iota(T.Rb[:, 0:1], [[0, 1]], 0, 0, ["Rb0"])
-    iota(T.free[:], [[0, 16]], 0, 0, ["free"])
-    iota(T.cur0[:], [[0, 4]], L, 0, ["cur0"])
-    iota(T.pat24[:], [[0, 24]], 1, 0, ["pat24"])
-    iota(T.Fl[:], [[0, 24]], 0, 0, ["dead", "go"])
-    iota(T.pat24[:, 12:13], [[0, 1]], 0, 0, ["pat24"])
-    iota(T.mt[:], [[0, 16]], 0, 0, ["mt"])
-    iota(T.patg[:], [[0, 64]], -65536, 0, ["patg"])
-    pick(T.patg[:], T.patg[:], [[0, 4], [1, 16]], OP.is_equal, 0, 0, ["patg"], ["patg"])
-    ts(T.pf[:, 5:6], pm, 12.0, None, OP.mult, None, ["pm"], ["p12"])
-    ms(T.S2[:], 0.0, ["S2"])
-    ts(T.idxu[:], T.lf[:, 0:12], T.pf[:, 5:6], None, OP.add, None, ["lf0", "p12"], ["idxu"])
-    for a in range(16):
-        ts(T.selA[:, 129 * a:128 * a + 128:16], T.blkf[:, 0:128:16], -1.0, None, OP.mult, None, ["blkf", "selA0"], ["selA%d" % (a + 1)])
-    SELA = ["selA%d" % i for i in range(17)]
-    ts(T.pi[:, 2:3], T.pi[:, 1:2], 2, None, OP.arith_shift_right, None, ["pi1"], ["pi2"])
-    ts(T.pi[:, 3:4], T.pi[:, 1:2], 3, None, OP.bitwise_and, None, ["pi1"], ["pi3"])
+    ts(T.pi[:, 2:3], T.pi[:, 0:1], 2, 3, OP.arith_shift_right, OP.bitwise_and, ["pi0"], ["pi2"])
+    ts(T.pi[:, 3:4], T.pi[:, 0:1], 3, None, OP.bitwise_and, None, ["pi0"], ["pi3"])
     ts(T.pi[:, 4:5], T.pi[:, 0:1], 4, 1, OP.arith_shift_right, OP.bitwise_and, ["pi0"], ["pi4"])
     ts(T.pi[:, 5:6], T.pi[:, 0:1], 2, 1, OP.arith_shift_right, OP.bitwise_and, ["pi0"], ["pi5"])
-    ms(T.St[:], 0.0, ["vp", "M", "nfp"])
-    cp(T.pf[:, 8:12], T.pi[:, 2:6], ["pi2", "pi3", "pi4", "pi5"], ["p8"])
-    ms(T.kcnf[:], 0.0, ["kcnf"])
-    ms(T.cbuf[:, 0:16], 0.0, ["c0"])
-    ms(T.cbuf[:, 208:224], 0.0, ["c1"])
-    ts(T.bc4[:, 0:3], T.lf[:, 48:51], T.pf[:, 8:9], None, OP.add, None, ["lf4", "p8"], ["bc4"])
-    tt(T.pf[:, 6:7], T.pf[:, 10:11], T.pf[:, 11:12], OP.not_equal, ["p8"], ["p6"])
-    ts(T.pf[:, 7:8], T.pf[:, 8:9], 16.0, None, OP.mult, None, ["p8"], ["p7"])
-    ts(T.lf[:, 52:64], T.lf[:, 36:48], T.pf[:, 10:11], 208.0, OP.not_equal, OP.mult, ["lf3", "p8"], ["lf5"])
-    ts(T.pf[:, 12:13], T.pf[:, 9:10], 4.0, T.pf[:, 7:8], OP.mult, OP.add, ["p8", "p7"], ["p12b"])
+    ts(T.pi[:, 6:7], T.pi[:, 0:1], 1, None, OP.bitwise_and, None, ["pi0"], ["pi6"])
+    cp(pm, T.pi[:, 1:2], ["pi1"], ["pm"])
+    for a in range(16):
+        ts(T.selA[:, 129 * a:128 * a + 128:16], T.blkf[:, 0:128:16], -1.0, None, OP.mult, None, ["blkf", "selA0"], ["selA%d" % (a + 1)])
+        if a == 0:
+            cp(T.pf[:, 8:13], T.pi[:, 2:7], ["pi2", "pi3", "pi4", "pi5", "pi6"], ["p8"])
+            for i, wgt in enumerate((64.0, 1024.0, 16384.0, -13312.0, -65.0)):
+                ts(pf(16 + i), pm, float(i), -wgt, OP.is_equal, OP.mult, ["pm"], ["ow%d" % i])
+        if a == 1:
+            red(pf(1), T.pf[:, 16:21], ["ow%d" % i for i in range(5)], ["ow"], OP.add)
+        if a % 8 == 7:
+            h = a // 8
+            act(T.selO[:, 1024 * h:1024 * h + 1024], T.selA[:, 1024 * h:1024 * h + 1024], AF.Copy,
+                ["selA%d" % i for i in range(a + 2)] + ["ow"], ["selO%d" % h], scale=pf(1))
+    SELA = ["selA%d" % i for i in range(17)]
+
+    tt(pf(13), pf(12), pf(10), OP.not_equal, ["p8"], ["p13"])
+    ts(pf(14), pf(10), 86.0, 83.0, OP.mult, OP.add, ["p8"], ["p14"])
+    ts(T.idf[:], T.idf[:], 0.0, None, OP.is_equal, None, ["idf0"], ["idf"])
+    ts(pf(15), pf(13), pf(14), pm, OP.mult, OP.add, ["p13", "p14", "pm"], ["p15"])
+    ms(T.odB[:, 0:16], 0.0, ["odB0"])
+    ts(T.zl[:, 0:6], T.lf[:, 24:30], pf(15), None, OP.add, None, ["lf2", "p15"], ["zl"])
+    ms(T.odT[:], 1.0, ["odT"])
+    cp(T.Zi[:], T.odi[:, 0:272].indirect(T.zl[:, 0:6]), ["odi", "odU", "odD", "odU2", "odD2", "odP", "zl"], ["Zi"])
+    ts(pf(5), pm, 12.0, 16.0, OP.mult, OP.add, ["pm"], ["p5"])
+    for i in range(3):
+        ts(T.nib[:, 84 * i:84 * i + 84], T.Zi[:, 0:84], 4 * i, 15, OP.arith_shift_right, OP.bitwise_and, ["Zi"], ["nib%d" % i])
+    for i in range(3):
+        ts(T.odT[:, i:Q:16], T.nib[:, 84 * i:84 * i + 84], 1.0 / 64, 1.0, OP.mult, OP.add, ["nib%d" % i, "odT"], ["odT%d" % i])
+    ts(T.idxu[:], T.lf[:, 0:12], pf(5), None, OP.add, None, ["lf0", "p5"], ["idxu"])
+    turn(T.odB[:, 16:208], T.odT[:, 0:192], ["odT0", "odT1", "odT2"], ["odB1"])
+    for name, src, f in (("idb", "idf", 1.0), ("n2k", "idf", -2048.0), ("nid", "idf", -1.0), ("blkb", "blkf", 1.0), ("kcon", "kf", 8192.0)):
+        act(T[name][:], T[src][:], AF.Copy, [src], [name], scale=f)
+
+    tt(pf(6), pf(10), pf(11), OP.not_equal, ["p8"], ["p6"])
+    ts(pf(7), pf(8), 16.0, None, OP.mult, None, ["p8"], ["p7"])
+    ts(T.lf[:, 52:64], T.lf[:, 36:48], pf(10), 208.0, OP.not_equal, OP.mult, ["lf3", "p8"], ["lf5"])
+    ts(pf(2), pf(9), 4.0, pf(7), OP.mult, OP.add, ["p8", "p7"], ["p2"])
     tt(T.lf[:, 64:76], T.lf[:, 52:64], T.lf[:, 24:36], OP.add, ["lf5", "lf2"], ["lf6"])
-    ts(pper, T.pf[:, 6:7], 208.0, T.pf[:, 12:13], OP.mult, OP.add, ["p6", "p12b"], ["pper"])
+    ts(pf(4), pf(6), 208.0, pf(2), OP.mult, OP.add, ["p6", "p2"], ["p4"])
     ts(T.perm2[:], T.lf[:, 64:76], pm, None, OP.add, None, ["lf6", "pm"], ["perm2"])
-    ts(T.perm1[:], T.lf[:, 12:24], pper, None, OP.add, None, ["lf1", "pper"], ["perm"])
-    od_spread(1)
-    od_spread(2)
+    ts(T.perm1[:], T.lf[:, 12:24], pf(4), None, OP.add, None, ["lf1", "p4"], ["perm"])
+    cp(T.bc12[:], T.lf[:, 0:12], ["lf0"], ["bc12"])
+    ts(T.bc4[:, 0:3], T.lf[:, 0:12:4], pf(8), None, OP.add, None, ["lf0", "p8"], ["bc4"])
+    iota(T.cur[:, 0:1], [[0, 1]], L + 15, 0, ["cur0"])
+    iota(T.pat24[:], [[0, 24]], 1, 0, ["pat24"])
+    iota(T.cb[:], [[-8191, 2], [0, 16]], -1, 0, ["cb"])
+    iota(T.pat24[:, 12:13], [[0, 1]], 0, 0, ["pat24"])
+    pick(T.tri[:], T.blkb[:], [[1, 128]], OP.is_gt, 0, -1, ["blkb"], ["tri"])
+    iota(T.j16[:], [[0, 12], [1, 16]], 0, 0, ["j16"])
+    iota(T.diag4[:], [[1, 16], [0, 4]], 0, 0, ["diag4a"])
+    pick(T.sel15[:], T.blkb[:], [[-16, 8], [0, 16]], OP.is_equal, -15, 1, ["blkb"], ["sel15"])
+    pick(T.lof[:], T.blkf[:], [[16, 8], [0, 16]], OP.is_ge, 7, -1, ["blkf"], ["lof"])
+    pick(T.hif[:], T.blkf[:], [[-16, 8], [0, 16]], OP.is_ge, -8, 1, ["blkf"], ["hif"])
+    iota(T.patg[:], [[0, 64]], -65536, 0, ["patg"])
+    iota(T.negE[:], [[0, 1024]], -1, 0, ["negE"])
+    pick(T.patg[:], T.patg[:], [[0, 4], [1, 16]], OP.is_equal, 0, 0, ["patg"], ["patg"])
+    pick(T.negE[:], T.negE[:], [[1, 64], [0, 16]], OP.is_equal, 0, -1, ["negE"], ["negE"])
+    iota(T.snd[:], [[0, 1024]], 0, 0, ["snd0", "snd1", "snd2", "snd3"])
 
-    def matrices():
-        act(T.offc[:], T.clamp[:], AF.Identity, ["clamp0"], ["offc"], bias=4095.0)
-        act(T.tri[:], T.blkf[:], AF.Copy, ["blkf"], ["tri"])
-        act(T.idb[:], T.idf[:], AF.Copy, ["idf"], ["idb"])
-        act(T.n2k[:], T.idf[:], AF.Copy, ["idf"], ["n2k"], scale=-2048.0)
-        act(T.nid[:], T.idf[:], AF.Copy, ["idf"], ["nid"], scale=-1.0)
-        act(T.kcon[:], T.ed[:], AF.Copy, ["ed"], ["kcon"], scale=8192.0)
-        pick(T.clamp[:], T.clamp[:], [[0, 12], [1, 16]], OP.is_equal, 0, 0, ["clamp0"], ["clamp0", "clamp"])
-        pick(T.tri[:], T.tri[:], [[1, 128]], OP.is_gt, 0, -1, ["tri"], ["tri"])
-        iota(T.negE[:], [[0, 1024]], -1, 0, ["negE"])
-        pick(T.negE[:], T.negE[:], [[1, 64], [0, 16]], OP.is_equal, 0, -1, ["negE"], ["negE"])
-        iota(T.snd[:], [[0, 1024]], 0, 0, ["snd0", "snd1", "snd2", "snd3"])
+    step[0] = "late"
+    turn(T.odB[:, 208:Q + 16], T.odT[:, 192:Q], ["odT0", "odT1", "odT2"], ["odB2"])
+    cp(pf(22), T.thi[:, 0:1], ["thi"], ["thf"])
+    mms("th_", "th", [(PP[:, 100:101], T.blkf[:], pf(22))], ["blkf", "thf"], 3)
+    ts(T.limh[:, 0:3], T.lf[:, 0:3], 0.0, PP[:, 100:101], OP.mult, OP.add, ["lf0"], ["lim0", "lim1", "lim2"], [3])
+    act(T.p8k[:], T.idf[:], AF.Copy, ["idf"], ["p8k"], scale=8192.0)
+    cp(T.odu[:], T.odi[:, 0:84], ["odi"], ["odu"])
+    ts(T.qc[:], T.lf[:, 24:36], pm, 65.0, OP.add, OP.add, ["lf2", "pm"], ["qc"])
+    ts(pf(3), pf(9), 16.0, 15.0, OP.mult, OP.add, ["p8"], ["p3"])
+    ts(pf(21), T.wti[:, 0:1], -1.0, None, OP.mult, None, ["wti"], ["wtf"])
+    ts(T.bcg[:], T.lf[:, 0:4], 0.0, pf(3), OP.mult, OP.add, ["lf0", "p3"], ["bcg"])
+    ts(T.diagS[:], T.j16[:], pm, 1.0 / 8192, OP.is_equal, OP.mult, ["j16", "pm"], ["diagS"])
+    ts(T.diag4[:], T.diag4[:], pm, None, OP.is_equal, None, ["diag4a", "pm"], ["diag4"])
+    for name, src in (("nblkf", "blkf"), ("nlo", "lof"), ("nhi", "hif")):
+        act(T[name][:], T[src][:], AF.Copy, [src], [name], scale=-1.0)
+    for h in range(2):
+        act(T.selW[:, 1024 * h:1024 * h + 1024], T.selA[:, 1024 * h:1024 * h + 1024], AF.Copy, SELA + ["wtf"], ["selW%d" % h], scale=pf(21))
 
-    def late_constants():
-        ts(T.qc[:], T.lf[:, 24:36], pm, 65.0, OP.add, OP.add, ["lf2", "pm"], ["qc"])
-        ts(T.bcp[:], T.lf[:, 0:4], 0.0, pm, OP.mult, OP.add, ["lf0", "pm"], ["bcp"])
-        ts(T.pf[:, 13:14], T.pf[:, 9:10], 16.0, 15.0, OP.mult, OP.add, ["p8"], ["p13"])
-        ts(T.bcg[:], T.lf[:, 0:4], 0.0, T.pf[:, 13:14], OP.mult, OP.add, ["lf0", "p13"], ["bcg"])
-
-    def input_constants(part):
-        if part == 0:
-            cp(T.thf[:, 0:1], T.thi[:, 0:1], ["thi"], ["thf"])
-            mm(PP[:, 20:21], T.blkf[:], T.thf[:, 0:1], True, True, ["blkf", "thf"], 3)
-            return
-        ts(T.wtf[:, 0:1], T.wti[:, 0:1], -1.0, None, OP.mult, None, ["wti"], ["wtf"])
-        ts(T.diag4[:], T.diag4[:], pm, None, OP.is_equal, None, ["diag4a", "pm"], ["diag4"])
-        if 0 not in OPT["relu"]:
-            cp(T.odu[:], T.odi[:], ["odi"], ["odu"])
-        ts(T.limh[:, 0:3], T.lf[:, 0:3], 0.0, PP[:, 20:21], OP.mult, OP.add, ["lf0"], ["lim2"], [3])
-        ts(T.limoff[:], T.off12[:], PP[:, 20:21], None, OP.subtract, None, ["off12"], ["limoff"], [3])
-
-    def guest_constants(t):
-        if t == 0:
-            act(T.nblkb[:], T.blkf[:], AF.Copy, ["blkf"], ["nblkb"], scale=-1.0)
-            act(T.nblkf[:], T.blkf[:], AF.Copy, ["blkf"], ["nblkf"], scale=-1.0)
-            act(T.diagS[:], T.diag[:], AF.Copy, ["diag"], ["diagS"], scale=1.0 / 8192)
-            if not THV[0]:
-                limits(2)
-        lo, hi = (0, 1024, 1536, 2048)[t:t + 2]
-        act(T.selW[:, lo:hi], T.selA[:, lo:hi], AF.Copy, SELA + ["wtf"], ["selW"], scale=T.wtf[:, 0:1])
-
-    vp, M = T.St[:, 0:12], T.St[:, 16:28]
+    M = T.M[:, 0:12]
     dead, go = T.Fl[:, 0:12], T.Fl[:, 12:24]
     Id, Ig = T.In[:, 0:12], T.In[:, 12:24]
     cnat = T.cbuf[:, 16:208]
+    I, nk, p8 = T.idb[:], T.n2k[:], T.p8k[:]
+    PV, PX, PT, PS, PM, PA, PI = PH[:, 16:28], PP[:, 16:28], PP[:, 32:44], PC[:, 0:12], PC[:, 16:28], PC[:, 32:44], PC[:, 48:49]
+    OWN = ["own"]
     nsent = [0]
-    ODA = []
-
-    def state():
-        ts(T.nf3[:], T.free[:, 0:16].indirect(T.bcp[:, 0:3]), -1.0, 1.0, OP.mult, OP.add, ["free", "bcp"], ["nf3"])
-
-    def state2():
-        tt(T.S2[:], T.St[:], T.nf3[:], OP.mult, ["vp", "M", "nfp", "nf3"], ["S2"])
-
-    def state3():
-        tt(T.kcnf[:], T.Kb[:, 15:192:16], T.nf3[:, 0:12], OP.mult, ["Kb", "nf3"], ["kcnf"])
-
-    def leavers(t):
-        i = t - 2
-        tt(T.u3[:], T.u2[:], T.qc[:], OP.add, ["u2", "qc"], ["u3"])
-        if not OPT["nfs"]:
-            state()
-        ts(T.slu[:], T.u3[:], -1.0, None, OP.add, None, ["u3"], ["slu"])
-        if not OPT["nfs"]:
-            state2()
-        tt(T.snd[:, 256 * i:256 * i + 256].indirect(T.slu[:]), T.ownc[:], T.mE[:], OP.add, ["slu", "ownc", "mE"], ["snd%d" % i])
-        dst = T.cores[(rank + 1 + t % (N - 1)) % N]
-        rid, pid, _ = topo.addr(dst)
-        mask = topo.mask(core, dst)
-        op("G", lambda: g.remote_dma(T.lnd[:, 64 * i:64 * i + 64], T.snd[:, 256 * i:256 * i + 64], T.sem["ga%d" % i], T.sem.sent, pid, rid, mask),
-           ["snd%d" % i])
-        nsent[0] += len(topo.engines(core, dst))
-
-    def unpack(t, part):
-        i = t - 3
-        src = T.cores[(rank - 1 - (t - 1) % (N - 1)) % N]
-        p = T.lnd[:, 64 * i:64 * i + 64]
-        if part == 0:
-            act(T.gy[:], p, AF.Identity, [], ["gy"], bias=MAGIC, wait=[(T.sem["ga%d" % i], len(topo.engines(src, core)))])
-            return
-        act(T.gx[:], T.gy[:], AF.Identity, ["gy"], ["gx"], bias=128.0 - MAGIC)
-        act(T.gxc[:], T.gy[:], AF.Identity, ["gy"], ["gxc"], bias=-MAGIC)
-
-    def unpack_p(t):
-        p = T.lnd[:, 64 * (t - 3):64 * (t - 3) + 64]
-        for a in range(16):
-            mm(PH[:, 0:4], T.selW[:, 128 * a:128 * a + 128], T.gx[:, a:64:16], a == 0, a == 15, ["selW", "gx"], 7)
-        mm(PD[0:64, 256:384], T.gx[:], T.idb[:], True, True, ["gx", "idb"], 2)
-        mm(PD[:, 384:448], T.blkf[:], p, True, False, ["blkf", "gxc"], 2)
-        mm(PD[:, 384:448], T.nblkb[:], T.gxc[:], False, True, ["nblkb", "gxc"], 2)
-
-    def unpack2():
-        act(T.gxT[0:64, :], PD[0:64, 256:384], AF.Copy, [], ["gxT"], b=[2])
-        act(T.mR[:], PD[:, 384:448], AF.Copy, [], ["mR"], scale=8192.0, b=[2])
-
-    def hsum(t):
-        ts(T.hi[:], PH[:, 0:4], 77.0 * t, None, OP.add, None, [], ["hi"], [7])
-
-    def hchain(t, best=False, part=None):
-        early = OPT["hearly"] and t < NT - 1
-        if part != 1 and not early:
-            hsum(t)
-        if (part != 1) if early else (part != 0):
-            ts(T.hi2[:], T.hi[:], W - 1, None, OP.bitwise_and, None, ["hi"], ["hi2"])
-        if part == 0:
-            return
-        if best and not early:
-            thresholds(t - 1)
-        cp(T.hu[:], T.hi2[:], ["hi2"], ["hu"])
-        if best and early:
-            thresholds(t - 1)
-        cp(T.gcu[:], colw.indirect(T.hu[:]), ["col", "hu"], ["gcu"])
-
-    def gdist_a(halves=False):
-        if halves:
-            act(T.G[:, 0:512], Xw.indirect(T.gcu[:, 0:32]), AF.Copy, XK + ["gcu"], ["G0"])
-            if OPT["gv"]:
-                cp(T.G[:, 512:1024], Xw.indirect(T.gcu[:, 32:64]), XK + ["gcu"], ["G1"])
-            else:
-                act(T.G[:, 512:1024], Xw.indirect(T.gcu[:, 32:64]), AF.Copy, XK + ["gcu"], ["G1"])
-        else:
-            act(T.G[:], Xw.indirect(T.gcu[:]), AF.Copy, XK + ["gcu"], ["G0", "G1"])
-
-    def gdist_p():
-        for h, (bank, nm) in enumerate(PG):
-            mm(bank[:], T.gxT[0:64, :], T.negE[0:64, 512 * h:512 * h + 512], True, False, ["gxT", "negE"], nm)
-            mm(bank[:], T.idb[:], T.G[:, 512 * h:512 * h + 512], False, True, ["idb", "G%d" % h], nm)
-
-    def gdist_s(h):
-        act(T.Ag[:, 512 * h:512 * h + 512], PG[h][0][:], AF.Abs, [], ["Ag%d" % h], b=[PG[h][1]])
-
-    def gdist_r():
-        for a in range(16):
-            mm(PQ[:, 0:64], T.selA[:, 128 * a:128 * a + 128], T.Ag[:, 64 * a:64 * a + 64], a == 0, a == 15, SELA + ["Ag%d" % (a // 8)], 6)
-
-    def judge_a(part=None):
-        if part != 1:
-            scan(T.Rg[:], T.patg[:], PQ[:, 0:64], OP.add, OP.max, ["patg"], ["Rg"], [6])
-        if part == 0:
-            return
-        tt(T.Eg[:], T.Rg[:, 0:64].indirect(T.bcg[:]), T.diag4[:], OP.mult, ["Rg", "bcg", "diag4"], ["Eg"])
-        mm(PQ[:, 64:128], T.nblkf[:], T.Eg[:], True, True, ["nblkf", "Eg"], 6)
 
     def to_all(s):
         mask = -1
@@ -414,364 +324,190 @@ def rank_program(g, core, T, topo):
                 mask &= topo.mask(s, d)
         return mask
 
-    def judge_b(t, part=None):
+    def refill(t):
+        act(T.GBb[:], T.odB[:, 0:(208 if t == 0 else Q + 16)].indirect(T.idxu[:]), AF.Copy, ["odB0", "odB1", "idxu"] + ["odB2"] * (t > 0), ["GB"])
+        if t > 0:
+            mms("Vm", "V", [(PV, T.idf[:], T.vm[:])], ["idf", "vm"], 7)
+        mms("V", "V", [(PV, m, T.GBb[:, a:192:16]) for a, m in enumerate(sel(T.selO))], ["selO0", "selO1", "GB"], 7)
+        if t == 0:
+            cp(T.oi[:], PV, [], ["oi"], [7])
+        else:
+            tt(T.oi[:], T.kcnf[:], PV, OP.add, ["kcnf"], ["oi"], [7])
+        ts(T.vu[:], PV, -4095.0, None, OP.add, None, [], ["vu"], [7])
+        ts(T.oi2[:], T.oi[:], W - 1, None, OP.bitwise_and, None, ["oi"], ["and"])
+        cp(T.ou[:], T.oi2[:], ["and"], ["ou"])
+        cp(T.vp[:], PV, [], ["vp"], [7])
+        ts(T.v4u[:], T.vp[:, 0:12].indirect(T.bc4[:, 0:3]), -4095.0, None, OP.add, None, ["vp", "bc4"], ["v4u"])
+        tt(cnat, colw.indirect(T.ou[:]), T.GBb[:], OP.add, ["col", "ou", "GB"], ["c"])
+        act(T.own4[:], Xw.indirect(T.v4u[:]), AF.Copy, XK + ["v4u"], ["own"])
+        turn(T.trb[:, 0:192], T.cbuf[:, 16:208], ["c"], ["tr1"])
+        turn(T.trb[:, 192:416], T.cbuf[:, 0:224], ["c", "c0", "c1"], ["tr2"])
+        cp(T.xo[:, 0:64], T.trb[:, 0:416].indirect(T.perm1[:, 0:4]), ["tr1", "tr2", "perm"], ["xo0"])
+        cp(T.xo[:, 64:192], T.trb[:, 0:416].indirect(T.perm1[:, 4:12]), ["tr1", "tr2", "perm"], ["xo1"])
+        cp(colw.indirect(T.vu[:]), cnat, ["vu", "c"], ["col"])
+        if 2 <= t < NT - 1:
+            act(T.ownc[:], Xw.indirect(T.vu[:]), AF.Copy, XK + ["vu"], ["ownc"])
+
+    def penalty(t):
+        act(T.nvb[:], T.vp[:, 0:12].indirect(T.bc12[:]), AF.Identity, ["vp", "bc12"], ["nvb"], bias=4096.0, scale=-1.0)
+        act(T.cO[:], T.trb[:, 0:416].indirect(T.perm2[:]), AF.Copy, ["tr1", "tr2", "perm2"], ["cO"])
+        act(T.sg[:], T.cO[:], AF.Sign, ["cO"], ["sg"], bias=-4095.5)
+        mms("Dv", "D", [(PD[:, 0:192], T.idf[:], T.nvb[:])], ["idf", "nvb"], 1)
+        mms("Dc", "D", [(PD[:, 0:192], T.idf[:], T.cO[:]), (PD[:, 0:192], nk, T.sg[:])], ["idf", "cO", "n2k", "sg"], 1)
+        act(T.ed[:], PD[:, 0:192], AF.Abs, [], ["ed"], bias=-2049.0, b=[1])
+        act(T.pen[:], T.ed[:], AF.Relu, ["ed"], ["pen"], bias=124.0, scale=-8.0)
+        if t < NT - 1:
+            mms("Cv", "C", [(PC[:, 64:256], I, T.kcon[:]), (PC[:, 64:256], T.idf[:], T.nvb[:])], ["idb", "kcon", "idf", "nvb"], 2)
+            mms("Cc", "C", [(PC[:, 64:256], T.idf[:], T.cO[:])], ["idf", "cO"], 2)
+
+    def ksum(name, c, src, n, keys):
+        mms(name, "K", [(PK[:, c:c + n // 4:4], m, src[:, 768 * c + a:768 * c + n:16]) for a, m in enumerate(sel(T.selA))], SELA + keys, 0)
+
+    def distances(t):
+        ns, n = 64 * SHARE[t], RELU[t]
+        e = 768 - ns
+        mms("zero", "K", [(PK[:, 0:192], I, T.zero[:])], ["idb", "zero"], 0)
+        mms("Kp", "K", [(PK[:, 0:192], nk, T.pen[:])], ["n2k", "pen"], 0)
+        act(T.Gs[:, 0:ns], Xw.indirect(T.xo[:, 144 + e // 16:192]), AF.Copy, XK + ["xo1"], ["Gs"])
+        mms("Gown" if t < NT - 1 else "Gsub", "G", [(PG0[:, 0:ns], T.nid[:], T.own4[:, e:768])], ["nid"] + OWN, 4)
+        mms("Gsub", "G", [(PG0[:, 0:ns], I, T.Gs[:, 0:ns])], ["idb", "Gs"], 4)
+        act(T.A[:, 2304 + e:3072], PG0[:, 0:ns], AF.Abs, [], ["As"], b=[4])
+        pieces = [(0, 0, 768), (1, 0, 768), (3, 0, e), (2, 0, CUT[t][0]), (2, CUT[t][0], CUT[t][1]), (2, CUT[t][1], 768)]
+        for i, (c, lo, hi) in enumerate(pieces):
+            if lo == hi:
+                continue
+            tt(T.dif[:, 768 * c + lo:768 * c + hi], Xw.indirect(T.xo[:, 48 * c + lo // 16:48 * c + hi // 16]), T.own4[:, lo:hi],
+               OP.subtract, XK + ["xo0"] + ["xo1"] * (c > 0) + OWN, ["g%d" % i])
+            if c == 1 and n:
+                ksum("r1", 1, T.dif, n, ["g1"])
+                ts(T.A[:, 768:768 + n], T.dif[:, 768:768 + n], -2.0, 0.0, OP.mult, OP.max, ["g1"], ["relu"])
+                lo = n
+            if lo < hi:
+                act(T.A[:, 768 * c + lo:768 * c + hi], T.dif[:, 768 * c + lo:768 * c + hi], AF.Abs, ["g%d" % i], ["a%d" % i])
+        for c, keys in enumerate((["a0"], ["a1", "relu"], ["a3", "a4", "a5"], ["a2", "As"])):
+            ksum("k%d" % c, c, T.A, 768, keys)
+
+    def arrive(t):
         i = t - 3
-        if part != 1:
-            tt(T.jud[:], PQ[:, 64:128], T.mR[:], OP.min, ["mR"], ["jud"], [6])
-        if part == 0:
-            return
-        red(T.bl[:, 8 * i + 4:8 * i + 5], T.jud[:], ["jud"], ["bl%d" % i])
+        src = T.cores[(rank - 1 - (t - 1) % (N - 1)) % N]
+        p = T.lnd[:, 64 * i:64 * i + 64]
+        act(T.gy[:], p, AF.Identity, [], ["gy"], bias=MAGIC, wait=[(T.sem["ga%d" % i], len(topo.engines(src, core)))])
+        act(T.gx[:], T.gy[:], AF.Identity, ["gy"], ["gx"], bias=-MAGIC)
+        mms("hash", "H", [(PH[:, 0:4], m, T.gx[:, a:64:16]) for a, m in enumerate(sel(T.selW))], ["selW0", "selW1", "gx"], 7)
+        ts(T.hi[:], PH[:, 0:4], 77.0 * t, None, OP.add, None, [], ["hi"], [7])
+        ts(T.hi2[:], T.hi[:], W - 1, None, OP.bitwise_and, None, ["hi"], ["hi2"])
+        cp(T.hu[:], T.hi2[:], ["hi2"], ["hu"])
+        cp(T.gcu[:], colw.indirect(T.hu[:]), ["col", "hu"], ["gcu"])
+        mms("gxT_", "gxT", [(PQ[0:64, 256:384], T.gx[:], I)], ["gx", "idb"], 6)
+        mms("m_", "m", [(PQ[:, 384:448], l[:], r) for l, r in ((T.lof, p), (T.nlo, T.gx[:]), (T.hif, p), (T.nhi, T.gx[:]))],
+            ["lof", "gx", "nlo", "hif", "nhi"], 6)
+        act(T.gxT[0:64, :], PQ[0:64, 256:384], AF.Copy, [], ["gxT"], b=[6])
+        act(T.mR[:], PQ[:, 384:448], AF.Copy, [], ["mR"], scale=-8192.0, b=[6])
+
+    def judge(t):
+        i = t - 3
+        for h, (bank, nm) in enumerate(PG):
+            part = slice(512 * h, 512 * h + 512)
+            act(T.G[:, part], Xw.indirect(T.gcu[:, 32 * h:32 * h + 32]), AF.Copy, XK + ["gcu"], ["G%d" % h])
+            mms("sub%d" % h, "sub%d" % h, [(bank[:], T.gxT[0:64, :], T.negE[0:64, part]), (bank[:], I, T.G[:, part])], ["gxT", "negE", "idb", "G%d" % h], nm)
+            act(T.Ag[:, part], bank[:], AF.Abs, [], ["Ag%d" % h], b=[nm])
+        mms("gsum", "gsum", [(PQ[:, 0:64], m, T.Ag[:, 64 * a:64 * a + 64]) for a, m in enumerate(sel(T.selA))], SELA + ["Ag0", "Ag1"], 6)
+        scan(T.Rg[:], T.patg[:], PQ[:, 0:64], OP.add, OP.max, ["patg"], ["Rg"], [6])
+        tt(T.Eg[:], T.Rg[:, 0:64].indirect(T.bcg[:]), T.diag4[:], OP.mult, ["Rg", "bcg", "diag4"], ["Eg"])
+        mms("gspread", "gspread", [(PQ[:, 64:128], T.nblkf[:], T.Eg[:])], ["nblkf", "Eg"], 6)
+        tt(T.jud[:], PQ[:, 64:128], T.mR[:], OP.min, ["mR"], ["jud"], [6])
+        red(T.bl[:, 8 * i + 4:8 * i + 5], T.jud[:], ["jud"], ["bl%d" % i], name="best")
         ids, dsts = [], []
         for d in range(1, N):
             rid, pid, _ = topo.addr(T.cores[(rank + d) % N])
             ids.append(DstId(rid=rid, pnc=pid))
             dsts.append(T.bl[:, 8 * i + d:8 * i + d + 1])
         tr = RemoteDMATransfer(dst_ids=ids, dma_engine_mask=to_all(core), remote_sem=T.sem["gb%d" % i], srcs=[T.bl[:, 8 * i + 4:8 * i + 5]], dsts=dsts)
-        op("G", lambda: g.remote_dma_fused([tr], local_sem=T.sem.sent), ["bl%d" % i])
+        op("G", lambda: g.remote_dma_fused([tr], local_sem=T.sem.sent), ["bl%d" % i], name="tell")
         nsent[0] += bin(to_all(core)).count("1")
 
     def thresholds(t):
         i = t - 3
         n = sum(bin(to_all(s)).count("1") for s in T.cores if s != core)
-        red(T.tiny[:, 0:1], T.bl[:, 8 * i + 1:8 * i + 5], ["bl%d" % i], ["bq"], wait=[(T.sem["gb%d" % i], n)])
-
-    def thresholds_s(t, between=None):
-        bq, y, z, nlim, nl4, limM, nlimM = (T.tiny[:, j:j + 1] for j in range(7))
-        act(y, bq, AF.Relu, ["bq", "nl4"], ["y"], bias=nl4, scale=0.25)
-        if between:
-            between()
-        act(z, y, AF.Identity, ["y"], ["z"], bias=MAGIC)
-        if t < NT - 2:
-            act(nlim, z, AF.Identity, ["z", "nlimM"], ["nlim"], bias=nlimM, scale=-1.0)
-        act(T.limh[:, t:t + 1], z, AF.Identity, ["z", "limM"], ["lim%d" % t], bias=limM)
-        if t < NT - 2:
-            act(T.limoff[:], T.off12[:], AF.Identity, ["off12", "nlim"], ["limoff"], bias=nlim)
-        if t == NT - 2:
-            limits(t)
-
-    def thresholds_v(t):
         lim = T.limh[:, t - 1:t]
-        thresholds(t)
-        ts(T.tiny[:, 1:2], T.tiny[:, 0:1], lim, 0.0, OP.subtract, OP.max, ["bq", "lim%d" % (t - 1)], ["y"])
-        ts(T.tinyi[:, 0:1], T.tiny[:, 1:2], 0.25, -0.375, OP.mult, OP.add, ["y"], ["bi"])
-        tt(T.limh[:, t:t + 1], lim, T.tinyi[:, 0:1], OP.add, ["bi", "lim%d" % (t - 1)], ["lim%d" % t])
+        act(T.tiny[:, 1:2], lim, AF.Identity, ["lim%d" % (t - 1)], ["lim15"], bias=1.5)
+        red(T.tiny[:, 0:1], T.bl[:, 8 * i + 1:8 * i + 5], ["bl%d" % i], ["bq"], wait=[(T.sem["gb%d" % i], n)])
+        ts(T.tinyi[:, 0:1], T.tiny[:, 0:1], T.tiny[:, 1:2], 0.25, OP.subtract, OP.mult, ["bq", "lim15"], ["bi"])
+        ts(T.limh[:, t:t + 1], T.tinyi[:, 0:1], lim, lim, OP.add, OP.max, ["bi", "lim%d" % (t - 1)], ["lim%d" % t], name="lim")
+
+    def least(t):
+        scan(T.Rb[:, 1:193], T.clamp[:], PK[:, 0:192], OP.min, OP.max, ["clamp"], ["Rb"], [0])
+        if t == 0:
+            cp(M, T.Rb[:, 16:193:16], ["Rb"], ["M"])
+        else:
+            tt(M, T.Rb[:, 16:193:16], PM, OP.max, ["Rb"], ["M"], [2])
+
+    def fates(t):
+        s = max(t - 1, 0)
+        lim, nf, NF = T.limh[:, s:s + 1], T.nf[:, 12 * t:12 * t + 12], "nf%d" % t
+        ts(dead, M, lim, 0.0, OP.add, OP.is_gt, ["M", "lim%d" % s], ["dead"])
+        if t >= 2:
+            tt(go, PA, dead, OP.is_gt, ["dead"], ["go"], [2])
+            scan(T.In[:], T.pat24[:], T.Fl[:], OP.mult, OP.add, ["pat24", "dead", "go"], ["In"])
+            mms("Xd", "X", [(PX, nk, dead), (PX, nk, dead)], ["n2k", "dead"], 3)
+            mms("Xg", "X", [(PX, nk, go)], ["n2k", "go"], 3)
+            mms("X", "X", [(PX, I, Ig)], ["idb", "In"], 3)
+            mms("B", "B", [(PP[:, 0:2], T.tri[:], T.In[:, 11:24:12])], ["tri", "In"], 3)
+            ts(T.q[:], Ig, PP[:, 1:2], float(U), OP.add, OP.min, ["In"], ["q"], [3])
+            ts(nf, PX, PP[:, 1:2], U - 2048.0, OP.add, OP.is_gt, [], [NF], [3], name="nf")
+            mms("T", "T", [(PT, I, Id), (PT, I, T.q[:]), (PT, nk, nf)], ["In", "q", NF], 3)
+        else:
+            ts(nf, M, lim, 0.0, OP.add, OP.is_le, ["M", "lim%d" % s], [NF], name="go")
+            scan(Id, T.pat24[:, 0:12], dead, OP.mult, OP.add, ["pat24", "dead"], ["In"])
+            mms("X", "T", [(PT, nk, nf), (PT, I, Id)], ["n2k", NF, "idb", "In"], 3)
+            mms("B", "B", [(PP[:, 0:1], T.tri[:], T.In[:, 11:12])], ["tri", "In"], 3)
+        ts(T.idxu[:], PT, PP[:, 0:1], T.cur[:, t:t + 1], OP.add, OP.add, ["cur%d" % t], ["idxu"], [3])
+        tt(T.keep[:], PK[:, 0:192], T.Rb[:, 0:192], OP.is_le, ["Rb", "Rb0"], ["keep"], [0])
+        scan(T.Kb[:], T.keep[:], PC[:, 64:256], OP.mult, OP.max, ["keep"], ["Kb"], [2])
+        tt(T.vm[:], T.vp[:], nf, OP.mult, ["vp", NF], ["vm"])
+        tt(T.kcnf[:], T.Kb[:, 15:192:16], nf, OP.mult, ["Kb", NF], ["kcnf"])
+        if t >= 2:
+            mms("S", "S", [(PS, p8, dead), (PS, I, T.q[:]), (PS, p8, nf)], ["p8k", "dead", "q", NF], 2)
+            leavers(t)
         if t < NT - 2:
-            ts(T.limoff[:], T.off12[:], T.limh[:, t:t + 1], None, OP.subtract, None, ["off12", "lim%d" % t], ["limoff"])
-
-    def limits(t):
-        lim = T.limh[:, t:t + 1]
-        act(T.tiny[:, 4:5], lim, AF.Identity, ["lim%d" % t], ["nl4"], bias=-0.375, scale=-0.25)
-        act(T.tiny[:, 5:6], lim, AF.Identity, ["lim%d" % t], ["limM"], bias=-MAGIC)
-        if t < NT - 3:
-            act(T.tiny[:, 6:7], lim, AF.Identity, ["lim%d" % t], ["nlimM"], bias=MAGIC, scale=-1.0)
-
-    def gath(c, lo=0, hi=768):
-        tt(T.dif[:, 768 * c + lo:768 * c + hi], Xw.indirect(T.xo[:, 48 * c + lo // 16:48 * c + hi // 16]), T.own4[:, lo:hi], OP.subtract,
-           XK + (["xo0"], ["xo0", "xo"], ["xo"], ["xo"])[c] + ["own4", "own4b"], ["dif%d_%d" % (c, lo > 0)])
-
-    def record(t):
-        if 2 <= t:
-            act(T.ownc[:], Xw.indirect(T.vu[:]), AF.Identity, XK + ["vu"], ["ownc"], bias=-128.0)
+            mms("I", "I", [(PI, T.blkb[:], T.In[:, 11:12])] + [(PI, T.sel15[:], T.q[:, 11:12])] * (t >= 2), ["blkb", "In", "sel15", "q"], 2)
+            act(T.cur[:, t + 1:t + 2], PI, AF.Identity, ["cur%d" % t], ["cur%d" % (t + 1)], bias=T.cur[:, t:t + 1], b=[2], name="cur")
+        mms("PM", "PM", [(PM, I, T.cb[:, 16:28]), (PM, p8, nf), (PM, T.idf[:], M)], ["cb", "p8k", NF, "idf", "M"], 2)
         if 1 <= t < NT - 2:
-            act(T.St[:, 32:48], T.nf3[:, 0:16], AF.Copy, ["nf3"], ["nfp"])
+            mms("PA", "PA", [(PA, I, T.cb[:, 0:12]), (PA, I, T.nf[:, 12 * t - 12:12 * t]), (PA, I, nf)], ["cb", "nf%d" % (t - 1), NF], 2)
 
-    def absol(c, lo=0, hi=768):
-        act(T.A[:, 768 * c + lo:768 * c + hi], T.dif[:, 768 * c + lo:768 * c + hi], AF.Abs, ["dif%d_0" % c], ["A%d_%d" % (c, lo > 0)])
+    def leavers(t):
+        i = t - 2
+        tt(T.slf[:], PS, T.qc[:], OP.min, ["qc"], ["slf"], [2])
+        ts(T.slu[:], T.slf[:], -1.0, None, OP.add, None, ["slf"], ["slu"])
+        tt(T.mE[:], T.M[:, 0:12].indirect(T.bc12[:]), T.diagS[:], OP.mult, ["M", "bc12", "diagS"], ["mE"])
+        tt(T.snd[:, 256 * i:256 * i + 256].indirect(T.slu[:]), T.ownc[:], T.mE[:], OP.add, ["slu", "ownc", "mE"], ["snd%d" % i], name="snd")
+        dst = T.cores[(rank + 1 + t % (N - 1)) % N]
+        rid, pid, _ = topo.addr(dst)
+        mask = topo.mask(core, dst)
+        op("G", lambda: g.remote_dma(T.lnd[:, 64 * i:64 * i + 64], T.snd[:, 256 * i:256 * i + 64], T.sem["ga%d" % i], T.sem.sent, pid, rid, mask),
+           ["snd%d" % i], name="send")
+        nsent[0] += len(topo.engines(core, dst))
 
-    def ksum(c, stop, more=()):
-        for a in range(16):
-            mm(PK[:, c:192:4], T.selA[:, 128 * a:128 * a + 128], T.A[:, 768 * c + a:768 * c + 768:16], False, stop and a == 15,
-               SELA + ["A%d_0" % c, "A%d_1" % c] + list(more), 0)
-
-    def share_g(n):
-        act(T.Gs[:, 0:n], Xw.indirect(T.xo[:, 192 - n // 16:192]), AF.Copy, XK + ["xo"], ["Gs"])
-
-    def share_a(n):
-        for h, (bank, nm) in enumerate(PG):
-            lo, hi = 512 * h, min(n, 512 * h + 512)
-            if lo < hi:
-                mm(bank[:, 0:hi - lo], T.nid[:], T.own4[:, 768 - n + lo:768 - n + hi], True, False, ["nid", "own4", "own4b"], nm)
-                mm(bank[:, 0:hi - lo], T.idb[:], T.Gs[:, lo:hi], False, True, ["idb", "Gs"], nm)
-
-    def share_b(n):
-        for h, (bank, nm) in enumerate(PG):
-            lo, hi = 512 * h, min(n, 512 * h + 512)
-            if lo < hi:
-                act(T.A[:, 3072 - n + lo:3072 - n + hi], bank[:, 0:hi - lo], AF.Abs, [], ["As%d" % h, "A3_1"], b=[nm])
-
-    def ynpart(c, second):
-        lo, hi = YCUT[c:c + 2]
-        if not second:
-            ts(T.yni[:, lo:hi], colw.indirect(T.odu[:, lo // 16:hi // 16]), W - 1, None, OP.bitwise_and, None, ["col", "odu"], ["yni%d" % c])
-            return
-        cp(T.ynf[:, lo:hi], T.yni[:, lo:hi], ["yni%d" % c], ["ynf%d" % c])
-        dma("Y", T.yn[:, lo:hi], T.ynf[:, lo:hi], ["ynf%d" % c], ["out%d" % c])
+    def results():
+        act(T.yvf[:], T.vp[:], AF.Identity, ["vp"], ["yvf"], bias=-4095.0)
+        dma("Y", T.yv[:], T.yvf[:], ["yvf"], ["outv"])
+        for c in range(len(YCUT) - 1):
+            lo, hi = YCUT[c:c + 2]
+            ts(T.yni[:, lo:hi], colw.indirect(T.odu[:, lo // 16:hi // 16]), W - 1, None, OP.bitwise_and, None, ["col", "odu"], ["yn%d" % c])
+            act(T.ynf[:, lo:hi], T.yni[:, lo:hi], AF.Copy, ["yn%d" % c], ["yf%d" % c])
+            dma("Y", T.yn[:, lo:hi], T.ynf[:, lo:hi], ["yf%d" % c], ["out%d" % c])
+        dma("Y", T.yg[:], T.jud[0:128:16, :], ["jud"], ["outg"])
+        act(T.ymf[:], M, AF.Copy, ["M"], ["ymf"], scale=-1.0)
+        dma("Y", T.ym[:], T.ymf[:], ["ymf"], ["outm"])
+        dma("Y", T.yt[:], T.limh[0:128:16, 0:NT], ["lim%d" % t for t in range(NT)], ["outt"])
 
     for t in range(NT):
-        last = t == NT - 1
-        ns = 64 * SHARE[t]
-        pc = (t + 1) // 2
-        if t >= 4 and OPT["ag"]:
-            gdist_s(0)
-        act(T.GB[:], T.odB[:, 0:PIECES[pc][1] + 1].indirect(T.idxu[:]), AF.Copy, ODB[:pc + 2] + ["idxu"], ["GB"])
-        if t >= 3 and OPT["nfs"]:
-            act(T.nf3[:], T.free[:, 0:16].indirect(T.bcp[:, 0:3]), AF.Identity, ["free", "bcp"], ["nf3"], bias=1.0, scale=-1.0)
-        for a in range(16):
-            mm(PH[:, 16:28], T.selA[:, 128 * a:128 * a + 128], T.GB[:, a:192:16], a == 0, a == 15, SELA + ["GB"], 7)
-        if t < 3:
-            ODA.append(t + 1)
-        if t >= 4:
-            if not OPT["ag"]:
-                gdist_s(0)
-            gdist_s(1)
-            gdist_r()
-        act(T.freeR[:], T.GB[:], AF.Sign, ["GB"], ["freeR"])
-        if t >= 5:
-            limits(t - 2)
-        if t in (2, 3):
-            od_c(t)
-        if t >= 3:
-            leavers(t - 1)
-            if OPT["nfs"]:
-                state2()
-            state3()
-        elif t > 0:
-            if t - 1 in LATE:
-                cp(colw.indirect(T.vu[:]), cnat, ["vu", "c"], ["col"])
-            state2()
-        tt(vp, T.S2[:, 0:12], PH[:, 16:28], OP.subtract, ["S2"], ["vp"], [7])
-        tt(T.oi[:], T.kcnf[:], PH[:, 16:28], OP.subtract, ["kcnf"], ["oi"], [7])
-        ts(T.v4u[:], T.St[:, 0:16].indirect(T.bc4[:, 0:3]), -4095.0, None, OP.add, None, ["vp", "bc4"], ["v4u"])
-        ts(T.oi2[:], T.oi[:], W - 1, None, OP.bitwise_and, None, ["oi"], ["oi2"])
-        if t >= 4:
-            judge_a(0)
-        else:
-            ts(T.vu[:], vp, -4095.0, None, OP.add, None, ["vp"], ["vu"])
-        cp(T.ou[:], T.oi2[:], ["oi2"], ["ou"])
-        if t >= 4:
-            judge_a(1)
-        if t in NVB:
-            act(T.nvb[:], T.St[:, 0:16].indirect(T.bc84[:, 0:12]), AF.Identity, ["vp", "bc84"], ["nvb"], bias=2047.0, scale=-1.0)
-        if t > 0:
-            act(T.own4[:], Xw.indirect(T.v4u[:]), AF.Copy, XK + ["v4u"], ["own4", "own4b"])
-        if ODA:
-            od_a(ODA.pop())
-        if t == 0:
-            matrices()
-            od_b(1)
-        tt(cnat, colw.indirect(T.ou[:]), T.freeR[:], OP.add, ["col", "ou", "freeR"], ["c"])
-        if t >= 4:
-            ts(T.vu[:], vp, -4095.0, None, OP.add, None, ["vp"], ["vu"])
-        turn(T.trb[:, 0:192], T.cbuf[:, 16:208], ["c"], ["tr1"])
-        turn(T.trb[:, 192:416], T.cbuf[:, 0:224], ["c", "c0", "c1"], ["tr2"])
-        if t >= 4:
-            judge_b(t - 1, 0)
-        if t in OPT["xo"]:
-            cp(T.xo[:, 0:64], T.trb[:, 0:416].indirect(T.perm1[:, 0:4]), ["tr1", "tr2", "perm"], ["xo0"])
-            cp(T.xo[:, 64:192], T.trb[:, 0:416].indirect(T.perm1[:, 4:12]), ["tr1", "tr2", "perm"], ["xo"])
-        else:
-            cp(T.xo[:], T.trb[:, 0:416].indirect(T.perm1[:]), ["tr1", "tr2", "perm"], ["xo", "xo0"])
-        if t >= 4:
-            judge_b(t - 1, 1)
-        if t not in NVB:
-            act(T.nvb[:], T.St[:, 0:16].indirect(T.bc84[:, 0:12]), AF.Identity, ["vp", "bc84"], ["nvb"], bias=2047.0, scale=-1.0)
-        act(T.cO[:], T.trb[:, 0:416].indirect(T.perm2[:]), AF.Copy, ["tr1", "tr2", "perm2"], ["cO"])
-        act(T.sg[:], T.cO[:], AF.Sign, ["cO"], ["sg"], bias=-4095.5)
-        if 0 < t < NT - 1:
-            share_g(ns)
-        mm(PK[:, 0:192], T.idb[:], T.offc[:], True, False, ["idb", "offc"], 0)
-        mm(PD[:, 0:192], T.idf[:], T.nvb[:], True, False, ["idf", "nvb"], 2)
-        mm(PD[:, 0:192], T.idf[:], T.cO[:], False, False, ["idf", "cO"], 2)
-        mm(PD[:, 0:192], T.n2k[:], T.sg[:], False, True, ["n2k", "sg"], 2)
-        if 0 < t < NT - 1:
-            share_a(ns)
-        if t == 0:
-            late_constants()
-            act(T.own4[:, 384:768], Xw.indirect(T.v4u[:, 24:48]), AF.Copy, XK + ["v4u"], ["own4b"])
-            cp(T.own4[:, 0:384], Xw.indirect(T.v4u[:, 0:24]), XK + ["v4u"], ["own4"])
-        gath(0)
-        if last:
-            act(T.ed[:], PD[:, 0:192], AF.Abs, [], ["ed"], b=[2])
-            act(T.pen[:], T.ed[:], AF.Relu, ["ed"], ["pen"], bias=32.0, scale=-2.0)
-            unpack(t, 0)
-            unpack(t, 1)
-            unpack_p(t)
-            absol(0)
-            unpack2()
-            ksum(0, False)
-            mm(PK[:, 0:192], T.n2k[:], T.pen[:], False, False, ["n2k", "pen"], 0)
-            gath(1)
-            gath(2, 0, 384)
-            absol(1)
-            ksum(1, False)
-            hchain(t)
-            gdist_a(True)
-            gdist_p()
-            gdist_s(0)
-            gdist_s(1)
-            gdist_r()
-            gath(2, 384, 768)
-            gath(3, 0, 768 - ns)
-        else:
-            if t == 0:
-                share_g(ns)
-                share_a(ns)
-            act(T.ed[:], PD[:, 0:192], AF.Abs, [], ["ed"], b=[2])
-            absol(0)
-            mm(PC[:, 0:192], T.idb[:], T.kcon[:], True, False, ["idb", "kcon"], 1)
-            mm(PC[:, 0:192], T.idf[:], T.cO[:], False, True, ["idf", "cO"], 1)
-            ksum(0, False)
-            gath(1)
-            if t >= 3:
-                unpack(t, 0)
-            act(T.pen[:], T.ed[:], AF.Relu, ["ed"], ["pen"], bias=32.0, scale=-2.0)
-            if t < 3 or not OPT["un"]:
-                share_b(ns)
-            n = OPT["vr"][t]
-            if t >= 3 and OPT["un"]:
-                unpack(t, 1)
-                unpack_p(t)
-                share_b(ns)
-            if n < 768:
-                absol(1, n, 768)
-            if t >= 3 and not OPT["un"]:
-                unpack(t, 1)
-                unpack_p(t)
-            mm(PK[:, 0:192], T.n2k[:], T.pen[:], False, False, ["n2k", "pen"], 0)
-            if n:
-                for a in range(16):
-                    mm(PK[:, 1:1 + n // 4:4], T.selA[:, 128 * a:128 * a + 128], T.dif[:, 768 + a:768 + n:16], False, False, SELA + ["dif1_0"], 0)
-            else:
-                ksum(1, False)
-            if t == 0:
-                input_constants(0)
-            half = t in OPT["half"]
-            gath(2, 0, 384 if half else 768)
-            if t >= 3 and OPT["hearly"] == 2:
-                hsum(t)
-            if n:
-                ts(T.A[:, 768:768 + n], T.dif[:, 768:768 + n], -2.0, 0.0, OP.mult, OP.max, ["dif1_0"], ["A1_0"])
-                ksum(1, False)
-            absol(2, 0, 384 if half else 768)
-            if half:
-                gath(2, 384, 768)
-                act(T.A[:, 1920:2304], T.dif[:, 1920:2304], AF.Abs, ["dif2_1"], ["A2_1"])
-            if t >= 3:
-                unpack2()
-            ksum(2, False)
-            if t >= 3 and OPT["hearly"] == 1:
-                hsum(t)
-            if t >= 3 and OPT["hearly"] == 2:
-                hchain(t, t >= 4, 0)
-            m = 768 - ns - OPT["end"][t]
-            if OPT["end"][t]:
-                gath(3, 0, m)
-                absol(3, 0, m)
-                gath(3, m, 768 - ns)
-                act(T.A[:, 2304 + m:3072 - ns], T.dif[:, 2304 + m:3072 - ns], AF.Abs, ["dif3_1"], ["A3_2"])
-            else:
-                gath(3, 0, m)
-                absol(3, 0, m)
-            if t >= 3 and OPT["hearly"] != 2:
-                hchain(t, t >= 4, 0)
-            ksum(3, True, ["As0", "As1", "A3_2"])
-        if t == 0:
-            input_constants(1)
-            od_c(1)
-        if t < 2:
-            od_spread(3 + 2 * t)
-            od_spread(4 + 2 * t)
-        if 3 <= t < NT - 1:
-            hchain(t, t >= 4, 1)
-        if 4 <= t < NT - 1:
-            thresholds_s(t - 1, lambda: record(t))
-        if 3 <= t < NT - 1:
-            gdist_a()
-        if t < 4:
-            record(t)
-        if t in (1, 2):
-            od_b(t + 1)
-        if t < 3:
-            guest_constants(t)
-        if t not in LATE:
-            cp(colw.indirect(T.vu[:]), cnat, ["vu", "c"], ["col"])
-        if THV[0] and t >= 4:
-            thresholds_v(t - 1)
-        if last:
-            if not THV[0]:
-                thresholds(t - 1)
-            ynpart(0, 0)
-            ts(T.yvf[:], vp, -4095.0, None, OP.add, None, ["vp"], ["yvf"])
-            dma("Y", T.yv[:], T.yvf[:], ["yvf"], ["outv"])
-            ynpart(0, 1)
-            judge_a()
-            share_g(ns)
-            share_a(ns)
-            act(T.A[:, 1536:2304], T.dif[:, 1536:2304], AF.Abs, ["dif2_0", "dif2_1"], ["A2_0", "A2_1"])
-            ksum(2, False)
-            if ns:
-                share_b(ns)
-            if ns < 768:
-                absol(3, 0, 768 - ns)
-            ksum(3, True, ["As0", "As1"])
-            if not THV[0]:
-                thresholds_s(t - 1)
-            ynpart(1, 0)
-            judge_b(t, 0)
-            dma("Y", T.yg[:], T.jud[0:128:16, :], ["jud"], ["outg"])
-            if OPT["yb"]:
-                ynpart(1, 1)
-            judge_b(t, 1)
-            if not OPT["yb"]:
-                ynpart(1, 1)
-            ynpart(2, 0)
-        scan(T.Rb[:, 1:193], T.clamp[:], PK[:, 0:192], OP.max, OP.max, ["clamp"], ["Rb"], [0])
-        if last:
-            ynpart(2, 1)
-        tt(M, T.S2[:, 16:28], T.Rb[:, 16:193:16], OP.max, ["S2", "Rb"], ["M"])
-        if last:
-            tt(T.ymf[:], T.off12[:], M, OP.subtract, ["off12", "M"], ["ymf"])
-            dma("Y", T.ym[:], T.ymf[:], ["ymf"], ["outm"])
-            thresholds(t)
-            lim = T.limh[:, t - 1:t]
-            ts(T.tinyi[:, 0:1], T.tiny[:, 0:1], 0.25, T.tiny[:, 4:5], OP.mult, OP.add, ["bq", "nl4"], ["bi"])
-            ts(T.limh[:, t:t + 1], T.tinyi[:, 0:1], lim, lim, OP.add, OP.max, ["bi", "lim%d" % (t - 1)], ["lim%d" % t])
-            dma("Y", T.yt[:], T.limh[0:128:16, 0:NT], ["lim2", "lim3", "lim4", "lim5", "lim6"], ["outt"])
-            break
-        tt(T.keep[:], PK[:, 0:192], T.Rb[:, 0:192], OP.is_le, ["Rb", "Rb0"], ["keep"], [0])
-        tt(dead, M, T.limoff[:], OP.is_gt, ["M", "limoff"], ["dead"])
-        if t >= 2:
-            tt(T.mt[:, 0:12], T.off12[:], M, OP.subtract, ["off12", "M"], ["mt"])
-            tt(go, T.S2[:, 32:44], dead, OP.is_gt, ["S2", "dead"], ["go"])
-            scan(T.Kb[:], T.keep[:], PC[:, 0:192], OP.mult, OP.max, ["keep"], ["Kb"], [1])
-        scan(T.In[:], T.pat24[:], T.Fl[:], OP.mult, OP.add, ["pat24", "dead", "go"], ["In"])
-        mm(PP[:, 0:2], T.tri[:], T.In[:, 11:24:12], True, True, ["tri", "In"], 3)
-        if t >= 3:
-            gdist_p()
-        if t >= 2:
-            tt(T.mE[:], T.mt[:, 0:16].indirect(T.bc84[:, 0:12]), T.diagS[:], OP.mult, ["mt", "bc84", "diagS"], ["mE"])
-        else:
-            scan(T.Kb[:], T.keep[:], PC[:, 0:192], OP.mult, OP.max, ["keep"], ["Kb"], [1])
-        bd, bg = PP[:, 0:1], PP[:, 1:2]
-        cur = T.cur0[:, 0:1] if t == 0 else PP[:, 8 + t:9 + t]
-        if t >= 2:
-            ts(T.Cl[:], Ig, bg, float(U), OP.add, OP.min, ["In"], ["Cl"], [3])
-            ts(T.lv[:], Ig, bg, float(U), OP.add, OP.is_le, ["In"], ["lv"], [3])
-            tt(T.t1[:], T.Cl[:], Id, OP.add, ["Cl", "In"], ["t1"])
-            tt(T.leave[:], T.lv[:], go, OP.mult, ["lv", "go"], ["leave"])
-            ts(T.t2[:], T.t1[:], bd, cur, OP.add, OP.add, ["t1", "cur0"], ["t2"], [3])
-            tt(T.free[:, 0:12], T.leave[:], dead, OP.add, ["leave", "dead"], ["free"])
-            tt(T.u1[:], T.Cl[:], T.qc[:], OP.subtract, ["Cl", "qc"], ["u1"])
-            tt(T.idxf[:], T.t2[:], T.free[:, 0:12], OP.mult, ["t2", "free"], ["idxf"])
-            tt(T.u2[:], T.u1[:], T.leave[:], OP.mult, ["u1", "leave"], ["u2"])
-        else:
-            ts(T.t2[:], Id, bd, cur, OP.add, OP.add, ["In", "cur0"], ["t2"], [3])
-            ts(T.nf3[:], T.Fl[:, 0:16].indirect(T.bcp[:, 0:3]), -1.0, 1.0, OP.mult, OP.add, ["dead", "go", "bcp"], ["nf3"])
-            tt(T.idxf[:], T.t2[:], dead, OP.mult, ["t2", "dead"], ["idxf"])
-            state3()
-        cp(T.idxu[:], T.idxf[:], ["idxf"], ["idxu"])
-        if t < NT - 2:
-            mm(PP[:, 9 + t:10 + t], T.sel15[:], T.t2[:, 11:12], True, True, ["sel15", "t2"], 3)
+        step[0] = t
+        for part in [refill, penalty, distances, least] + [fates] * (t < NT - 1) + [arrive, judge, thresholds] * (t >= 3):
+            part(t)
+    results()
 
-    op("G", None, ["out0", "out1", "out2", "outv", "outg", "outm", "outt"], wait=[(T.sem.sent, nsent[0])])
-    _emit(g, T, ops)
+    step[0] = "end"
+    op("G", None, ["out0", "out1", "out2", "outv", "outg", "outm", "outt"], wait=[(T.sem.sent, nsent[0])], name="end")
+    _emit(g, T, _sequence(setup, calls))

from concourse.bass import DstId, RemoteDMATransfer
from concourse.mybir import AluOpType as OP, AxisListType, ActivationFunctionType as AF

W, L, U, NT, Q = 4096, 192, 64, 7, 1344
F32, BF, I32, U16 = "float32", "bfloat16", "int32", "uint16"
MAGIC = 12582912.0
SHARE = [7, 7, 7, 4, 4, 4, 8]
RELU = [256, 256, 256, 256, 256, 256, 0]
CUT = [(384, 640)] * 6 + [(768, 768)]
YCUT = [0, 512, 960, 1344]

R0 = '+odB2 +qc +odu GB V oi vp and ou c tr1 tr2 nvb vu Dv +wtf xo1 own0 own1 zero own2 cO sg +thf +th_ xo0 Dc Gown Gs ed +p3 tag +bcg pen g0 Gsub g1 Kp a0 r1 g2 relu a1 k0 As a2 g3 g4 k1 g5 a3 +lim0 a4 col k3 a5 +p8k k2'
R1 = '+nhi -Rb -M +selW1 -dead -go -In -X -vm -B +nlo -idxu +nblkf -keep GB -I -Kb Vm V -kcnf +selW0 +diagS oi vu and own0 ou own1 c vp +diag4 tr2 own2 nvb tr1 -PM xo0 Gown Dv xo1 g0 cO -PA g1 sg g2 relu Gs Dc ed pen -cur zero a0 Gsub Kp a1 g3 r1 a2 As k0 g4 k1 g5 a3 k3 a4 a5 k2 col tag'
R3 = '-Rb -M -sub1 -lim15 -dead -go -Ag0 -Xg -keep -In -mE -Xd -X -B -nf -q -Ag1 -T -vm -Kb -S -idxu -slf GB -kcnf -slu -gsum Vm V -snd -Rg -I oi vu and -Eg ou own0 -gspread -PM c -jud vp own1 tr1 tr2 -best -send xo0 -PA nvb Dv xo1 own2 cO sg g0 Gs Dc Gsub a0 zero -tell gy gx g2 Gown k0 hash -bq g1 gxT_ g3 ed hi r1 g4 hi2 As g5 a2 a1 pen -cur relu m_ hu a3 gcu a4 -bi k3 a5 k1 col Kp gxT G0 G1 k2 sub0 mR -lim tag'
R6 = '-sub1 -Rb -M -dead -go -Xd -keep -In -mE -cur -Xg -X -B -q -nf -PA -T -Ag0 -Kb -vm -idxu -S -Ag1 -slf -slu -kcnf GB -gsum -snd Vm V -I -Rg -send oi vu own0 and -Eg ou zero -gspread c -jud vp own1 nvb tr1 tr2 -PM own2 xo0 yvf Dv gy gx cO g0 hash -lim15 hi xo1 sg a0 hi2 -best gxT_ Dc hu m_ gcu ed g1 G0 gxT col k0 sub0 G1 g2 sub1 mR yn0 g3 Ag0 outv pen Ag1 gsum Rg a1 Gs -tell a3 k1 -bq yf0 Eg gspread -bi jud best outg tell yn1 Gsub out0 a2 As -lim Kp yn2 k2 bq yf1 k3 out1 lim15 Rb bi M yf2 ymf out2 lim outt outm'
SHARE, RELU = [8, 8, 8, 6, 6, 6, 8], [512] * 6 + [0]
R0 = 'zero +odB2 ownc GB +qc V oi vu and ou vp c tr2 v4u +odu nvb tr1 +wtf Dv +p3 own cO Gown sg xo1 Dc xo0 Gs +thf ed pen Gsub g0 a0 tag g1 g2 a1 Kp As relu g3 a2 +th_ a3 r1 g4 a4 g5 +lim0 a5 k0 k1 k3 +bcg col +p8k k2'
R1 = '-Rb +nblkf -M +nlo -dead -go -In -X -B -idxu -vm -keep +selW1 +nhi -Kb +diag4 -I Vm +diagS -kcnf GB +selW0 V oi vp -PM and -PA v4u nvb ou c own tr1 tr2 Dv Gown vu cO xo0 sg xo1 Gs Dc -cur ed pen g0 g1 zero g2 a0 relu g3 a1 Gsub tag a2 Kp r1 g4 k0 k1 As a3 g5 a4 k3 a5 col ownc k2'
R3 = '-Rb -sub1 -M -dead -go -keep -Xd -In -mE -Ag0 -Xg -lim15 -Ag1 -X -B -nf -q -T -S -vm -Kb -idxu -slf -slu Vm GB -kcnf -gsum V -snd -Rg vp oi -I v4u and -Eg own -PM ou vu c -PA -gspread -jud tr2 Gown nvb tr1 -best cO Dv xo0 xo1 g0 -cur zero g2 Gs -send Gsub sg Dc a0 ed g1 gy gx -tell g3 k0 pen As gxT_ hash a2 hi m_ Kp r1 g5 g4 a1 hi2 relu hu a5 -bq k3 a3 gcu gxT k1 mR -bi a4 k2 tag -lim G0 col G1 ownc sub0'
R6 = '-PA -Rb -Ag0 -M -sub1 -dead -Ag1 -go -Xg -keep -In -Xd -mE -X -B -cur -q -nf -Kb -T -S -vm -gsum -idxu -slf -slu GB -kcnf Vm -snd -Rg V vp oi v4u -send and zero yvf -Eg nvb ou c -gspread -PM -jud Dv tr2 tr1 own vu gy xo0 g0 gx hash cO hi xo1 sg gxT_ Dc hi2 -lim15 a0 m_ hu gcu ed G0 gxT k0 -best g1 sub0 G1 sub1 mR col pen g3 -tell outv -bq Ag0 Ag1 g2 a1 a2 gsum yn0 k1 Rg Gs Eg gspread Kp jud best yn1 a3 -I yf0 -bi out0 yn2 tell Gsub As yf1 outg -lim bq out1 k2 lim15 k3 Rb yf2 bi M ymf out2 lim outt ownc outm'
R0 = 'GB zero V +odu vp oi +odB2 nvb v4u Cv and +qc ou Dv c tr2 tr1 +thf own Gown +th_ cO +wtf xo0 vu +p3 xo1 sg Gs g0 Dc g1 g2 Cc ed pen Gsub a0 a1 Kp relu g3 As a2 a3 r1 g4 g5 a4 +bcg k0 k1 k3 a5 +p8k col k2 +lim0'
R1 = '-Rb -M -dead +selW1 -go -In +nblkf -X +nhi -B -vm -idxu GB -keep Vm V +diag4 -Kb -kcnf zero +diagS oi -I vp and +selW0 v4u ou +nlo c nvb Dv own -PM -PA tr2 tr1 Gown cO -cur Cc sg vu xo0 xo1 Dc Gs g0 Cv ed pen g1 g2 a0 a1 Gsub relu g3 a2 g4 As g5 Kp r1 a3 a4 a5 k0 k1 k3 k2 col ownc'
R3 = '-sub1 -Rb -M -dead -go -In -Xg -Ag0 -Ag1 -Xd -X -B -mE -nf -q -vm -T -S -gsum -keep Vm -idxu -Kb GB V -slf -lim15 -kcnf -slu -I -Rg -snd vp oi v4u own and -Eg -gspread ou -PM nvb c -PA zero -jud tr1 -send -cur tr2 -best cO Gown Dv xo0 xo1 g0 vu Cc Cv g5 Gs sg a0 a5 Gsub g3 g2 gy g1 Dc -tell gx k0 ed hash gxT_ As hi m_ a2 g4 hi2 relu a3 k3 pen hu a1 a4 -bq gxT mR gcu r1 k1 col Kp -bi G0 -lim k2 G1 ownc sub0'
R6 = '-sub1 -Ag0 -Rb -M -Ag1 -dead -Xd -go -In -X -keep -Xg -B -Kb -nf -q -vm -T -mE -S -idxu -gsum -slf -kcnf -slu Vm GB V -snd -Rg oi vp -send and v4u ou -Eg c nvb -gspread tr1 zero own tr2 -PM xo0 -jud gy vu Dv g0 -lim15 gx cO hash sg hi yvf Dc -best gxT_ a0 hi2 hu xo1 m_ ed gcu G0 g3 gxT outv G1 k0 pen mR col sub0 Ag0 sub1 g1 Ag1 gsum a1 g2 -tell k1 yn0 Rg Eg gspread Kp jud Gs a3 -bq best a2 -bi yn1 yf0 -lim out0 yn2 Gsub k2 As outg yf1 yf2 k3 lim15 out1 out2 tell bq Rb bi M lim outt ymf outm'
ROUNDS = [R0, R1, R1, R3, R3, R3, R6]


def _sb(n, dt):
    return ("sbuf", [128, n], dt)


SCRATCH = {
    "X": _sb(4112, BF), "col": _sb(W, I32), "odi": _sb(272, I32), "odu": _sb(84, U16), "Zi": _sb(96, I32), "nib": _sb(252, I32),
    "odT": _sb(Q, BF), "odB": _sb(Q + 16, BF), "wti": _sb(4, I32), "thi": _sb(4, I32),
    "pi": _sb(8, I32), "pf": _sb(32, F32), "j16": _sb(192, F32), "ia": _sb(128, F32), "ib": _sb(128, F32), "ic": _sb(128, F32),
    "lf": _sb(96, F32), "diagS": _sb(192, F32), "diag4": _sb(64, F32), "clamp": _sb(192, F32), "kf": _sb(192, F32),
    "patg": _sb(64, F32), "pat24": _sb(24, F32), "zero": _sb(192, BF), "kcon": _sb(192, BF), "qc": _sb(12, F32), "cb": _sb(32, BF),
    "blkf": _sb(128, F32), "nblkf": _sb(128, F32), "blkb": _sb(128, BF), "lof": _sb(128, F32), "hif": _sb(128, F32),
    "nlo": _sb(128, BF), "nhi": _sb(128, BF), "tri": _sb(128, BF), "sel15": _sb(128, BF),
    "idf": _sb(128, F32), "idb": _sb(128, BF), "nid": _sb(128, BF), "n2k": _sb(128, BF), "p8k": _sb(128, BF),
    "selA": _sb(2048, BF), "selW": _sb(2048, BF), "selO": _sb(2048, BF), "negE": _sb(1024, BF),
    "bc12": _sb(12, U16), "bcg": _sb(4, U16), "perm1": _sb(12, U16), "perm2": _sb(12, U16), "zl": _sb(8, U16),
    "vp": _sb(12, F32), "vm": _sb(12, F32), "M": _sb(12, F32), "kcnf": _sb(12, F32), "nf": _sb(96, BF), "q": _sb(12, BF), "cur": _sb(8, F32),
    "idxu": _sb(12, U16), "GBb": _sb(192, BF), "oi": _sb(12, I32), "oi2": _sb(12, I32), "ou": _sb(12, U16), "vu": _sb(12, U16),
    "cbuf": _sb(224, F32), "trb": _sb(416, F32), "xo": _sb(192, U16),
    "own4": _sb(768, BF), "v4u": _sb(48, U16), "bc4": _sb(4, U16), "dif": _sb(3072, BF), "A": _sb(3072, BF), "Gs": _sb(512, BF),
    "nvb": _sb(192, F32), "cO": _sb(192, F32), "sg": _sb(192, BF), "ed": _sb(192, F32), "pen": _sb(192, BF),
    "Rb": _sb(200, F32), "keep": _sb(192, F32), "Kb": _sb(192, F32), "Fl": _sb(24, BF), "In": _sb(24, BF),
    "limh": _sb(8, F32), "tiny": _sb(8, F32), "tinyi": _sb(4, I32),
    "slf": _sb(12, F32), "slu": _sb(12, U16), "mE": _sb(192, F32), "ownc": _sb(192, F32),
    "snd": _sb(4 * 256, F32), "lnd": _sb(4 * 64, F32), "gy": _sb(64, F32), "gx": _sb(64, BF), "gxT": _sb(128, BF),
    "mR": _sb(64, F32), "hi": _sb(4, I32), "hi2": _sb(4, I32), "hu": _sb(4, U16), "gcu": _sb(64, U16), "G": _sb(1024, BF), "Ag": _sb(1024, BF),
    "Rg": _sb(64, F32), "Eg": _sb(64, F32), "jud": _sb(64, F32), "bl": _sb(32, F32),
    "yni": _sb(Q, I32), "ynf": _sb(Q, F32), "yvf": _sb(12, F32), "ymf": _sb(12, F32),
}
for _b in range(8):
    SCRATCH["ps%d" % _b] = ("psum", [128, 512], F32)

NDMA = 17
SEMAPHORES = ["cV", "cS", "cP", "cG", "sent"] + ["d%d" % i for i in range(NDMA)] + ["ga%d" % i for i in range(4)] + ["gb%d" % i for i in range(4)]


def _sequence(setup, calls):
    ops, left = list(setup), dict(calls)
    for t in range(NT):
        for name in ROUNDS[t].split():
            ops += left.pop({"-": (name[1:], t - 1), "+": (name[1:], "late")}.get(name[0], (name, t)), [])
    ops += left.pop(("end", "end"))
    assert not left, sorted(left, key=str)
    return ops


def _emit(g, T, ops):
    queue = {"V": g.vector, "S": g.scalar, "P": g.tensor, "G": g, "Y": g.sync}
    writer, readers, banks = {}, {}, {}
    known = {e: {} for e in queue}
    for n, o in enumerate(ops):
        e = o["e"]
        deps = set(writer[k] for k in o["r"] + o["w"] if k in writer)
        for k in o["w"]:
            deps.update(readers.get(k, []))
        for b in o["b"]:
            deps.update(m for f, m in banks.setdefault(b, {}).items() if f != e)
            banks[b][e] = n
        o["need"] = []
        for m in sorted(deps, reverse=True):
            key = ("dma", m) if ops[m]["dma"] is not None else ops[m]["e"]
            if known[e].get(key, -1) >= m:
                continue
            o["need"].append(m)
            ops[m]["inc"] = True
            for kk, vv in ops[m]["clock"].items():
                known[e][kk] = max(known[e].get(kk, -1), vv)
            known[e][key] = m
        o["clock"] = dict(known[e])
        for k in o["r"]:
            readers.setdefault(k, []).append(n)
        for k in o["w"]:
            writer[k] = n
            readers[k] = []
    count = {e: 0 for e in queue}
    first = {o["sum"]: n for n, o in reversed(list(enumerate(ops))) if o["e"] == "P"}
    last = {o["sum"]: n for n, o in enumerate(ops) if o["e"] == "P"}
    for n, o in enumerate(ops):
        q = queue[o["e"]]
        for m in o["need"]:
            q.wait_ge(*ops[m]["done"])
        for s, v in o["wait"]:
            q.wait_ge(s, v)
        if o["f"] is None:
            continue
        ins = o["f"](first[o["sum"]] == n, last[o["sum"]] == n) if o["e"] == "P" else o["f"]()
        if o["dma"] is not None:
            o["done"] = (T.sem["d%d" % o["dma"]], 16)
            ins.then_inc(*o["done"])
        elif o["inc"]:
            count[o["e"]] += 1
            o["done"] = (T.sem["c" + o["e"]], count[o["e"]])
            ins.then_inc(o["done"][0], 1)


def rank_program(g, core, T, topo):
    rank = T.rank_of(core)
    if rank is None:
        return
    N = len(T.cores)
    setup, calls, step = [], {}, [None]
    ndma = [0]
    V, S, PE = g.vector, g.scalar, g.tensor

    def op(e, f, r=(), w=(), b=(), wait=(), dma=None, name=None, total=None):
        o = {"e": e, "f": f, "r": list(r), "w": list(w), "b": list(b), "wait": list(wait), "dma": dma, "inc": False, "sum": total}
        if step[0] is None:
            setup.append(o)
        else:
            calls.setdefault((name or w[0], step[0]), []).append(o)

    def dma(e, out, in_, r, w):
        q = g.sync if e == "Y" else g.scalar
        op(e, lambda: q.dma_start(out, in_), r, w, dma=ndma[0])
        ndma[0] += 1

    def tt(out, a, b_, o, r, w, b=(), name=None):
        op("V", lambda: V.tensor_tensor(out, a, b_, o), r, w, b, name=name)

    def ts(out, a, s1, s2, o0, o1, r, w, b=(), name=None):
        if o1 is None:
            op("V", lambda: V.tensor_scalar(out, a, s1, None, o0), r, w, b, name=name)
        else:
            op("V", lambda: V.tensor_scalar(out, a, s1, s2, o0, o1), r, w, b, name=name)

    def cp(out, a, r, w, b=()):
        op("V", lambda: V.tensor_copy(out, a), r, w, b)

    def turn(out, a, r, w):
        op("V", lambda: V.transpose(out, a), r, w)

    def ms(out, c, w):
        op("V", lambda: V.memset(out, c), (), w)

    def scan(out, d0, d1, o0, o1, r, w, b=()):
        op("V", lambda: V.tensor_tensor_scan(out, d0, d1, 0.0, o0, o1), r, w, b)

    def red(out, a, r, w, o=OP.max, wait=(), name=None):
        op("V", lambda: V.tensor_reduce(out, a, AxisListType.X, o), r, w, wait=wait, name=name)

    def act(out, a, fn, r, w, bias=0.0, scale=1.0, b=(), wait=(), name=None):
        op("S", lambda: S.activation(out, a, fn, bias=bias, scale=scale), r, w, b, wait, name=name)

    def mms(name, total, terms, r, b, go_on=False):
        def f(first, last):
            for i, (out, lhsT, rhs) in enumerate(terms):
                ins = PE.matmul(out, lhsT, rhs, first and i == 0 and not go_on, last and i == len(terms) - 1)
            return ins
        op("P", f, r, (), [b], name=name, total=(total, step[0]))

    def iota(out, pat, base, cm, w, small=True):
        if small:
            op("G", lambda: g.iota(out, pat, base, cm, allow_small_or_imprecise_dtypes=True), (), w)
        else:
            op("G", lambda: g.iota(out, pat, base, cm), (), w)

    def pick(out, a, pat, o, base, cm, r, w, fill=0.0, name=None):
        op("G", lambda: g.affine_select(out, a, pat, o, fill, base, cm), r, w, name=name)

    PK, PD, PC, PP, PG0, PG1, PQ, PH = [T["ps%d" % i] for i in range(8)]
    PG = ((PG0, 4), (PG1, 5))
    Xw = T.X[:, 0:4112]
    colw = T.col[:, 0:W]
    pf = lambda i: T.pf[:, i:i + 1]

    def sel(m, lo=0, hi=16):
        return [m[:, 128 * a:128 * a + 128] for a in range(lo, hi)]

    dma("Y", T.odi[:, 0:84], T.od[:], [], ["odi"])
    dma("Y", T.odi[0:112, 84:168], T.od[16:128, :], [], ["odU"])
    dma("Y", T.odi[16:128, 168:252], T.od[0:112, :], [], ["odD"])
    dma("S", T.odi[112:128, 84:168], T.od[0:16, :], [], ["odU2"])
    dma("S", T.odi[0:16, 168:252], T.od[112:128, :], [], ["odD2"])
    dma("Y", T.col[:], T.nb[:], [], ["col"])
    dma("Y", T.X[:, 0:W], T.xs[:], [], ["Xa"])
    ms(T.thi[:], 0, ["thi"])
    ms(T.odi[:, 252:272], 0, ["odP"])
    ms(T.selA[:], 0.0, ["selA0"])
    dma("S", T.X[:, W:W + 16], T.xs[:, 0:16], [], ["Xb"])
    dma("S", T.wti[:, 0:1], T.wt[:], [], ["wti"])
    dma("S", T.thi[0:128:16, 0:1], T.th[:], [], ["thi"])
    XK = ["Xa", "Xb"]

    pm = pf(0)
    iota(T.pi[:, 0:1], [[0, 1]], 0, 1, ["pi0"], False)
    iota(T.ia[:], [[-16, 8], [0, 16]], 0, 1, ["ia"])
    iota(T.lf[:, 24:36], [[16, 12]], 0, 0, ["lf2"])
    iota(T.lf[:, 0:12], [[1, 12]], 0, 0, ["lf0"])
    iota(T.idf[:], [[1, 128]], 0, -1, ["idf0"])
    iota(T.lf[:, 12:24], [[1, 4], [64, 3]], 0, 0, ["lf1"])
    iota(T.lf[:, 36:48], [[0, 6], [1, 2]], 0, 0, ["lf3"])
    iota(T.cbuf[:, 0:16], [[0, 16]], 0, 0, ["c0"])
    iota(T.cbuf[:, 208:224], [[0, 16]], 0, 0, ["c1"])
    iota(T.zero[:], [[0, 192]], 0, 0, ["zero"])
    iota(T.kf[:], [[16, 12], [-1, 16]], 16, 0, ["kf"])
    iota(T.clamp[:], [[0, 192]], -4095, 0, ["clamp0"])
    iota(T.Rb[:, 0:1], [[0, 1]], 0, 0, ["Rb0"])
    pick(T.clamp[:], T.clamp[:], [[0, 12], [1, 16]], OP.is_equal, 0, 0, ["clamp0"], ["clamp0", "clamp"], 65536.0)
    ts(T.ib[:], T.ia[:], 0.0, None, OP.is_ge, None, ["ia"], ["ib"])
    ts(T.ic[:], T.ia[:], 15.0, None, OP.is_le, None, ["ia"], ["ic"])
    ts(T.pi[:, 1:2], T.pi[:, 0:1], 15, None, OP.bitwise_and, None, ["pi0"], ["pi1"])
    tt(T.blkf[:], T.ib[:], T.ic[:], OP.mult, ["ib", "ic"], ["blkf"])
    ts(T.pi[:, 2:3], T.pi[:, 0:1], 2, 3, OP.arith_shift_right, OP.bitwise_and, ["pi0"], ["pi2"])
    ts(T.pi[:, 3:4], T.pi[:, 0:1], 3, None, OP.bitwise_and, None, ["pi0"], ["pi3"])
    ts(T.pi[:, 4:5], T.pi[:, 0:1], 4, 1, OP.arith_shift_right, OP.bitwise_and, ["pi0"], ["pi4"])
    ts(T.pi[:, 5:6], T.pi[:, 0:1], 2, 1, OP.arith_shift_right, OP.bitwise_and, ["pi0"], ["pi5"])
    ts(T.pi[:, 6:7], T.pi[:, 0:1], 1, None, OP.bitwise_and, None, ["pi0"], ["pi6"])
    cp(pm, T.pi[:, 1:2], ["pi1"], ["pm"])
    for a in range(16):
        ts(T.selA[:, 129 * a:128 * a + 128:16], T.blkf[:, 0:128:16], -1.0, None, OP.mult, None, ["blkf", "selA0"], ["selA%d" % (a + 1)])
        if a == 0:
            cp(T.pf[:, 8:13], T.pi[:, 2:7], ["pi2", "pi3", "pi4", "pi5", "pi6"], ["p8"])
            for i, wgt in enumerate((64.0, 1024.0, 16384.0, -13312.0, -65.0)):
                ts(pf(16 + i), pm, float(i), -wgt, OP.is_equal, OP.mult, ["pm"], ["ow%d" % i])
        if a == 1:
            red(pf(1), T.pf[:, 16:21], ["ow%d" % i for i in range(5)], ["ow"], OP.add)
        if a % 8 == 7:
            h = a // 8
            act(T.selO[:, 1024 * h:1024 * h + 1024], T.selA[:, 1024 * h:1024 * h + 1024], AF.Copy,
                ["selA%d" % i for i in range(a + 2)] + ["ow"], ["selO%d" % h], scale=pf(1))
    SELA = ["selA%d" % i for i in range(17)]

    tt(pf(13), pf(12), pf(10), OP.not_equal, ["p8"], ["p13"])
    ts(pf(14), pf(10), 86.0, 83.0, OP.mult, OP.add, ["p8"], ["p14"])
    ts(T.idf[:], T.idf[:], 0.0, None, OP.is_equal, None, ["idf0"], ["idf"])
    ts(pf(15), pf(13), pf(14), pm, OP.mult, OP.add, ["p13", "p14", "pm"], ["p15"])
    ms(T.odB[:, 0:16], 0.0, ["odB0"])
    ts(T.zl[:, 0:6], T.lf[:, 24:30], pf(15), None, OP.add, None, ["lf2", "p15"], ["zl"])
    ms(T.odT[:], 1.0, ["odT"])
    cp(T.Zi[:], T.odi[:, 0:272].indirect(T.zl[:, 0:6]), ["odi", "odU", "odD", "odU2", "odD2", "odP", "zl"], ["Zi"])
    ts(pf(5), pm, 12.0, 16.0, OP.mult, OP.add, ["pm"], ["p5"])
    for i in range(3):
        ts(T.nib[:, 84 * i:84 * i + 84], T.Zi[:, 0:84], 4 * i, 15, OP.arith_shift_right, OP.bitwise_and, ["Zi"], ["nib%d" % i])
    for i in range(3):
        ts(T.odT[:, i:Q:16], T.nib[:, 84 * i:84 * i + 84], 1.0 / 64, 1.0, OP.mult, OP.add, ["nib%d" % i, "odT"], ["odT%d" % i])
    ts(T.idxu[:], T.lf[:, 0:12], pf(5), None, OP.add, None, ["lf0", "p5"], ["idxu"])
    turn(T.odB[:, 16:208], T.odT[:, 0:192], ["odT0", "odT1", "odT2"], ["odB1"])
    for name, src, f in (("idb", "idf", 1.0), ("n2k", "idf", -2048.0), ("nid", "idf", -1.0), ("blkb", "blkf", 1.0), ("kcon", "kf", 8192.0)):
        act(T[name][:], T[src][:], AF.Copy, [src], [name], scale=f)

    tt(pf(6), pf(10), pf(11), OP.not_equal, ["p8"], ["p6"])
    ts(pf(7), pf(8), 16.0, None, OP.mult, None, ["p8"], ["p7"])
    ts(T.lf[:, 52:64], T.lf[:, 36:48], pf(10), 208.0, OP.not_equal, OP.mult, ["lf3", "p8"], ["lf5"])
    ts(pf(2), pf(9), 4.0, pf(7), OP.mult, OP.add, ["p8", "p7"], ["p2"])
    tt(T.lf[:, 64:76], T.lf[:, 52:64], T.lf[:, 24:36], OP.add, ["lf5", "lf2"], ["lf6"])
    ts(pf(4), pf(6), 208.0, pf(2), OP.mult, OP.add, ["p6", "p2"], ["p4"])
    ts(T.perm2[:], T.lf[:, 64:76], pm, None, OP.add, None, ["lf6", "pm"], ["perm2"])
    ts(T.perm1[:], T.lf[:, 12:24], pf(4), None, OP.add, None, ["lf1", "p4"], ["perm"])
    cp(T.bc12[:], T.lf[:, 0:12], ["lf0"], ["bc12"])
    ts(T.bc4[:, 0:3], T.lf[:, 0:12:4], pf(8), None, OP.add, None, ["lf0", "p8"], ["bc4"])
    iota(T.cur[:, 0:1], [[0, 1]], L + 15, 0, ["cur0"])
    iota(T.pat24[:], [[0, 24]], 1, 0, ["pat24"])
    iota(T.cb[:], [[-8191, 2], [0, 16]], -1, 0, ["cb"])
    iota(T.pat24[:, 12:13], [[0, 1]], 0, 0, ["pat24"])
    pick(T.tri[:], T.blkb[:], [[1, 128]], OP.is_gt, 0, -1, ["blkb"], ["tri"])
    iota(T.j16[:], [[0, 12], [1, 16]], 0, 0, ["j16"])
    iota(T.diag4[:], [[1, 16], [0, 4]], 0, 0, ["diag4a"])
    pick(T.sel15[:], T.blkb[:], [[-16, 8], [0, 16]], OP.is_equal, -15, 1, ["blkb"], ["sel15"])
    pick(T.lof[:], T.blkf[:], [[16, 8], [0, 16]], OP.is_ge, 7, -1, ["blkf"], ["lof"])
    pick(T.hif[:], T.blkf[:], [[-16, 8], [0, 16]], OP.is_ge, -8, 1, ["blkf"], ["hif"])
    iota(T.patg[:], [[0, 64]], -65536, 0, ["patg"])
    iota(T.negE[:], [[0, 1024]], -1, 0, ["negE"])
    pick(T.patg[:], T.patg[:], [[0, 4], [1, 16]], OP.is_equal, 0, 0, ["patg"], ["patg"])
    pick(T.negE[:], T.negE[:], [[1, 64], [0, 16]], OP.is_equal, 0, -1, ["negE"], ["negE"])
    iota(T.snd[:], [[0, 1024]], 0, 0, ["snd0", "snd1", "snd2", "snd3"])

    step[0] = "late"
    turn(T.odB[:, 208:Q + 16], T.odT[:, 192:Q], ["odT0", "odT1", "odT2"], ["odB2"])
    cp(pf(22), T.thi[:, 0:1], ["thi"], ["thf"])
    mms("th_", "th", [(PP[:, 100:101], T.blkf[:], pf(22))], ["blkf", "thf"], 3)
    ts(T.limh[:, 0:3], T.lf[:, 0:3], 0.0, PP[:, 100:101], OP.mult, OP.add, ["lf0"], ["lim0", "lim1", "lim2"], [3])
    act(T.p8k[:], T.idf[:], AF.Copy, ["idf"], ["p8k"], scale=8192.0)
    cp(T.odu[:], T.odi[:, 0:84], ["odi"], ["odu"])
    ts(T.qc[:], T.lf[:, 24:36], pm, 65.0, OP.add, OP.add, ["lf2", "pm"], ["qc"])
    ts(pf(3), pf(9), 16.0, 15.0, OP.mult, OP.add, ["p8"], ["p3"])
    ts(pf(21), T.wti[:, 0:1], -1.0, None, OP.mult, None, ["wti"], ["wtf"])
    ts(T.bcg[:], T.lf[:, 0:4], 0.0, pf(3), OP.mult, OP.add, ["lf0", "p3"], ["bcg"])
    ts(T.diagS[:], T.j16[:], pm, 1.0 / 8192, OP.is_equal, OP.mult, ["j16", "pm"], ["diagS"])
    ts(T.diag4[:], T.diag4[:], pm, None, OP.is_equal, None, ["diag4a", "pm"], ["diag4"])
    for name, src in (("nblkf", "blkf"), ("nlo", "lof"), ("nhi", "hif")):
        act(T[name][:], T[src][:], AF.Copy, [src], [name], scale=-1.0)
    for h in range(2):
        act(T.selW[:, 1024 * h:1024 * h + 1024], T.selA[:, 1024 * h:1024 * h + 1024], AF.Copy, SELA + ["wtf"], ["selW%d" % h], scale=pf(21))

    M = T.M[:, 0:12]
    dead, go = T.Fl[:, 0:12], T.Fl[:, 12:24]
    Id, Ig = T.In[:, 0:12], T.In[:, 12:24]
    cnat = T.cbuf[:, 16:208]
    I, nk, p8 = T.idb[:], T.n2k[:], T.p8k[:]
    PV, PX, PT, PS, PM, PA, PI = PH[:, 16:28], PP[:, 16:28], PP[:, 32:44], PC[:, 0:12], PC[:, 16:28], PC[:, 32:44], PC[:, 48:49]
    OWN = ["own"]
    nsent = [0]

    def to_all(s):
        mask = -1
        for d in T.cores:
            if d != s:
                mask &= topo.mask(s, d)
        return mask

    def refill(t):
        act(T.GBb[:], T.odB[:, 0:(208 if t == 0 else Q + 16)].indirect(T.idxu[:]), AF.Copy, ["odB0", "odB1", "idxu"] + ["odB2"] * (t > 0), ["GB"])
        if t > 0:
            mms("Vm", "V", [(PV, T.idf[:], T.vm[:])], ["idf", "vm"], 7)
        mms("V", "V", [(PV, m, T.GBb[:, a:192:16]) for a, m in enumerate(sel(T.selO))], ["selO0", "selO1", "GB"], 7)
        if t == 0:
            cp(T.oi[:], PV, [], ["oi"], [7])
        else:
            tt(T.oi[:], T.kcnf[:], PV, OP.add, ["kcnf"], ["oi"], [7])
        ts(T.vu[:], PV, -4095.0, None, OP.add, None, [], ["vu"], [7])
        ts(T.oi2[:], T.oi[:], W - 1, None, OP.bitwise_and, None, ["oi"], ["and"])
        cp(T.ou[:], T.oi2[:], ["and"], ["ou"])
        cp(T.vp[:], PV, [], ["vp"], [7])
        ts(T.v4u[:], T.vp[:, 0:12].indirect(T.bc4[:, 0:3]), -4095.0, None, OP.add, None, ["vp", "bc4"], ["v4u"])
        tt(cnat, colw.indirect(T.ou[:]), T.GBb[:], OP.add, ["col", "ou", "GB"], ["c"])
        act(T.own4[:], Xw.indirect(T.v4u[:]), AF.Copy, XK + ["v4u"], ["own"])
        turn(T.trb[:, 0:192], T.cbuf[:, 16:208], ["c"], ["tr1"])
        turn(T.trb[:, 192:416], T.cbuf[:, 0:224], ["c", "c0", "c1"], ["tr2"])
        cp(T.xo[:, 0:64], T.trb[:, 0:416].indirect(T.perm1[:, 0:4]), ["tr1", "tr2", "perm"], ["xo0"])
        cp(T.xo[:, 64:192], T.trb[:, 0:416].indirect(T.perm1[:, 4:12]), ["tr1", "tr2", "perm"], ["xo1"])
        cp(colw.indirect(T.vu[:]), cnat, ["vu", "c"], ["col"])
        if 2 <= t < NT - 1:
            act(T.ownc[:], Xw.indirect(T.vu[:]), AF.Copy, XK + ["vu"], ["ownc"])

    def penalty(t):
        act(T.nvb[:], T.vp[:, 0:12].indirect(T.bc12[:]), AF.Identity, ["vp", "bc12"], ["nvb"], bias=4096.0, scale=-1.0)
        act(T.cO[:], T.trb[:, 0:416].indirect(T.perm2[:]), AF.Copy, ["tr1", "tr2", "perm2"], ["cO"])
        act(T.sg[:], T.cO[:], AF.Sign, ["cO"], ["sg"], bias=-4095.5)
        mms("Dv", "D", [(PD[:, 0:192], T.idf[:], T.nvb[:])], ["idf", "nvb"], 1)
        mms("Dc", "D", [(PD[:, 0:192], T.idf[:], T.cO[:]), (PD[:, 0:192], nk, T.sg[:])], ["idf", "cO", "n2k", "sg"], 1)
        act(T.ed[:], PD[:, 0:192], AF.Abs, [], ["ed"], bias=-2049.0, b=[1])
        act(T.pen[:], T.ed[:], AF.Relu, ["ed"], ["pen"], bias=124.0, scale=-8.0)
        if t < NT - 1:
            mms("Cv", "C", [(PC[:, 64:256], I, T.kcon[:]), (PC[:, 64:256], T.idf[:], T.nvb[:])], ["idb", "kcon", "idf", "nvb"], 2)
            mms("Cc", "C", [(PC[:, 64:256], T.idf[:], T.cO[:])], ["idf", "cO"], 2)

    def ksum(name, c, src, n, keys):
        mms(name, "K", [(PK[:, c:c + n // 4:4], m, src[:, 768 * c + a:768 * c + n:16]) for a, m in enumerate(sel(T.selA))], SELA + keys, 0)

    def distances(t):
        ns, n = 64 * SHARE[t], RELU[t]
        e = 768 - ns
        mms("zero", "K", [(PK[:, 0:192], I, T.zero[:])], ["idb", "zero"], 0)
        mms("Kp", "K", [(PK[:, 0:192], nk, T.pen[:])], ["n2k", "pen"], 0)
        act(T.Gs[:, 0:ns], Xw.indirect(T.xo[:, 144 + e // 16:192]), AF.Copy, XK + ["xo1"], ["Gs"])
        mms("Gown" if t < NT - 1 else "Gsub", "G", [(PG0[:, 0:ns], T.nid[:], T.own4[:, e:768])], ["nid"] + OWN, 4)
        mms("Gsub", "G", [(PG0[:, 0:ns], I, T.Gs[:, 0:ns])], ["idb", "Gs"], 4)
        act(T.A[:, 2304 + e:3072], PG0[:, 0:ns], AF.Abs, [], ["As"], b=[4])
        pieces = [(0, 0, 768), (1, 0, 768), (3, 0, e), (2, 0, CUT[t][0]), (2, CUT[t][0], CUT[t][1]), (2, CUT[t][1], 768)]
        for i, (c, lo, hi) in enumerate(pieces):
            if lo == hi:
                continue
            tt(T.dif[:, 768 * c + lo:768 * c + hi], Xw.indirect(T.xo[:, 48 * c + lo // 16:48 * c + hi // 16]), T.own4[:, lo:hi],
               OP.subtract, XK + ["xo0"] + ["xo1"] * (c > 0) + OWN, ["g%d" % i])
            if c == 1 and n:
                ksum("r1", 1, T.dif, n, ["g1"])
                ts(T.A[:, 768:768 + n], T.dif[:, 768:768 + n], -2.0, 0.0, OP.mult, OP.max, ["g1"], ["relu"])
                lo = n
            if lo < hi:
                act(T.A[:, 768 * c + lo:768 * c + hi], T.dif[:, 768 * c + lo:768 * c + hi], AF.Abs, ["g%d" % i], ["a%d" % i])
        for c, keys in enumerate((["a0"], ["a1", "relu"], ["a3", "a4", "a5"], ["a2", "As"])):
            ksum("k%d" % c, c, T.A, 768, keys)

    def arrive(t):
        i = t - 3
        src = T.cores[(rank - 1 - (t - 1) % (N - 1)) % N]
        p = T.lnd[:, 64 * i:64 * i + 64]
        act(T.gy[:], p, AF.Identity, [], ["gy"], bias=MAGIC, wait=[(T.sem["ga%d" % i], len(topo.engines(src, core)))])
        act(T.gx[:], T.gy[:], AF.Identity, ["gy"], ["gx"], bias=-MAGIC)
        mms("hash", "H", [(PH[:, 0:4], m, T.gx[:, a:64:16]) for a, m in enumerate(sel(T.selW))], ["selW0", "selW1", "gx"], 7)
        ts(T.hi[:], PH[:, 0:4], 77.0 * t, None, OP.add, None, [], ["hi"], [7])
        ts(T.hi2[:], T.hi[:], W - 1, None, OP.bitwise_and, None, ["hi"], ["hi2"])
        cp(T.hu[:], T.hi2[:], ["hi2"], ["hu"])
        cp(T.gcu[:], colw.indirect(T.hu[:]), ["col", "hu"], ["gcu"])
        mms("gxT_", "gxT", [(PQ[0:64, 256:384], T.gx[:], I)], ["gx", "idb"], 6)
        mms("m_", "m", [(PQ[:, 384:448], l[:], r) for l, r in ((T.lof, p), (T.nlo, T.gx[:]), (T.hif, p), (T.nhi, T.gx[:]))],
            ["lof", "gx", "nlo", "hif", "nhi"], 6)
        act(T.gxT[0:64, :], PQ[0:64, 256:384], AF.Copy, [], ["gxT"], b=[6])
        act(T.mR[:], PQ[:, 384:448], AF.Copy, [], ["mR"], scale=-8192.0, b=[6])

    def judge(t):
        i = t - 3
        for h, (bank, nm) in enumerate(PG):
            part = slice(512 * h, 512 * h + 512)
            act(T.G[:, part], Xw.indirect(T.gcu[:, 32 * h:32 * h + 32]), AF.Copy, XK + ["gcu"], ["G%d" % h])
            mms("sub%d" % h, "sub%d" % h, [(bank[:], T.gxT[0:64, :], T.negE[0:64, part]), (bank[:], I, T.G[:, part])], ["gxT", "negE", "idb", "G%d" % h], nm)
            act(T.Ag[:, part], bank[:], AF.Abs, [], ["Ag%d" % h], b=[nm])
        mms("gsum", "gsum", [(PQ[:, 0:64], m, T.Ag[:, 64 * a:64 * a + 64]) for a, m in enumerate(sel(T.selA))], SELA + ["Ag0", "Ag1"], 6)
        scan(T.Rg[:], T.patg[:], PQ[:, 0:64], OP.add, OP.max, ["patg"], ["Rg"], [6])
        tt(T.Eg[:], T.Rg[:, 0:64].indirect(T.bcg[:]), T.diag4[:], OP.mult, ["Rg", "bcg", "diag4"], ["Eg"])
        mms("gspread", "gspread", [(PQ[:, 64:128], T.nblkf[:], T.Eg[:])], ["nblkf", "Eg"], 6)
        tt(T.jud[:], PQ[:, 64:128], T.mR[:], OP.min, ["mR"], ["jud"], [6])
        red(T.bl[:, 8 * i + 4:8 * i + 5], T.jud[:], ["jud"], ["bl%d" % i], name="best")
        ids, dsts = [], []
        for d in range(1, N):
            rid, pid, _ = topo.addr(T.cores[(rank + d) % N])
            ids.append(DstId(rid=rid, pnc=pid))
            dsts.append(T.bl[:, 8 * i + d:8 * i + d + 1])
        tr = RemoteDMATransfer(dst_ids=ids, dma_engine_mask=to_all(core), remote_sem=T.sem["gb%d" % i], srcs=[T.bl[:, 8 * i + 4:8 * i + 5]], dsts=dsts)
        op("G", lambda: g.remote_dma_fused([tr], local_sem=T.sem.sent), ["bl%d" % i], name="tell")
        nsent[0] += bin(to_all(core)).count("1")

    def thresholds(t):
        i = t - 3
        n = sum(bin(to_all(s)).count("1") for s in T.cores if s != core)
        lim = T.limh[:, t - 1:t]
        act(T.tiny[:, 1:2], lim, AF.Identity, ["lim%d" % (t - 1)], ["lim15"], bias=1.5)
        red(T.tiny[:, 0:1], T.bl[:, 8 * i + 1:8 * i + 5], ["bl%d" % i], ["bq"], wait=[(T.sem["gb%d" % i], n)])
        ts(T.tinyi[:, 0:1], T.tiny[:, 0:1], T.tiny[:, 1:2], 0.25, OP.subtract, OP.mult, ["bq", "lim15"], ["bi"])
        ts(T.limh[:, t:t + 1], T.tinyi[:, 0:1], lim, lim, OP.add, OP.max, ["bi", "lim%d" % (t - 1)], ["lim%d" % t], name="lim")

    def least(t):
        scan(T.Rb[:, 1:193], T.clamp[:], PK[:, 0:192], OP.min, OP.max, ["clamp"], ["Rb"], [0])
        if t == 0:
            cp(M, T.Rb[:, 16:193:16], ["Rb"], ["M"])
        else:
            tt(M, T.Rb[:, 16:193:16], PM, OP.max, ["Rb"], ["M"], [2])

    def fates(t):
        s = max(t - 1, 0)
        lim, nf, NF = T.limh[:, s:s + 1], T.nf[:, 12 * t:12 * t + 12], "nf%d" % t
        ts(dead, M, lim, 0.0, OP.add, OP.is_gt, ["M", "lim%d" % s], ["dead"])
        if t >= 2:
            tt(go, PA, dead, OP.is_gt, ["dead"], ["go"], [2])
            scan(T.In[:], T.pat24[:], T.Fl[:], OP.mult, OP.add, ["pat24", "dead", "go"], ["In"])
            mms("Xd", "X", [(PX, nk, dead), (PX, nk, dead)], ["n2k", "dead"], 3)
            mms("Xg", "X", [(PX, nk, go)], ["n2k", "go"], 3)
            mms("X", "X", [(PX, I, Ig)], ["idb", "In"], 3)
            mms("B", "B", [(PP[:, 0:2], T.tri[:], T.In[:, 11:24:12])], ["tri", "In"], 3)
            ts(T.q[:], Ig, PP[:, 1:2], float(U), OP.add, OP.min, ["In"], ["q"], [3])
            ts(nf, PX, PP[:, 1:2], U - 2048.0, OP.add, OP.is_gt, [], [NF], [3], name="nf")
            mms("T", "T", [(PT, I, Id), (PT, I, T.q[:]), (PT, nk, nf)], ["In", "q", NF], 3)
        else:
            ts(nf, M, lim, 0.0, OP.add, OP.is_le, ["M", "lim%d" % s], [NF], name="go")
            scan(Id, T.pat24[:, 0:12], dead, OP.mult, OP.add, ["pat24", "dead"], ["In"])
            mms("X", "T", [(PT, nk, nf), (PT, I, Id)], ["n2k", NF, "idb", "In"], 3)
            mms("B", "B", [(PP[:, 0:1], T.tri[:], T.In[:, 11:12])], ["tri", "In"], 3)
        ts(T.idxu[:], PT, PP[:, 0:1], T.cur[:, t:t + 1], OP.add, OP.add, ["cur%d" % t], ["idxu"], [3])
        tt(T.keep[:], PK[:, 0:192], T.Rb[:, 0:192], OP.is_le, ["Rb", "Rb0"], ["keep"], [0])
        scan(T.Kb[:], T.keep[:], PC[:, 64:256], OP.mult, OP.max, ["keep"], ["Kb"], [2])
        tt(T.vm[:], T.vp[:], nf, OP.mult, ["vp", NF], ["vm"])
        tt(T.kcnf[:], T.Kb[:, 15:192:16], nf, OP.mult, ["Kb", NF], ["kcnf"])
        if t >= 2:
            mms("S", "S", [(PS, p8, dead), (PS, I, T.q[:]), (PS, p8, nf)], ["p8k", "dead", "q", NF], 2)
            leavers(t)
        if t < NT - 2:
            mms("I", "I", [(PI, T.blkb[:], T.In[:, 11:12])] + [(PI, T.sel15[:], T.q[:, 11:12])] * (t >= 2), ["blkb", "In", "sel15", "q"], 2)
            act(T.cur[:, t + 1:t + 2], PI, AF.Identity, ["cur%d" % t], ["cur%d" % (t + 1)], bias=T.cur[:, t:t + 1], b=[2], name="cur")
        mms("PM", "PM", [(PM, I, T.cb[:, 16:28]), (PM, p8, nf), (PM, T.idf[:], M)], ["cb", "p8k", NF, "idf", "M"], 2)
        if 1 <= t < NT - 2:
            mms("PA", "PA", [(PA, I, T.cb[:, 0:12]), (PA, I, T.nf[:, 12 * t - 12:12 * t]), (PA, I, nf)], ["cb", "nf%d" % (t - 1), NF], 2)

    def leavers(t):
        i = t - 2
        tt(T.slf[:], PS, T.qc[:], OP.min, ["qc"], ["slf"], [2])
        ts(T.slu[:], T.slf[:], -1.0, None, OP.add, None, ["slf"], ["slu"])
        tt(T.mE[:], T.M[:, 0:12].indirect(T.bc12[:]), T.diagS[:], OP.mult, ["M", "bc12", "diagS"], ["mE"])
        tt(T.snd[:, 256 * i:256 * i + 256].indirect(T.slu[:]), T.ownc[:], T.mE[:], OP.add, ["slu", "ownc", "mE"], ["snd%d" % i], name="snd")
        dst = T.cores[(rank + 1 + t % (N - 1)) % N]
        rid, pid, _ = topo.addr(dst)
        mask = topo.mask(core, dst)
        op("G", lambda: g.remote_dma(T.lnd[:, 64 * i:64 * i + 64], T.snd[:, 256 * i:256 * i + 64], T.sem["ga%d" % i], T.sem.sent, pid, rid, mask),
           ["snd%d" % i], name="send")
        nsent[0] += len(topo.engines(core, dst))

    def results():
        act(T.yvf[:], T.vp[:], AF.Identity, ["vp"], ["yvf"], bias=-4095.0)
        dma("Y", T.yv[:], T.yvf[:], ["yvf"], ["outv"])
        for c in range(len(YCUT) - 1):
            lo, hi = YCUT[c:c + 2]
            ts(T.yni[:, lo:hi], colw.indirect(T.odu[:, lo // 16:hi // 16]), W - 1, None, OP.bitwise_and, None, ["col", "odu"], ["yn%d" % c])
            act(T.ynf[:, lo:hi], T.yni[:, lo:hi], AF.Copy, ["yn%d" % c], ["yf%d" % c])
            dma("Y", T.yn[:, lo:hi], T.ynf[:, lo:hi], ["yf%d" % c], ["out%d" % c])
        dma("Y", T.yg[:], T.jud[0:128:16, :], ["jud"], ["outg"])
        act(T.ymf[:], M, AF.Copy, ["M"], ["ymf"], scale=-1.0)
        dma("Y", T.ym[:], T.ymf[:], ["ymf"], ["outm"])
        dma("Y", T.yt[:], T.limh[0:128:16, 0:NT], ["lim%d" % t for t in range(NT)], ["outt"])

    for t in range(NT):
        step[0] = t
        for part in [refill, penalty, distances, least] + [fates] * (t < NT - 1) + [arrive, judge, thresholds] * (t >= 3):
            part(t)
    results()

    step[0] = "end"
    op("G", None, ["out0", "out1", "out2", "outv", "outg", "outm", "outt"], wait=[(T.sem.sent, nsent[0])], name="end")
    _emit(g, T, _sequence(setup, calls))
